import numpy as np
import ml_dtypes


def mxq(x, axis, fmt="e4m3"):
    dtype, down = {"e4m3": (ml_dtypes.float8_e4m3fn, 7), "e5m2": (ml_dtypes.float8_e5m2, 14)}[fmt]
    v = np.moveaxis(np.asarray(x, np.float32).astype(ml_dtypes.bfloat16).astype(np.float64), axis, -1)
    blocks = v.reshape(v.shape[:-1] + (-1, 32))
    amax = np.abs(blocks).max(-1, keepdims=True)
    byte = np.maximum(np.where(amax > 0, np.frexp(amax)[1] - 1 + 127, 0) - down, 1)
    scale = np.exp2(byte - 127.0)
    codes = (blocks / scale).astype(np.float32).astype(dtype).astype(np.float64)
    return np.moveaxis((codes * scale).reshape(v.shape), -1, axis)


WIDE = False


def mx_kscale(k):
    if not WIDE:
        return np.ones(k)
    levels = np.array([10, -10, 5, -5, 0])
    if k % 512:
        return np.exp2(np.random.permutation(np.resize(levels, k // 32))).repeat(32)
    a = np.empty((k // 512, 16))
    for p in range(k // 512):
        a[p, :8] = np.random.permutation(np.resize(levels, 8))
        for g in range(8):
            far = levels[np.abs(levels - a[p, g]) >= 10]
            a[p, g + 8] = far[np.random.randint(len(far))]
    return np.exp2(a.ravel()).repeat(32)


def f64(x):
    return np.asarray(x).astype(np.float64)


def striped(idx):
    return np.tile(idx.reshape(-1, 16).T, (8, 1)).astype(np.uint16)


def unstriped(offs):
    return offs[:16].T.reshape(-1).astype(np.int64)


def pack_weight(w):
    k, n = w.shape
    w = f64(np.asarray(w, np.float32).astype(ml_dtypes.bfloat16)).reshape(k // 32, 32, n)
    amax = np.abs(w).max(1)
    byte = np.clip(np.where(amax > 0, np.frexp(amax)[1] - 1 + 127 - 7, 1), 1, 254)
    scaled = (w * np.exp2(127.0 - byte)[:, None, :]).reshape(k, n).astype(np.float32)
    words = np.ascontiguousarray(scaled.reshape(k // 512, 128, 4, n).transpose(0, 1, 3, 2)).astype(ml_dtypes.float8_e4m3fn).view(np.uint8)
    return words, np.ascontiguousarray(byte.astype(np.uint8).reshape(k // 512, 16, n))


def unpack_weight(words, scales):
    g, p, n, _ = words.shape
    vals = np.ascontiguousarray(words).view(ml_dtypes.float8_e4m3fn).astype(np.float64) * np.repeat(np.exp2(scales.astype(np.float64) - 127.0), 8, axis=1)[..., None]
    return vals.transpose(0, 1, 3, 2).reshape(g * 512, n)


def relu(v):
    return np.maximum(v, 0.0)


K, T, S, H, N = 1024, 2048, 512, 512, 256
P = 2 ** 7


def setup_inputs():
    n = np.random.standard_normal
    s = mx_kscale(K)[:, None]
    u = mx_kscale(H)
    packed_xT = pack_weight(n((K, T)) * s)
    return {
        "x_words": packed_xT[0],
        "x_scales": packed_xT[1],
        "w1": (n((K, H)) / np.sqrt(K) / s * u).astype(np.float32),
        "w2": (n((H, N)) / np.sqrt(H) / u[:, None]).astype(np.float32),
        "own1": (np.tile(n(S) * 0.7, (P, 1))).astype(np.float32),
        "oth1": (np.tile(n(S) * 0.7, (P, 1))).astype(np.float32),
        "own2": (np.tile(n(S) * 0.7, (P, 1))).astype(np.float32),
        "oth2": (np.tile(n(S) * 0.7, (P, 1))).astype(np.float32),
        "offs": striped(np.random.permutation(T)[:S]),
        "mix1": striped(np.random.permutation(S)),
        "mix2": striped(np.random.permutation(S)),
    }


def reference(x_words, x_scales, w1, w2, own1, oth1, own2, oth2, offs, mix1, mix2):
    xq = unpack_weight(x_words, x_scales)[:, unstriped(offs)]
    y = relu(mxq(f64(w1), 0, "e4m3").T @ xq)
    h1 = y * f64(own1)[:1] + y[:, unstriped(mix1)] * f64(oth1)[:1]
    h2 = h1 * f64(own2)[:1] + h1[:, unstriped(mix2)] * f64(oth2)[:1]
    return mxq(f64(w2), 0, "e4m3").T @ mxq(h2, 0, "e4m3")

@@ -1,0 +1,236 @@
+from contextlib import ExitStack
+
+import concourse.mybir as mybir
+from concourse.masks import make_identity
+
+K, T, S, H, N = 1024, 2048, 512, 512, 256
+FLOPS = 2 * K * H * S + 2 * H * N * S
+
+F32 = mybir.dt.float32
+BF16 = mybir.dt.bfloat16
+I32 = mybir.dt.int32
+U32 = mybir.dt.uint32
+U16 = mybir.dt.uint16
+U8 = mybir.dt.uint8
+FP8X4 = mybir.dt.float8_e4m3fn_x4
+MULT = mybir.AluOpType.mult
+ADD = mybir.AluOpType.add
+RELU = mybir.ActivationFunctionType.Relu
+COPY = mybir.ActivationFunctionType.Copy
+
+P = 128
+PACK = 4
+K_PASS = P * PACK
+PASSES = K // K_PASS
+FEATURE_TILES = H // P
+TOKEN_BLOCKS = S // P
+OUT_TILES = N // P
+SPARE = 16
+LIST_ROWS = 16
+
+
+def tile_picked_ybutter_relu_p_kernel(
+    tc, x_words, x_scales, w1, w2, own1, oth1, own2, oth2, offs, mix1, mix2, out
+):
+    nc = tc.nc
+    with ExitStack() as ctx:
+        keep = ctx.enter_context(tc.tile_pool(name="keep", bufs=1))
+        ring = ctx.enter_context(tc.tile_pool(name="ring", bufs=2))
+        psum = ctx.enter_context(tc.psum_pool(name="psum", bufs=1))
+
+        def entries(list_tile, first, count):
+            return list_tile[:, first // LIST_ROWS : (first + count) // LIST_ROWS]
+
+        def load_w1(raw, b, g):
+            rows = w1[g * K_PASS : (g + 1) * K_PASS, b * P : (b + 1) * P]
+            nc.sync.dma_start(raw[:, :, g, :], rows.rearrange("(p j) c -> p j c", j=PACK))
+
+        def interleave(grouped, raw):
+            nc.scalar.copy(
+                grouped.rearrange("p (c i j) -> p c j i", i=4, j=PACK),
+                raw.rearrange("p j (c i) -> p c j i", i=4),
+            )
+
+        def quantise(name, grouped, width):
+            codes = keep.tile([P, width], U32, name=name + "_codes", align_bytes=64)
+            scales = keep.tile([P, width], U8, name=name + "_scales", align_bytes=64)
+            nc.vector.quantize_mx(out=codes[:].bitcast(FP8X4), scales=scales[:], in_=grouped)
+            return codes, scales
+
+        def load_row(name, src):
+            row = keep.tile([P, S], F32, name=name)
+            nc.sync.dma_start(row[:], src)
+            return row
+
+        scale_table = keep.tile([P, T], U8, name="scale_table")
+        nc.vector.memset(scale_table[:].bitcast(I32), 0)
+        for q in range(4):
+            nc.scalar.dma_start(
+                scale_table[32 * q : 32 * q + 4 * PASSES, :].bitcast(I32),
+                x_scales[:, 4 * q : 4 * q + 4, :].bitcast(I32),
+            )
+
+        w1_raw = [keep.tile([P, PACK, PASSES, P], F32, name=f"w1_raw{b}") for b in range(FEATURE_TILES)]
+        offs_tile = keep.tile([P, S // LIST_ROWS], U16, name="offs_tile")
+        mix1_tile = keep.tile([P, S // LIST_ROWS], U16, name="mix1_tile")
+        mix2_tile = keep.tile([P, S // LIST_ROWS], U16, name="mix2_tile")
+        load_w1(w1_raw[0], 0, 0)
+        nc.sync.dma_start(offs_tile[:], offs)
+        nc.sync.dma_start(mix1_tile[:], mix1)
+        nc.sync.dma_start(mix2_tile[:], mix2)
+        load_w1(w1_raw[0], 0, 1)
+        word_tables = []
+        for g in range(PASSES):
+            table = keep.tile([P, T], U32, name=f"word_table{g}")
+            nc.sync.dma_start(table[:].bitcast(I32), x_words[g].rearrange("p n t -> p (n t)").bitcast(I32))
+            word_tables.append(table)
+        oth1_row = load_row("oth1_row", oth1)
+        own1_row = load_row("own1_row", own1)
+        for g in range(PASSES):
+            load_w1(w1_raw[1], 1, g)
+        own2_row = load_row("own2_row", own2)
+        oth2_row = load_row("oth2_row", oth2)
+        for b in range(2, FEATURE_TILES):
+            for g in range(PASSES):
+                load_w1(w1_raw[b], b, g)
+        w2_raw = keep.tile([P, PACK, N], F32, name="w2_raw")
+        nc.sync.dma_start(w2_raw[:], w2.rearrange("(p j) n -> p j n", j=PACK))
+
+        identity = keep.tile([P, P], F32, name="identity")
+        make_identity(nc, identity[:])
+        y = [keep.tile([P, S + SPARE], F32, name=f"y{b}") for b in range(FEATURE_TILES)]
+        h1 = [keep.tile([P, S + SPARE], F32, name=f"h1_{b}") for b in range(FEATURE_TILES)]
+        for window in y + h1:
+            nc.gpsimd.memset(window[:, S:], 0.0)
+
+        def quantised_w1(b):
+            grouped = ring.tile([P, PASSES, P * PACK], BF16, name="w1_grouped", align_bytes=64)
+            for g in range(PASSES):
+                interleave(grouped[:, g, :], w1_raw[b][:, :, g, :])
+            return quantise(f"w1_{b}", grouped[:].rearrange("p g c -> p (g c)"), PASSES * P)
+
+        x_codes = [keep.tile([P, S], U32, name=f"x_codes{g}", align_bytes=64) for g in range(PASSES)]
+        x_bytes = keep.tile([P, S], U8, name="x_bytes", align_bytes=64)
+
+        def first_product(b, w_codes, w_scales, first, count):
+            acc = psum.tile([P, count], F32, name="acc", tag="acc", bufs=2)
+            cols = slice(first, first + count)
+            for g in range(PASSES):
+                nc.tensor.matmul_mx(
+                    out=acc[:],
+                    lhsT=w_codes[:, g * P : (g + 1) * P].bitcast(FP8X4),
+                    lhsT_scale=w_scales[:, g * P : (g + 1) * P],
+                    rhs=x_codes[g][:, cols].bitcast(FP8X4),
+                    rhs_scale=x_bytes[4 * g :, cols],
+                    start=(g == 0),
+                    stop=(g == PASSES - 1),
+                )
+            nc.scalar.activation(y[b][:, cols], acc[:], RELU)
+
+        w_codes, w_scales = quantised_w1(0)
+        nc.vector.tensor_copy(x_codes[0][:], word_tables[0][:].indirect(offs_tile[:]))
+        nc.vector.tensor_copy(x_bytes[:], scale_table[:].indirect(offs_tile[:]))
+        half = S // 2
+        for first in (0, half):
+            nc.vector.tensor_copy(
+                x_codes[1][:, first : first + half], word_tables[1][:].indirect(entries(offs_tile, first, half))
+            )
+            first_product(0, w_codes, w_scales, first, half)
+
+        turned = psum.tile([P, TOKEN_BLOCKS, P], F32, name="turned", tag="turned")
+        for tb in range(TOKEN_BLOCKS):
+            nc.tensor.transpose(turned[:, tb, :], own1_row[:, tb * P : (tb + 1) * P], identity[:])
+        own1_col = keep.tile([P, TOKEN_BLOCKS], F32, name="own1_col")
+        nc.scalar.copy(own1_col[:], turned[:, :, 0])
+
+        h2_banks = [psum.tile([P, H], F32, name=f"h2_bank{tb}") for tb in range(TOKEN_BLOCKS)]
+
+        def add_into_h2(term, b, tb, start=False, stop=False):
+            nc.tensor.matmul(
+                h2_banks[tb][:, b * P : (b + 1) * P], term, identity[:], start=start, stop=stop, is_transpose=True
+            )
+
+        def partner1(b):
+            term = ring.tile([P, S], F32, name="partner1")
+            nc.vector.tensor_tensor(term[:], y[b][:].indirect(mix1_tile[:]), oth1_row[:], MULT)
+            return term
+
+        def own1_by_transposes(b):
+            turned = psum.tile([P, TOKEN_BLOCKS, P], F32, name="turned", tag="turned")
+            scaled = ring.tile([P, TOKEN_BLOCKS, P], F32, name="scaled")
+            back = psum.tile([P, S], F32, name="back", tag="back")
+            for tb in range(TOKEN_BLOCKS):
+                nc.tensor.transpose(turned[:, tb, :], y[b][:, tb * P : (tb + 1) * P], identity[:])
+            for tb in range(TOKEN_BLOCKS):
+                nc.scalar.activation(scaled[:, tb, :], turned[:, tb, :], COPY, scale=own1_col[:, tb : tb + 1])
+            for tb in range(TOKEN_BLOCKS):
+                nc.tensor.transpose(back[:, tb * P : (tb + 1) * P], scaled[:, tb, :], identity[:])
+            return back
+
+        def own2_term(b):
+            term = ring.tile([P, S], F32, name="own2_term")
+            nc.vector.tensor_tensor(term[:], h1[b][:, :S], own2_row[:], MULT)
+            for tb in range(TOKEN_BLOCKS):
+                add_into_h2(term[:, tb * P : (tb + 1) * P], b, tb, start=(b == 0))
+
+        own_term = ring.tile([P, S], F32, name="own1_term")
+        partner_term = partner1(0)
+        nc.vector.tensor_tensor(own_term[:], y[0][:, :S], own1_row[:], MULT)
+        for b in range(FEATURE_TILES):
+            last = b == FEATURE_TILES - 1
+            if not last:
+                w_codes, w_scales = quantised_w1(b + 1)
+                first_product(b + 1, w_codes, w_scales, 0, S)
+            nc.vector.tensor_tensor(h1[b][:, :S], own_term[:], partner_term[:], ADD)
+            if not last:
+                own_term = own1_by_transposes(b + 1)
+                partner_term = partner1(b + 1)
+            own2_term(b)
+            if b == 0:
+                term = ring.tile([P, S], F32, name="partner2_whole")
+                nc.vector.tensor_tensor(term[:], h1[0][:].indirect(mix2_tile[:]), oth2_row[:], MULT)
+                for tb in range(TOKEN_BLOCKS):
+                    add_into_h2(term[:, tb * P : (tb + 1) * P], 0, tb)
+
+        w2_grouped = keep.tile([P, N * PACK], BF16, name="w2_grouped", align_bytes=64)
+        interleave(w2_grouped[:], w2_raw[:])
+        w2_codes, w2_scales = quantise("w2", w2_grouped[:], N)
+
+        out_view = out.rearrange("(m p) s -> p m s", p=P)
+        for tb in range(TOKEN_BLOCKS):
+            tokens = slice(tb * P, (tb + 1) * P)
+            for b in range(1, FEATURE_TILES):
+                term = ring.tile([P, P], F32, name="partner2", bufs=6)
+                nc.vector.tensor_tensor(
+                    term[:], h1[b][:].indirect(entries(mix2_tile, tb * P, P)), oth2_row[:, tokens], MULT
+                )
+                add_into_h2(term[:], b, tb, stop=(b == FEATURE_TILES - 1))
+            h2_rows = ring.tile([P, 2, P, 2], BF16, name="h2_rows")
+            nc.scalar.copy(h2_rows[:], h2_banks[tb][:].rearrange("s (p u e) -> s u p e", u=2, e=2))
+            pairs = h2_rows[:].rearrange("s u p e -> s (u p e)").bitcast(F32)
+            pair_bank = psum.tile([P, 2, P], F32, name="pair_bank", tag="acc", bufs=2)
+            for u in range(2):
+                nc.tensor.transpose(pair_bank[:, u, :], pairs[:, u * P : (u + 1) * P], identity[:])
+            h2_grouped = ring.tile([P, P * PACK], BF16, name="h2_grouped", align_bytes=64)
+            nc.scalar.copy(
+                h2_grouped[:].bitcast(F32).rearrange("p (s u) -> p s u", u=2),
+                pair_bank[:].rearrange("p u s -> p s u"),
+            )
+            h2_codes, h2_scales = quantise(f"h2_{tb}", h2_grouped[:], P)
+            result = psum.tile([P, OUT_TILES, P], F32, name="result", tag=("turned", "back")[tb % 2])
+            for m in range(OUT_TILES):
+                nc.tensor.matmul_mx(
+                    out=result[:, m, :],
+                    lhsT=w2_codes[:, m * P : (m + 1) * P].bitcast(FP8X4),
+                    lhsT_scale=w2_scales[:, m * P : (m + 1) * P],
+                    rhs=h2_codes[:].bitcast(FP8X4),
+                    rhs_scale=h2_scales[:],
+                    start=True,
+                    stop=True,
+                )
+            staged = ring.tile([P, OUT_TILES, P], F32, name="staged", bufs=4)
+            if tb < 2:
+                nc.scalar.copy(staged[:], result[:])
+            else:
+                nc.vector.tensor_copy(staged[:], result[:])
+            nc.sync.dma_start(out_view[:, :, tokens], staged[:])

@@ -22,7 +22,6 @@ P = 128
 PACK = 4
 K_PASS = P * PACK
 PASSES = K // K_PASS
-FEATURE_TILES = H // P
 TOKEN_BLOCKS = S // P
 OUT_TILES = N // P
 SPARE = 16
@@ -36,19 +35,15 @@ def tile_picked_ybutter_relu_p_kernel(
     with ExitStack() as ctx:
         keep = ctx.enter_context(tc.tile_pool(name="keep", bufs=1))
         ring = ctx.enter_context(tc.tile_pool(name="ring", bufs=2))
-        psum = ctx.enter_context(tc.psum_pool(name="psum", bufs=1))
+        psum = ctx.enter_context(tc.psum_pool(name="psum", bufs=8))
 
         def entries(list_tile, first, count):
             return list_tile[:, first // LIST_ROWS : (first + count) // LIST_ROWS]
 
-        def load_w1(raw, b, g):
-            rows = w1[g * K_PASS : (g + 1) * K_PASS, b * P : (b + 1) * P]
-            nc.sync.dma_start(raw[:, :, g, :], rows.rearrange("(p j) c -> p j c", j=PACK))
-
-        def interleave(grouped, raw):
-            nc.scalar.copy(
+        def interleave(copy, grouped, planes):
+            copy(
                 grouped.rearrange("p (c i j) -> p c j i", i=4, j=PACK),
-                raw.rearrange("p j (c i) -> p c j i", i=4),
+                planes.rearrange("p j (c i) -> p c j i", i=4),
             )
 
         def quantise(name, grouped, width):
@@ -57,167 +52,163 @@ def tile_picked_ybutter_relu_p_kernel(
             nc.vector.quantize_mx(out=codes[:].bitcast(FP8X4), scales=scales[:], in_=grouped)
             return codes, scales
 
-        def load_row(name, src):
-            row = keep.tile([P, S], F32, name=name)
-            nc.sync.dma_start(row[:], src)
-            return row
+        offs_tile = keep.tile([P, S // LIST_ROWS], U16, name="offs_tile")
+        mix1_tile = keep.tile([P, S // LIST_ROWS], U16, name="mix1_tile")
+        mix2_tile = keep.tile([P, S // LIST_ROWS], U16, name="mix2_tile")
+        nc.sync.dma_start(offs_tile[:], offs)
 
+        own_rows = keep.tile([P, P], F32, name="own_rows")
+        for v, own in enumerate((own1, own2)):
+            nc.scalar.dma_start(
+                own_rows[64 * v : 64 * (v + 1), :], own[:16, :].rearrange("r (b c) -> (r b) c", c=P)
+            )
         scale_table = keep.tile([P, T], U8, name="scale_table")
-        nc.vector.memset(scale_table[:].bitcast(I32), 0)
+        nc.gpsimd.memset(scale_table[:].bitcast(I32), 0)
         for q in range(4):
             nc.scalar.dma_start(
                 scale_table[32 * q : 32 * q + 4 * PASSES, :].bitcast(I32),
                 x_scales[:, 4 * q : 4 * q + 4, :].bitcast(I32),
             )
 
-        w1_raw = [keep.tile([P, PACK, PASSES, P], F32, name=f"w1_raw{b}") for b in range(FEATURE_TILES)]
-        offs_tile = keep.tile([P, S // LIST_ROWS], U16, name="offs_tile")
-        mix1_tile = keep.tile([P, S // LIST_ROWS], U16, name="mix1_tile")
-        mix2_tile = keep.tile([P, S // LIST_ROWS], U16, name="mix2_tile")
-        load_w1(w1_raw[0], 0, 0)
-        nc.sync.dma_start(offs_tile[:], offs)
-        nc.sync.dma_start(mix1_tile[:], mix1)
-        nc.sync.dma_start(mix2_tile[:], mix2)
-        load_w1(w1_raw[0], 0, 1)
-        word_tables = []
+        w1_raw, word_tables = [], []
         for g in range(PASSES):
+            raw = keep.tile([P, PACK, H], F32, name=f"w1_raw{g}")
+            nc.sync.dma_start(raw[:], w1[g * K_PASS : (g + 1) * K_PASS, :].rearrange("(p j) c -> p j c", j=PACK))
+            w1_raw.append(raw)
             table = keep.tile([P, T], U32, name=f"word_table{g}")
             nc.sync.dma_start(table[:].bitcast(I32), x_words[g].rearrange("p n t -> p (n t)").bitcast(I32))
             word_tables.append(table)
-        oth1_row = load_row("oth1_row", oth1)
-        own1_row = load_row("own1_row", own1)
-        for g in range(PASSES):
-            load_w1(w1_raw[1], 1, g)
-        own2_row = load_row("own2_row", own2)
-        oth2_row = load_row("oth2_row", oth2)
-        for b in range(2, FEATURE_TILES):
-            for g in range(PASSES):
-                load_w1(w1_raw[b], b, g)
         w2_raw = keep.tile([P, PACK, N], F32, name="w2_raw")
         nc.sync.dma_start(w2_raw[:], w2.rearrange("(p j) n -> p j n", j=PACK))
+        nc.sync.dma_start(mix1_tile[:], mix1)
+        oth1_row = keep.tile([P, S], F32, name="oth1_row")
+        nc.sync.dma_start(oth1_row[:], oth1)
+        nc.sync.dma_start(mix2_tile[:], mix2)
+        oth2_row = keep.tile([P, S], F32, name="oth2_row")
+        nc.sync.dma_start(oth2_row[:], oth2)
 
         identity = keep.tile([P, P], F32, name="identity")
         make_identity(nc, identity[:])
-        y = [keep.tile([P, S + SPARE], F32, name=f"y{b}") for b in range(FEATURE_TILES)]
-        h1 = [keep.tile([P, S + SPARE], F32, name=f"h1_{b}") for b in range(FEATURE_TILES)]
+        y = [keep.tile([P, S + SPARE], F32, name=f"y{t}") for t in range(PACK)]
+        h1 = [keep.tile([P, S + SPARE], F32, name=f"h1_{t}") for t in range(PACK)]
         for window in y + h1:
             nc.gpsimd.memset(window[:, S:], 0.0)
 
-        def quantised_w1(b):
-            grouped = ring.tile([P, PASSES, P * PACK], BF16, name="w1_grouped", align_bytes=64)
-            for g in range(PASSES):
-                interleave(grouped[:, g, :], w1_raw[b][:, :, g, :])
-            return quantise(f"w1_{b}", grouped[:].rearrange("p g c -> p (g c)"), PASSES * P)
+        own_bank = psum.tile([P, P], F32, name="bank")
+        nc.tensor.transpose(own_bank[:], own_rows[:], identity[:])
+        own_cols = keep.tile([P, 2, TOKEN_BLOCKS], F32, name="own_cols")
+        nc.scalar.copy(own_cols[:], own_bank[:].rearrange("s (v r) -> s v r", v=2)[:, :, :TOKEN_BLOCKS])
+
+        def quantised_w1(g, copies):
+            grouped = keep.tile([P, PACK, P, PACK], BF16, name=f"w1_grouped{g}", align_bytes=64)
+            share = P // len(copies)
+            for n, copy in enumerate(copies):
+                m = slice(n * share, (n + 1) * share)
+                copy(
+                    grouped[:, :, m, :].rearrange("p t m j -> p m j t"),
+                    w1_raw[g][:].rearrange("p j (m t) -> p m j t", t=PACK)[:, m, :, :],
+                )
+            return quantise(f"w1_{g}", grouped[:].rearrange("p t m j -> p (t m j)"), H)
 
         x_codes = [keep.tile([P, S], U32, name=f"x_codes{g}", align_bytes=64) for g in range(PASSES)]
         x_bytes = keep.tile([P, S], U8, name="x_bytes", align_bytes=64)
 
-        def first_product(b, w_codes, w_scales, first, count):
-            acc = psum.tile([P, count], F32, name="acc", tag="acc", bufs=2)
-            cols = slice(first, first + count)
-            for g in range(PASSES):
-                nc.tensor.matmul_mx(
-                    out=acc[:],
-                    lhsT=w_codes[:, g * P : (g + 1) * P].bitcast(FP8X4),
-                    lhsT_scale=w_scales[:, g * P : (g + 1) * P],
-                    rhs=x_codes[g][:, cols].bitcast(FP8X4),
-                    rhs_scale=x_bytes[4 * g :, cols],
-                    start=(g == 0),
-                    stop=(g == PASSES - 1),
-                )
-            nc.scalar.activation(y[b][:, cols], acc[:], RELU)
-
-        w_codes, w_scales = quantised_w1(0)
-        nc.vector.tensor_copy(x_codes[0][:], word_tables[0][:].indirect(offs_tile[:]))
-        nc.vector.tensor_copy(x_bytes[:], scale_table[:].indirect(offs_tile[:]))
         half = S // 2
+        pieces = [(0, 0, half), (0, half, half)] + [(t, 0, S) for t in range(1, PACK)]
+        accs = [
+            psum.tile([P, count], F32, name="bank") for t, first, count in pieces
+        ]
+
+        def first_product_pass(g, weights, piece, acc):
+            t, first, count = piece
+            cols = slice(first, first + count)
+            nc.tensor.matmul_mx(
+                out=acc[:],
+                lhsT=weights[0][:, t * P : (t + 1) * P].bitcast(FP8X4),
+                lhsT_scale=weights[1][:, t * P : (t + 1) * P],
+                rhs=x_codes[g][:, cols].bitcast(FP8X4),
+                rhs_scale=x_bytes[4 * g :, cols],
+                start=(g == 0),
+                stop=(g == PASSES - 1),
+            )
+
+        weights = quantised_w1(0, [nc.scalar.copy])
+        nc.vector.tensor_copy(x_bytes[:], scale_table[:].indirect(offs_tile[:]))
+        nc.vector.tensor_copy(x_codes[0][:], word_tables[0][:].indirect(offs_tile[:]))
+        for piece, acc in zip(pieces, accs):
+            first_product_pass(0, weights, piece, acc)
+        weights = quantised_w1(1, [nc.scalar.copy, nc.vector.tensor_copy])
         for first in (0, half):
             nc.vector.tensor_copy(
                 x_codes[1][:, first : first + half], word_tables[1][:].indirect(entries(offs_tile, first, half))
             )
-            first_product(0, w_codes, w_scales, first, half)
 
-        turned = psum.tile([P, TOKEN_BLOCKS, P], F32, name="turned", tag="turned")
-        for tb in range(TOKEN_BLOCKS):
-            nc.tensor.transpose(turned[:, tb, :], own1_row[:, tb * P : (tb + 1) * P], identity[:])
-        own1_col = keep.tile([P, TOKEN_BLOCKS], F32, name="own1_col")
-        nc.scalar.copy(own1_col[:], turned[:, :, 0])
+        w2_grouped = keep.tile([P, N * PACK], BF16, name="w2_grouped", align_bytes=64)
+        interleave(nc.vector.tensor_copy, w2_grouped[:], w2_raw[:])
+        w2_codes, w2_scales = quantise("w2", w2_grouped[:], N)
 
-        h2_banks = [psum.tile([P, H], F32, name=f"h2_bank{tb}") for tb in range(TOKEN_BLOCKS)]
+        def finish_y(n):
+            t, first, count = pieces[n]
+            first_product_pass(1, weights, pieces[n], accs[n])
+            nc.scalar.activation(y[t][:, first : first + count], accs[n][:], RELU)
 
-        def add_into_h2(term, b, tb, start=False, stop=False):
-            nc.tensor.matmul(
-                h2_banks[tb][:, b * P : (b + 1) * P], term, identity[:], start=start, stop=stop, is_transpose=True
-            )
-
-        def partner1(b):
-            term = ring.tile([P, S], F32, name="partner1")
-            nc.vector.tensor_tensor(term[:], y[b][:].indirect(mix1_tile[:]), oth1_row[:], MULT)
-            return term
-
-        def own1_by_transposes(b):
-            turned = psum.tile([P, TOKEN_BLOCKS, P], F32, name="turned", tag="turned")
-            scaled = ring.tile([P, TOKEN_BLOCKS, P], F32, name="scaled")
-            back = psum.tile([P, S], F32, name="back", tag="back")
+        def own_term(values, v):
+            turned = psum.tile([P, TOKEN_BLOCKS, P], F32, name="bank")
+            scaled = ring.tile([P, TOKEN_BLOCKS, P], F32, name="scaled", bufs=3)
+            back = psum.tile([P, S], F32, name="bank")
             for tb in range(TOKEN_BLOCKS):
-                nc.tensor.transpose(turned[:, tb, :], y[b][:, tb * P : (tb + 1) * P], identity[:])
+                nc.tensor.transpose(turned[:, tb, :], values[:, tb * P : (tb + 1) * P], identity[:])
             for tb in range(TOKEN_BLOCKS):
-                nc.scalar.activation(scaled[:, tb, :], turned[:, tb, :], COPY, scale=own1_col[:, tb : tb + 1])
+                nc.scalar.activation(scaled[:, tb, :], turned[:, tb, :], COPY, scale=own_cols[:, v, tb : tb + 1])
             for tb in range(TOKEN_BLOCKS):
                 nc.tensor.transpose(back[:, tb * P : (tb + 1) * P], scaled[:, tb, :], identity[:])
             return back
 
-        def own2_term(b):
-            term = ring.tile([P, S], F32, name="own2_term")
-            nc.vector.tensor_tensor(term[:], h1[b][:, :S], own2_row[:], MULT)
-            for tb in range(TOKEN_BLOCKS):
-                add_into_h2(term[:, tb * P : (tb + 1) * P], b, tb, start=(b == 0))
+        def partner_term(window, list_tile, factor, first, count):
+            term = ring.tile([P, count], F32, name=f"partner{count}", bufs=3 if count == S else 2)
+            nc.vector.tensor_tensor(
+                term[:], window[:].indirect(entries(list_tile, first, count)), factor[:, first : first + count], MULT
+            )
+            return term
 
-        own_term = ring.tile([P, S], F32, name="own1_term")
-        partner_term = partner1(0)
-        nc.vector.tensor_tensor(own_term[:], y[0][:, :S], own1_row[:], MULT)
-        for b in range(FEATURE_TILES):
-            last = b == FEATURE_TILES - 1
-            if not last:
-                w_codes, w_scales = quantised_w1(b + 1)
-                first_product(b + 1, w_codes, w_scales, 0, S)
-            nc.vector.tensor_tensor(h1[b][:, :S], own_term[:], partner_term[:], ADD)
-            if not last:
-                own_term = own1_by_transposes(b + 1)
-                partner_term = partner1(b + 1)
-            own2_term(b)
-            if b == 0:
-                term = ring.tile([P, S], F32, name="partner2_whole")
-                nc.vector.tensor_tensor(term[:], h1[0][:].indirect(mix2_tile[:]), oth2_row[:], MULT)
-                for tb in range(TOKEN_BLOCKS):
-                    add_into_h2(term[:, tb * P : (tb + 1) * P], 0, tb)
+        h2 = keep.tile([P, PACK, S], BF16, name="h2")
 
-        w2_grouped = keep.tile([P, N * PACK], BF16, name="w2_grouped", align_bytes=64)
-        interleave(w2_grouped[:], w2_raw[:])
-        w2_codes, w2_scales = quantise("w2", w2_grouped[:], N)
+        finish_y(0)
+        finish_y(1)
+        finish_y(2)
+        partner = partner_term(y[0], mix1_tile, oth1_row, 0, S)
+        for t in range(PACK):
+            own = own_term(y[t], 0)
+            if t + 2 < PACK:
+                finish_y(t + 3)
+            following = (
+                partner_term(y[t + 1], mix1_tile, oth1_row, 0, S)
+                if t + 1 < PACK
+                else partner_term(h1[0], mix2_tile, oth2_row, 0, S)
+            )
+            nc.vector.tensor_tensor(h1[t][:, :S], own[:], partner[:], ADD)
+            partner = following
+
+        for t in range(PACK - 1):
+            own = own_term(h1[t], 1)
+            if t + 2 < PACK:
+                following = partner_term(h1[t + 1], mix2_tile, oth2_row, 0, S)
+            nc.vector.tensor_tensor(h2[:, t, :], own[:], partner[:], ADD)
+            partner = following
+        last = PACK - 1
+        own = own_term(h1[last], 1)
 
         out_view = out.rearrange("(m p) s -> p m s", p=P)
         for tb in range(TOKEN_BLOCKS):
             tokens = slice(tb * P, (tb + 1) * P)
-            for b in range(1, FEATURE_TILES):
-                term = ring.tile([P, P], F32, name="partner2", bufs=6)
-                nc.vector.tensor_tensor(
-                    term[:], h1[b][:].indirect(entries(mix2_tile, tb * P, P)), oth2_row[:, tokens], MULT
-                )
-                add_into_h2(term[:], b, tb, stop=(b == FEATURE_TILES - 1))
-            h2_rows = ring.tile([P, 2, P, 2], BF16, name="h2_rows")
-            nc.scalar.copy(h2_rows[:], h2_banks[tb][:].rearrange("s (p u e) -> s u p e", u=2, e=2))
-            pairs = h2_rows[:].rearrange("s u p e -> s (u p e)").bitcast(F32)
-            pair_bank = psum.tile([P, 2, P], F32, name="pair_bank", tag="acc", bufs=2)
-            for u in range(2):
-                nc.tensor.transpose(pair_bank[:, u, :], pairs[:, u * P : (u + 1) * P], identity[:])
-            h2_grouped = ring.tile([P, P * PACK], BF16, name="h2_grouped", align_bytes=64)
-            nc.scalar.copy(
-                h2_grouped[:].bitcast(F32).rearrange("p (s u) -> p s u", u=2),
-                pair_bank[:].rearrange("p u s -> p s u"),
+            partner = partner_term(h1[last], mix2_tile, oth2_row, tb * P, P)
+            nc.vector.tensor_tensor(h2[:, last, tokens], own[:, tokens], partner[:], ADD)
+            h2_grouped = ring.tile([P, P * PACK], BF16, name="h2_grouped", bufs=TOKEN_BLOCKS - 1, align_bytes=64)
+            interleave(
+                nc.scalar.copy if tb + 1 < TOKEN_BLOCKS else nc.vector.tensor_copy, h2_grouped[:], h2[:, :, tokens]
             )
             h2_codes, h2_scales = quantise(f"h2_{tb}", h2_grouped[:], P)
-            result = psum.tile([P, OUT_TILES, P], F32, name="result", tag=("turned", "back")[tb % 2])
+            result = psum.tile([P, OUT_TILES, P], F32, name="bank")
             for m in range(OUT_TILES):
                 nc.tensor.matmul_mx(
                     out=result[:, m, :],
@@ -228,9 +219,7 @@ def tile_picked_ybutter_relu_p_kernel(
                     start=True,
                     stop=True,
                 )
-            staged = ring.tile([P, OUT_TILES, P], F32, name="staged", bufs=4)
-            if tb < 2:
-                nc.scalar.copy(staged[:], result[:])
-            else:
-                nc.vector.tensor_copy(staged[:], result[:])
+            staged = ring.tile([P, OUT_TILES, P], F32, name="staged", bufs=TOKEN_BLOCKS)
+            copy_out = nc.scalar.copy if tb % 2 == 0 else nc.vector.tensor_copy
+            copy_out(staged[:], result[:])
             nc.sync.dma_start(out_view[:, :, tokens], staged[:])

@@ -25,6 +25,8 @@ PASSES = K // K_PASS
 TOKEN_BLOCKS = S // P
 OUT_TILES = N // P
 SPARE = 16
+SPARE_COPY = 192
+HALF = H // 2
 LIST_ROWS = 16
 
 
@@ -35,7 +37,12 @@ def tile_picked_ybutter_relu_p_kernel(
     with ExitStack() as ctx:
         keep = ctx.enter_context(tc.tile_pool(name="keep", bufs=1))
         ring = ctx.enter_context(tc.tile_pool(name="ring", bufs=2))
-        psum = ctx.enter_context(tc.psum_pool(name="psum", bufs=8))
+        psum = ctx.enter_context(tc.psum_pool(name="psum", bufs=1))
+        banks = [psum.tile([P, S], F32, name=f"bank{b}") for b in range(8)]
+
+        def blocks(tile):
+            return tile[:].rearrange("p (b c) -> p b c", c=P)
+
 
         def entries(list_tile, first, count):
             return list_tile[:, first // LIST_ROWS : (first + count) // LIST_ROWS]
@@ -57,158 +64,170 @@ def tile_picked_ybutter_relu_p_kernel(
         mix2_tile = keep.tile([P, S // LIST_ROWS], U16, name="mix2_tile")
         nc.sync.dma_start(offs_tile[:], offs)
 
-        own_rows = keep.tile([P, P], F32, name="own_rows")
-        for v, own in enumerate((own1, own2)):
-            nc.scalar.dma_start(
-                own_rows[64 * v : 64 * (v + 1), :], own[:16, :].rearrange("r (b c) -> (r b) c", c=P)
-            )
         scale_table = keep.tile([P, T], U8, name="scale_table")
         nc.gpsimd.memset(scale_table[:].bitcast(I32), 0)
-        for q in range(4):
-            nc.scalar.dma_start(
-                scale_table[32 * q : 32 * q + 4 * PASSES, :].bitcast(I32),
-                x_scales[:, 4 * q : 4 * q + 4, :].bitcast(I32),
-            )
-
-        w1_raw, word_tables = [], []
-        for g in range(PASSES):
-            raw = keep.tile([P, PACK, H], F32, name=f"w1_raw{g}")
-            nc.sync.dma_start(raw[:], w1[g * K_PASS : (g + 1) * K_PASS, :].rearrange("(p j) c -> p j c", j=PACK))
-            w1_raw.append(raw)
-            table = keep.tile([P, T], U32, name=f"word_table{g}")
-            nc.sync.dma_start(table[:].bitcast(I32), x_words[g].rearrange("p n t -> p (n t)").bitcast(I32))
-            word_tables.append(table)
-        w2_raw = keep.tile([P, PACK, N], F32, name="w2_raw")
-        nc.sync.dma_start(w2_raw[:], w2.rearrange("(p j) n -> p j n", j=PACK))
-        nc.sync.dma_start(mix1_tile[:], mix1)
-        oth1_row = keep.tile([P, S], F32, name="oth1_row")
-        nc.sync.dma_start(oth1_row[:], oth1)
-        nc.sync.dma_start(mix2_tile[:], mix2)
-        oth2_row = keep.tile([P, S], F32, name="oth2_row")
-        nc.sync.dma_start(oth2_row[:], oth2)
-
         identity = keep.tile([P, P], F32, name="identity")
         make_identity(nc, identity[:])
-        y = [keep.tile([P, S + SPARE], F32, name=f"y{t}") for t in range(PACK)]
-        h1 = [keep.tile([P, S + SPARE], F32, name=f"h1_{t}") for t in range(PACK)]
-        for window in y + h1:
-            nc.gpsimd.memset(window[:, S:], 0.0)
+        factor_rows = keep.tile([P, P], F32, name="factor_rows")
+        nc.vector.memset(factor_rows[:], 0.0)
 
-        own_bank = psum.tile([P, P], F32, name="bank")
-        nc.tensor.transpose(own_bank[:], own_rows[:], identity[:])
-        own_cols = keep.tile([P, 2, TOKEN_BLOCKS], F32, name="own_cols")
-        nc.scalar.copy(own_cols[:], own_bank[:].rearrange("s (v r) -> s v r", v=2)[:, :, :TOKEN_BLOCKS])
+        def load_w1(v, g):
+            raw = keep.tile([P, PACK, HALF], F32, name=f"w1_raw{v}_{g}")
+            rows = w1[g * K_PASS : (g + 1) * K_PASS, v * HALF : (v + 1) * HALF]
+            nc.sync.dma_start(raw[:], rows.rearrange("(p j) c -> p j c", j=PACK))
+            return raw
 
-        def quantised_w1(g, copies):
-            grouped = keep.tile([P, PACK, P, PACK], BF16, name=f"w1_grouped{g}", align_bytes=64)
-            share = P // len(copies)
-            for n, copy in enumerate(copies):
-                m = slice(n * share, (n + 1) * share)
-                copy(
-                    grouped[:, :, m, :].rearrange("p t m j -> p m j t"),
-                    w1_raw[g][:].rearrange("p j (m t) -> p m j t", t=PACK)[:, m, :, :],
-                )
-            return quantise(f"w1_{g}", grouped[:].rearrange("p t m j -> p (t m j)"), H)
+        w1_raw, word_tables = {}, []
+        for g in range(PASSES):
+            w1_raw[0, g] = load_w1(0, g)
+            if g == 0:
+                for q in range(4):
+                    nc.sync.dma_start(
+                        scale_table[32 * q : 32 * q + 4 * PASSES, :].bitcast(I32),
+                        x_scales[:, 4 * q : 4 * q + 4, :].bitcast(I32),
+                    )
+            else:
+                for n, factor in enumerate((own1, own2, oth2, oth1)):
+                    nc.sync.dma_start(
+                        factor_rows[TOKEN_BLOCKS * n : TOKEN_BLOCKS * (n + 1), :],
+                        factor[:1, :].rearrange("r (b c) -> (r b) c", c=P),
+                    )
+            table = keep.tile([P, T], U32, name=f"word_table{g}", tag=f"table{g}", align_bytes=64)
+            nc.sync.dma_start(table[:].bitcast(I32), x_words[g].rearrange("p n t -> p (n t)").bitcast(I32))
+            word_tables.append(table)
+        w1_raw[1, 0] = load_w1(1, 0)
+        nc.sync.dma_start(mix1_tile[:], mix1)
+        w1_raw[1, 1] = load_w1(1, 1)
+        nc.sync.dma_start(mix2_tile[:], mix2)
+        w2_raw = keep.tile([P, PACK, N], F32, name="w2_raw")
+        nc.sync.dma_start(w2_raw[:], w2.rearrange("(p j) n -> p j n", j=PACK))
+
+        y = [keep.tile([P, S + SPARE], F32, name=f"y{t}", tag=f"y{t}", align_bytes=64) for t in range(PACK)]
+        h1 = [keep.tile([P, S + SPARE_COPY * (t + 1 < PACK)], F32, name=f"h1_{t}") for t in range(PACK)]
+        for window in y + h1[: PACK - 1]:
+            nc.vector.memset(window[:, S:], 0.0)
+
+        def token_cols(tb):
+            return slice(tb * P, (tb + 1) * P)
+
+        def quantised_w1(v, g, tag, copy=nc.scalar.copy):
+            grouped = keep.tile([P, 2, P, PACK], BF16, name=f"w1_grouped{v}_{g}", tag=tag, align_bytes=64)
+            copy(
+                grouped[:].rearrange("p u (m e) j -> p m j u e", e=2),
+                w1_raw[v, g][:].rearrange("p j (m u e) -> p m j u e", u=2, e=2),
+            )
+            return quantise(f"w1_{v}_{g}", grouped[:].rearrange("p u c j -> p (u c j)"), HALF)
 
         x_codes = [keep.tile([P, S], U32, name=f"x_codes{g}", align_bytes=64) for g in range(PASSES)]
         x_bytes = keep.tile([P, S], U8, name="x_bytes", align_bytes=64)
 
         half = S // 2
         pieces = [(0, 0, half), (0, half, half)] + [(t, 0, S) for t in range(1, PACK)]
-        accs = [
-            psum.tile([P, count], F32, name="bank") for t, first, count in pieces
-        ]
+        accs = [banks[n][:, :count] for n, (t, first, count) in enumerate(pieces)]
 
-        def first_product_pass(g, weights, piece, acc):
-            t, first, count = piece
+        def first_product_pass(g, weights, n):
+            t, first, count = pieces[n]
             cols = slice(first, first + count)
             nc.tensor.matmul_mx(
-                out=acc[:],
-                lhsT=weights[0][:, t * P : (t + 1) * P].bitcast(FP8X4),
-                lhsT_scale=weights[1][:, t * P : (t + 1) * P],
+                out=accs[n],
+                lhsT=weights[0][:, token_cols(t % 2)].bitcast(FP8X4),
+                lhsT_scale=weights[1][:, token_cols(t % 2)],
                 rhs=x_codes[g][:, cols].bitcast(FP8X4),
                 rhs_scale=x_bytes[4 * g :, cols],
                 start=(g == 0),
                 stop=(g == PASSES - 1),
             )
 
-        weights = quantised_w1(0, [nc.scalar.copy])
+        def finish_y(weights, n):
+            t, first, count = pieces[n]
+            first_product_pass(1, weights, n)
+            nc.scalar.activation(y[t][:, first : first + count], accs[n], RELU)
+
+        nc.tensor.transpose(banks[5][:, :P], factor_rows[:], identity[:])
+        factor_cols = keep.tile([P, 4, TOKEN_BLOCKS], F32, name="factor_cols")
+        nc.scalar.copy(factor_cols[:], banks[5][:, : 4 * TOKEN_BLOCKS].rearrange("s (v r) -> s v r", v=4))
+        first_cols = keep.tile([P, TOKEN_BLOCKS], F32, name="first_cols", tag="last_w1", align_bytes=64)
+        nc.scalar.copy(first_cols[:], banks[5][:, :TOKEN_BLOCKS])
+        for tb in range(TOKEN_BLOCKS):
+            nc.tensor.transpose(
+                banks[6][:, token_cols(tb)], factor_cols[:, 3, tb : tb + 1].to_broadcast([P, P]), identity[:]
+            )
+        oth1_row = keep.tile([P, S], F32, name="oth1_row")
+        nc.scalar.copy(oth1_row[:], banks[6][:])
+
+        weights = quantised_w1(0, 0, "early0")
         nc.vector.tensor_copy(x_bytes[:], scale_table[:].indirect(offs_tile[:]))
         nc.vector.tensor_copy(x_codes[0][:], word_tables[0][:].indirect(offs_tile[:]))
-        for piece, acc in zip(pieces, accs):
-            first_product_pass(0, weights, piece, acc)
-        weights = quantised_w1(1, [nc.scalar.copy, nc.vector.tensor_copy])
+        for n in range(3):
+            first_product_pass(0, weights, n)
+        weights = quantised_w1(0, 1, "early1")
         for first in (0, half):
             nc.vector.tensor_copy(
                 x_codes[1][:, first : first + half], word_tables[1][:].indirect(entries(offs_tile, first, half))
             )
+        late_weights = quantised_w1(1, 0, "table1", nc.vector.tensor_copy)
+        for n in range(3):
+            finish_y(weights, n)
 
-        w2_grouped = keep.tile([P, N * PACK], BF16, name="w2_grouped", align_bytes=64)
-        interleave(nc.vector.tensor_copy, w2_grouped[:], w2_raw[:])
-        w2_codes, w2_scales = quantise("w2", w2_grouped[:], N)
 
-        def finish_y(n):
-            t, first, count = pieces[n]
-            first_product_pass(1, weights, pieces[n], accs[n])
-            nc.scalar.activation(y[t][:, first : first + count], accs[n][:], RELU)
-
-        def own_term(values, v):
-            turned = psum.tile([P, TOKEN_BLOCKS, P], F32, name="bank")
-            scaled = ring.tile([P, TOKEN_BLOCKS, P], F32, name="scaled", bufs=3)
-            back = psum.tile([P, S], F32, name="bank")
+        def own_term(t, turned, back):
+            scaled = ring.tile([P, S], F32, name="scaled", align_bytes=64)
+            own_cols = first_cols[:] if t == 0 else factor_cols[:, 0, :]
             for tb in range(TOKEN_BLOCKS):
-                nc.tensor.transpose(turned[:, tb, :], values[:, tb * P : (tb + 1) * P], identity[:])
+                nc.tensor.transpose(turned[:, token_cols(tb)], y[t][:, token_cols(tb)], identity[:])
             for tb in range(TOKEN_BLOCKS):
-                nc.scalar.activation(scaled[:, tb, :], turned[:, tb, :], COPY, scale=own_cols[:, v, tb : tb + 1])
+                nc.scalar.activation(
+                    scaled[:, token_cols(tb)], turned[:, token_cols(tb)], COPY, scale=own_cols[:, tb : tb + 1]
+                )
             for tb in range(TOKEN_BLOCKS):
-                nc.tensor.transpose(back[:, tb * P : (tb + 1) * P], scaled[:, tb, :], identity[:])
+                nc.tensor.transpose(back[:, token_cols(tb)], scaled[:, token_cols(tb)], identity[:])
             return back
 
-        def partner_term(window, list_tile, factor, first, count):
-            term = ring.tile([P, count], F32, name=f"partner{count}", bufs=3 if count == S else 2)
-            nc.vector.tensor_tensor(
-                term[:], window[:].indirect(entries(list_tile, first, count)), factor[:, first : first + count], MULT
-            )
+        def partner_term(t):
+            term = keep.tile([P, S], F32, name=f"partner{t}")[:]
+            nc.vector.tensor_tensor(term, y[t][:].indirect(mix1_tile[:]), oth1_row[:], MULT)
             return term
 
-        h2 = keep.tile([P, PACK, S], BF16, name="h2")
+        picked = [None] + [keep.tile([P, S], F32, name=f"picked{t}")[:] for t in range(1, PACK)]
+        h2_turned = [keep.tile([P, 2, 2 * P], BF16, name=f"h2_turned{tb}") for tb in range(TOKEN_BLOCKS)]
 
-        finish_y(0)
-        finish_y(1)
-        finish_y(2)
-        partner = partner_term(y[0], mix1_tile, oth1_row, 0, S)
-        for t in range(PACK):
-            own = own_term(y[t], 0)
-            if t + 2 < PACK:
-                finish_y(t + 3)
-            following = (
-                partner_term(y[t + 1], mix1_tile, oth1_row, 0, S)
-                if t + 1 < PACK
-                else partner_term(h1[0], mix2_tile, oth2_row, 0, S)
+        def pick(t):
+            nc.vector.tensor_copy(picked[t], h1[t][:].indirect(mix2_tile[:]))
+
+        def turn_pair(bank, first, values, v, tb):
+            pair = bank[:, first : first + 2 * P].rearrange("s (u c) -> s u c", u=2)
+            for u in range(2):
+                nc.tensor.transpose(pair[:, u, :], values[2 * v + u][:, token_cols(tb)], identity[:])
+            return pair
+
+        def own_pairs(v, bank_pair):
+            scaled = []
+            for b, bank in enumerate(bank_pair):
+                pairs = [turn_pair(bank, n * 2 * P, h1, v, 2 * b + n) for n in range(2)]
+                for n, pair in enumerate(pairs):
+                    tb = 2 * b + n
+                    term = keep.tile([P, 2, P], F32, name=f"own2_term{v}_{tb}")
+                    nc.scalar.activation(term[:], pair, COPY, scale=factor_cols[:, 1, tb : tb + 1])
+                    scaled.append(term)
+            return scaled
+
+        def combine(v, tb, pair, own):
+            nc.vector.scalar_tensor_tensor(
+                h2_turned[tb][:, :, token_cols(v)], pair, factor_cols[:, 2, tb : tb + 1], own[:], MULT, ADD
             )
-            nc.vector.tensor_tensor(h1[t][:, :S], own[:], partner[:], ADD)
-            partner = following
-
-        for t in range(PACK - 1):
-            own = own_term(h1[t], 1)
-            if t + 2 < PACK:
-                following = partner_term(h1[t + 1], mix2_tile, oth2_row, 0, S)
-            nc.vector.tensor_tensor(h2[:, t, :], own[:], partner[:], ADD)
-            partner = following
-        last = PACK - 1
-        own = own_term(h1[last], 1)
 
         out_view = out.rearrange("(m p) s -> p m s", p=P)
-        for tb in range(TOKEN_BLOCKS):
-            tokens = slice(tb * P, (tb + 1) * P)
-            partner = partner_term(h1[last], mix2_tile, oth2_row, tb * P, P)
-            nc.vector.tensor_tensor(h2[:, last, tokens], own[:, tokens], partner[:], ADD)
-            h2_grouped = ring.tile([P, P * PACK], BF16, name="h2_grouped", bufs=TOKEN_BLOCKS - 1, align_bytes=64)
-            interleave(
-                nc.scalar.copy if tb + 1 < TOKEN_BLOCKS else nc.vector.tensor_copy, h2_grouped[:], h2[:, :, tokens]
+
+        def second_product(tb, bank):
+            words = blocks(bank)[:, :2, :]
+            for u in range(2):
+                nc.tensor.transpose(words[:, u, :], h2_turned[tb][:, u, :].bitcast(F32), identity[:])
+            h2_grouped = keep.tile([P, P * PACK], BF16, name=f"h2_grouped{tb}", align_bytes=64)
+            nc.scalar.copy(
+                h2_grouped[:].bitcast(F32).rearrange("p (s u) -> p s u", u=2), words.rearrange("p u s -> p s u")
             )
             h2_codes, h2_scales = quantise(f"h2_{tb}", h2_grouped[:], P)
-            result = psum.tile([P, OUT_TILES, P], F32, name="bank")
+            result = blocks(bank)[:, 2:, :]
             for m in range(OUT_TILES):
                 nc.tensor.matmul_mx(
                     out=result[:, m, :],
@@ -220,6 +239,41 @@ def tile_picked_ybutter_relu_p_kernel(
                     stop=True,
                 )
             staged = ring.tile([P, OUT_TILES, P], F32, name="staged", bufs=TOKEN_BLOCKS)
-            copy_out = nc.scalar.copy if tb % 2 == 0 else nc.vector.tensor_copy
-            copy_out(staged[:], result[:])
-            nc.sync.dma_start(out_view[:, :, tokens], staged[:])
+            nc.scalar.copy(staged[:], result)
+            nc.sync.dma_start(out_view[:, :, token_cols(tb)], staged[:])
+
+        partners = [partner_term(0), partner_term(1)]
+        owns = [own_term(0, banks[5], banks[6])]
+        for n in (3, 4):
+            first_product_pass(0, late_weights, n)
+        weights = quantised_w1(1, 1, "last_w1")
+        picked[0] = keep.tile([P, S], F32, name="picked0", tag="last_w1", align_bytes=64)[:]
+        owns.append(own_term(1, banks[7], banks[0]))
+        for n in (3, 4):
+            finish_y(weights, n)
+
+        for t in range(2):
+            nc.vector.tensor_tensor(h1[t][:, :S], owns[t][:], partners[t], ADD)
+            pick(t)
+
+        first_pairs = [turn_pair(banks[(6, 0)[tb // 2]], tb % 2 * 2 * P, picked, 0, tb) for tb in range(TOKEN_BLOCKS)]
+
+        partners = [partner_term(2), partner_term(3)]
+        owns = [own_term(2, banks[5], banks[7]), own_term(3, banks[1], banks[2])]
+        first_owns = own_pairs(0, (banks[3], banks[4]))
+        for tb in range(TOKEN_BLOCKS):
+            combine(0, tb, first_pairs[tb], first_owns[tb])
+        w2_grouped = keep.tile([P, N * PACK], BF16, name="w2_grouped", tag="y2", align_bytes=64)
+        interleave(nc.scalar.copy, w2_grouped[:], w2_raw[:])
+        w2_codes, w2_scales = quantise("w2", w2_grouped[:], N)
+        nc.vector.tensor_tensor(h1[2][:, :S], owns[0][:], partners[0], ADD)
+        nc.vector.tensor_tensor(h1[3][:], owns[1][:], partners[1], ADD)
+        pick(2)
+        owns = own_pairs(1, (banks[5], banks[1]))
+        for tb in range(TOKEN_BLOCKS):
+            nc.vector.tensor_copy(picked[3][:, token_cols(tb)], h1[3][:].indirect(entries(mix2_tile, tb * P, P)))
+        for tb in range(TOKEN_BLOCKS):
+            pair = turn_pair(banks[(3, 4, 7, 2)[tb]], 0, picked, 1, tb)
+            combine(1, tb, pair, owns[tb])
+        for tb in range(TOKEN_BLOCKS):
+            second_product(tb, banks[(6, 0, 5, 1)[tb]])

@@ -53,8 +53,8 @@ def tile_picked_ybutter_relu_p_kernel(
                 planes.rearrange("p j (c i) -> p c j i", i=4),
             )
 
-        def quantise(name, grouped, width):
-            codes = keep.tile([P, width], U32, name=name + "_codes", align_bytes=64)
+        def quantise(name, grouped, width, tag=""):
+            codes = keep.tile([P, width], U32, name=name + "_codes", tag=tag or name, align_bytes=64)
             scales = keep.tile([P, width], U8, name=name + "_scales", align_bytes=64)
             nc.vector.quantize_mx(out=codes[:].bitcast(FP8X4), scales=scales[:], in_=grouped)
             return codes, scales
@@ -110,20 +110,23 @@ def tile_picked_ybutter_relu_p_kernel(
         def token_cols(tb):
             return slice(tb * P, (tb + 1) * P)
 
-        def quantised_w1(v, g, tag, copy=nc.scalar.copy):
+        def regrouped_w1(v, g, tag, copy=nc.scalar.copy):
             grouped = keep.tile([P, 2, P, PACK], BF16, name=f"w1_grouped{v}_{g}", tag=tag, align_bytes=64)
             copy(
                 grouped[:].rearrange("p u (m e) j -> p m j u e", e=2),
                 w1_raw[v, g][:].rearrange("p j (m u e) -> p m j u e", u=2, e=2),
             )
-            return quantise(f"w1_{v}_{g}", grouped[:].rearrange("p u c j -> p (u c j)"), HALF)
+            return grouped[:].rearrange("p u c j -> p (u c j)")
+
+        def quantised_w1(v, g, tag):
+            return quantise(f"w1_{v}_{g}", regrouped_w1(v, g, tag), HALF)
 
         x_codes = [keep.tile([P, S], U32, name=f"x_codes{g}", align_bytes=64) for g in range(PASSES)]
         x_bytes = keep.tile([P, S], U8, name="x_bytes", align_bytes=64)
 
         half = S // 2
         pieces = [(0, 0, half), (0, half, half)] + [(t, 0, S) for t in range(1, PACK)]
-        accs = [banks[n][:, :count] for n, (t, first, count) in enumerate(pieces)]
+        accs = [banks[b][:, :count] for b, (t, first, count) in zip((0, 1, 2, 5, 7), pieces)]
 
         def first_product_pass(g, weights, n):
             t, first, count = pieces[n]
@@ -165,7 +168,7 @@ def tile_picked_ybutter_relu_p_kernel(
             nc.vector.tensor_copy(
                 x_codes[1][:, first : first + half], word_tables[1][:].indirect(entries(offs_tile, first, half))
             )
-        late_weights = quantised_w1(1, 0, "table1", nc.vector.tensor_copy)
+        late_grouped = regrouped_w1(1, 0, "table1", nc.vector.tensor_copy)
         for n in range(3):
             finish_y(weights, n)
 
@@ -188,7 +191,7 @@ def tile_picked_ybutter_relu_p_kernel(
             nc.vector.tensor_tensor(term, y[t][:].indirect(mix1_tile[:]), oth1_row[:], MULT)
             return term
 
-        picked = [None] + [keep.tile([P, S], F32, name=f"picked{t}")[:] for t in range(1, PACK)]
+        picked = [None] + [keep.tile([P, S], F32, name=f"picked{t}", tag=f"picked{t}", align_bytes=64)[:] for t in range(1, PACK)]
         h2_turned = [keep.tile([P, 2, 2 * P], BF16, name=f"h2_turned{tb}") for tb in range(TOKEN_BLOCKS)]
 
         def pick(t):
@@ -239,41 +242,41 @@ def tile_picked_ybutter_relu_p_kernel(
                     stop=True,
                 )
             staged = ring.tile([P, OUT_TILES, P], F32, name="staged", bufs=TOKEN_BLOCKS)
-            nc.scalar.copy(staged[:], result)
+            copy_out = nc.vector.tensor_copy if tb + 1 == TOKEN_BLOCKS else nc.scalar.copy
+            copy_out(staged[:], result)
             nc.sync.dma_start(out_view[:, :, token_cols(tb)], staged[:])
 
         partners = [partner_term(0), partner_term(1)]
         owns = [own_term(0, banks[5], banks[6])]
-        for n in (3, 4):
-            first_product_pass(0, late_weights, n)
+        late_weights = quantise("w1_1_0", late_grouped, HALF, "y0")
         weights = quantised_w1(1, 1, "last_w1")
         picked[0] = keep.tile([P, S], F32, name="picked0", tag="last_w1", align_bytes=64)[:]
         owns.append(own_term(1, banks[7], banks[0]))
         for n in (3, 4):
+            first_product_pass(0, late_weights, n)
             finish_y(weights, n)
 
         for t in range(2):
             nc.vector.tensor_tensor(h1[t][:, :S], owns[t][:], partners[t], ADD)
             pick(t)
 
-        first_pairs = [turn_pair(banks[(6, 0)[tb // 2]], tb % 2 * 2 * P, picked, 0, tb) for tb in range(TOKEN_BLOCKS)]
-
         partners = [partner_term(2), partner_term(3)]
-        owns = [own_term(2, banks[5], banks[7]), own_term(3, banks[1], banks[2])]
-        first_owns = own_pairs(0, (banks[3], banks[4]))
-        for tb in range(TOKEN_BLOCKS):
-            combine(0, tb, first_pairs[tb], first_owns[tb])
+        owns = [own_term(2, banks[3], banks[4]), own_term(3, banks[1], banks[2])]
+        first_owns = own_pairs(0, (banks[5], banks[7]))
         w2_grouped = keep.tile([P, N * PACK], BF16, name="w2_grouped", tag="y2", align_bytes=64)
         interleave(nc.scalar.copy, w2_grouped[:], w2_raw[:])
-        w2_codes, w2_scales = quantise("w2", w2_grouped[:], N)
         nc.vector.tensor_tensor(h1[2][:, :S], owns[0][:], partners[0], ADD)
-        nc.vector.tensor_tensor(h1[3][:], owns[1][:], partners[1], ADD)
         pick(2)
-        owns = own_pairs(1, (banks[5], banks[1]))
+        nc.vector.tensor_tensor(h1[3][:], owns[1][:], partners[1], ADD)
+        owns = own_pairs(1, (banks[3], banks[1]))
+        first_pairs = [turn_pair(banks[(4, 2)[tb // 2]], tb % 2 * 2 * P, picked, 0, tb) for tb in range(TOKEN_BLOCKS)]
         for tb in range(TOKEN_BLOCKS):
-            nc.vector.tensor_copy(picked[3][:, token_cols(tb)], h1[3][:].indirect(entries(mix2_tile, tb * P, P)))
+            combine(0, tb, first_pairs[tb], first_owns[tb])
+        for first in (0, half):
+            nc.vector.tensor_copy(picked[3][:, first : first + half], h1[3][:].indirect(entries(mix2_tile, first, half)))
         for tb in range(TOKEN_BLOCKS):
-            pair = turn_pair(banks[(3, 4, 7, 2)[tb]], 0, picked, 1, tb)
+            pair = turn_pair(banks[(5, 7, 6, 0)[tb]], 0, picked, 1, tb)
             combine(1, tb, pair, owns[tb])
+        w2_codes, w2_scales = quantise("w2", w2_grouped[:], N, "picked3")
         for tb in range(TOKEN_BLOCKS):
-            second_product(tb, banks[(6, 0, 5, 1)[tb]])
+            second_product(tb, banks[(4, 2, 3, 1)[tb]])

@@ -22,12 +22,16 @@ P = 128
 PACK = 4
 K_PASS = P * PACK
 PASSES = K // K_PASS
+TILES = H // P
+HALF = H // 2
+HALF_TOKENS = S // 2
 TOKEN_BLOCKS = S // P
 OUT_TILES = N // P
-SPARE = 16
-SPARE_COPY = 192
-HALF = H // 2
+QUADRANTS = 4
 LIST_ROWS = 16
+SPARE_PRODUCT = 16
+SPARE_COPY = 192
+OWN1, OWN2, OTH2, OTH1 = range(4)
 
 
 def tile_picked_ybutter_relu_p_kernel(
@@ -40,18 +44,11 @@ def tile_picked_ybutter_relu_p_kernel(
         psum = ctx.enter_context(tc.psum_pool(name="psum", bufs=1))
         banks = [psum.tile([P, S], F32, name=f"bank{b}") for b in range(8)]
 
-        def blocks(tile):
-            return tile[:].rearrange("p (b c) -> p b c", c=P)
-
+        def block(b):
+            return slice(b * P, (b + 1) * P)
 
         def entries(list_tile, first, count):
             return list_tile[:, first // LIST_ROWS : (first + count) // LIST_ROWS]
-
-        def interleave(copy, grouped, planes):
-            copy(
-                grouped.rearrange("p (c i j) -> p c j i", i=4, j=PACK),
-                planes.rearrange("p j (c i) -> p c j i", i=4),
-            )
 
         def quantise(name, grouped, width, tag=""):
             codes = keep.tile([P, width], U32, name=name + "_codes", tag=tag or name, align_bytes=64)
@@ -77,24 +74,25 @@ def tile_picked_ybutter_relu_p_kernel(
             nc.sync.dma_start(raw[:], rows.rearrange("(p j) c -> p j c", j=PACK))
             return raw
 
-        w1_raw, word_tables = {}, []
-        for g in range(PASSES):
-            w1_raw[0, g] = load_w1(0, g)
-            if g == 0:
-                for q in range(4):
-                    nc.sync.dma_start(
-                        scale_table[32 * q : 32 * q + 4 * PASSES, :].bitcast(I32),
-                        x_scales[:, 4 * q : 4 * q + 4, :].bitcast(I32),
-                    )
-            else:
-                for n, factor in enumerate((own1, own2, oth2, oth1)):
-                    nc.sync.dma_start(
-                        factor_rows[TOKEN_BLOCKS * n : TOKEN_BLOCKS * (n + 1), :],
-                        factor[:1, :].rearrange("r (b c) -> (r b) c", c=P),
-                    )
+        def load_words(g):
             table = keep.tile([P, T], U32, name=f"word_table{g}", tag=f"table{g}", align_bytes=64)
             nc.sync.dma_start(table[:].bitcast(I32), x_words[g].rearrange("p n t -> p (n t)").bitcast(I32))
-            word_tables.append(table)
+            return table
+
+        w1_raw = {(0, 0): load_w1(0, 0)}
+        for q in range(QUADRANTS):
+            nc.sync.dma_start(
+                scale_table[32 * q : 32 * q + 4 * PASSES, :].bitcast(I32),
+                x_scales[:, 4 * q : 4 * q + 4, :].bitcast(I32),
+            )
+        word_tables = [load_words(0)]
+        w1_raw[0, 1] = load_w1(0, 1)
+        for n, factor in enumerate((own1, own2, oth2, oth1)):
+            nc.sync.dma_start(
+                factor_rows[TOKEN_BLOCKS * n : TOKEN_BLOCKS * (n + 1), :],
+                factor[:1, :].rearrange("r (b c) -> (r b) c", c=P),
+            )
+        word_tables.append(load_words(1))
         w1_raw[1, 0] = load_w1(1, 0)
         nc.sync.dma_start(mix1_tile[:], mix1)
         w1_raw[1, 1] = load_w1(1, 1)
@@ -102,15 +100,22 @@ def tile_picked_ybutter_relu_p_kernel(
         w2_raw = keep.tile([P, PACK, N], F32, name="w2_raw")
         nc.sync.dma_start(w2_raw[:], w2.rearrange("(p j) n -> p j n", j=PACK))
 
-        y = [keep.tile([P, S + SPARE], F32, name=f"y{t}", tag=f"y{t}", align_bytes=64) for t in range(PACK)]
-        h1 = [keep.tile([P, S + SPARE_COPY * (t + 1 < PACK)], F32, name=f"h1_{t}") for t in range(PACK)]
-        for window in y + h1[: PACK - 1]:
+        y = [keep.tile([P, S + SPARE_PRODUCT], F32, name=f"y{t}", tag=f"y{t}", align_bytes=64) for t in range(TILES)]
+        h1 = [keep.tile([P, S + SPARE_COPY * (t + 1 < TILES)], F32, name=f"h1_{t}") for t in range(TILES)]
+        for window in y + h1[: TILES - 1]:
             nc.vector.memset(window[:, S:], 0.0)
 
-        def token_cols(tb):
-            return slice(tb * P, (tb + 1) * P)
+        nc.tensor.transpose(banks[5][:, :P], factor_rows[:], identity[:])
+        factor_cols = keep.tile([P, 4, TOKEN_BLOCKS], F32, name="factor_cols")
+        nc.scalar.copy(factor_cols[:], banks[5][:, : 4 * TOKEN_BLOCKS].rearrange("s (n b) -> s n b", n=4))
+        own1_for_tile0 = keep.tile([P, TOKEN_BLOCKS], F32, name="own1_for_tile0", tag="last_w1", align_bytes=64)
+        nc.scalar.copy(own1_for_tile0[:], banks[5][:, OWN1 * TOKEN_BLOCKS : (OWN1 + 1) * TOKEN_BLOCKS])
+        for b in range(TOKEN_BLOCKS):
+            nc.tensor.transpose(banks[6][:, block(b)], factor_cols[:, OTH1, b : b + 1].to_broadcast([P, P]), identity[:])
+        oth1_row = keep.tile([P, S], F32, name="oth1_row")
+        nc.scalar.copy(oth1_row[:], banks[6][:])
 
-        def regrouped_w1(v, g, tag, copy=nc.scalar.copy):
+        def regrouped_w1(v, g, tag, copy):
             grouped = keep.tile([P, 2, P, PACK], BF16, name=f"w1_grouped{v}_{g}", tag=tag, align_bytes=64)
             copy(
                 grouped[:].rearrange("p u (m e) j -> p m j u e", e=2),
@@ -118,165 +123,154 @@ def tile_picked_ybutter_relu_p_kernel(
             )
             return grouped[:].rearrange("p u c j -> p (u c j)")
 
-        def quantised_w1(v, g, tag):
-            return quantise(f"w1_{v}_{g}", regrouped_w1(v, g, tag), HALF)
-
         x_codes = [keep.tile([P, S], U32, name=f"x_codes{g}", align_bytes=64) for g in range(PASSES)]
         x_bytes = keep.tile([P, S], U8, name="x_bytes", align_bytes=64)
 
-        half = S // 2
-        pieces = [(0, 0, half), (0, half, half)] + [(t, 0, S) for t in range(1, PACK)]
-        accs = [banks[b][:, :count] for b, (t, first, count) in zip((0, 1, 2, 5, 7), pieces)]
+        first_half = [(0, 0, HALF_TOKENS, 0), (0, HALF_TOKENS, HALF_TOKENS, 1), (1, 0, S, 2)]
+        second_half = [(2, 0, S, 5), (3, 0, S, 7)]
 
-        def first_product_pass(g, weights, n):
-            t, first, count = pieces[n]
-            cols = slice(first, first + count)
+        def first_product_pass(g, weights, piece):
+            t, first, count, bank = piece
+            tokens = slice(first, first + count)
+            codes, scales = weights
             nc.tensor.matmul_mx(
-                out=accs[n],
-                lhsT=weights[0][:, token_cols(t % 2)].bitcast(FP8X4),
-                lhsT_scale=weights[1][:, token_cols(t % 2)],
-                rhs=x_codes[g][:, cols].bitcast(FP8X4),
-                rhs_scale=x_bytes[4 * g :, cols],
+                out=banks[bank][:, :count],
+                lhsT=codes[:, block(t % 2)].bitcast(FP8X4),
+                lhsT_scale=scales[:, block(t % 2)],
+                rhs=x_codes[g][:, tokens].bitcast(FP8X4),
+                rhs_scale=x_bytes[4 * g :, tokens],
                 start=(g == 0),
                 stop=(g == PASSES - 1),
             )
 
-        def finish_y(weights, n):
-            t, first, count = pieces[n]
-            first_product_pass(1, weights, n)
-            nc.scalar.activation(y[t][:, first : first + count], accs[n], RELU)
+        def finish_y(weights, piece):
+            t, first, count, bank = piece
+            first_product_pass(1, weights, piece)
+            nc.scalar.activation(y[t][:, first : first + count], banks[bank][:, :count], RELU)
 
-        nc.tensor.transpose(banks[5][:, :P], factor_rows[:], identity[:])
-        factor_cols = keep.tile([P, 4, TOKEN_BLOCKS], F32, name="factor_cols")
-        nc.scalar.copy(factor_cols[:], banks[5][:, : 4 * TOKEN_BLOCKS].rearrange("s (v r) -> s v r", v=4))
-        first_cols = keep.tile([P, TOKEN_BLOCKS], F32, name="first_cols", tag="last_w1", align_bytes=64)
-        nc.scalar.copy(first_cols[:], banks[5][:, :TOKEN_BLOCKS])
-        for tb in range(TOKEN_BLOCKS):
-            nc.tensor.transpose(
-                banks[6][:, token_cols(tb)], factor_cols[:, 3, tb : tb + 1].to_broadcast([P, P]), identity[:]
-            )
-        oth1_row = keep.tile([P, S], F32, name="oth1_row")
-        nc.scalar.copy(oth1_row[:], banks[6][:])
-
-        weights = quantised_w1(0, 0, "early0")
+        weights = quantise("w1_0_0", regrouped_w1(0, 0, "w1_grouped0_0", nc.scalar.copy), HALF)
         nc.vector.tensor_copy(x_bytes[:], scale_table[:].indirect(offs_tile[:]))
         nc.vector.tensor_copy(x_codes[0][:], word_tables[0][:].indirect(offs_tile[:]))
-        for n in range(3):
-            first_product_pass(0, weights, n)
-        weights = quantised_w1(0, 1, "early1")
-        for first in (0, half):
+        for piece in first_half:
+            first_product_pass(0, weights, piece)
+        weights = quantise("w1_0_1", regrouped_w1(0, 1, "w1_grouped0_1", nc.scalar.copy), HALF)
+        for first in (0, HALF_TOKENS):
             nc.vector.tensor_copy(
-                x_codes[1][:, first : first + half], word_tables[1][:].indirect(entries(offs_tile, first, half))
+                x_codes[1][:, first : first + HALF_TOKENS],
+                word_tables[1][:].indirect(entries(offs_tile, first, HALF_TOKENS)),
             )
-        late_grouped = regrouped_w1(1, 0, "table1", nc.vector.tensor_copy)
-        for n in range(3):
-            finish_y(weights, n)
+        second_grouped = regrouped_w1(1, 0, "table1", nc.vector.tensor_copy)
+        for piece in first_half:
+            finish_y(weights, piece)
 
-
-        def own_term(t, turned, back):
+        def own1_term(t, turned, back):
             scaled = ring.tile([P, S], F32, name="scaled", align_bytes=64)
-            own_cols = first_cols[:] if t == 0 else factor_cols[:, 0, :]
-            for tb in range(TOKEN_BLOCKS):
-                nc.tensor.transpose(turned[:, token_cols(tb)], y[t][:, token_cols(tb)], identity[:])
-            for tb in range(TOKEN_BLOCKS):
-                nc.scalar.activation(
-                    scaled[:, token_cols(tb)], turned[:, token_cols(tb)], COPY, scale=own_cols[:, tb : tb + 1]
-                )
-            for tb in range(TOKEN_BLOCKS):
-                nc.tensor.transpose(back[:, token_cols(tb)], scaled[:, token_cols(tb)], identity[:])
+            own_cols = own1_for_tile0[:] if t == 0 else factor_cols[:, OWN1, :]
+            for b in range(TOKEN_BLOCKS):
+                nc.tensor.transpose(turned[:, block(b)], y[t][:, block(b)], identity[:])
+            for b in range(TOKEN_BLOCKS):
+                nc.scalar.activation(scaled[:, block(b)], turned[:, block(b)], COPY, scale=own_cols[:, b : b + 1])
+            for b in range(TOKEN_BLOCKS):
+                nc.tensor.transpose(back[:, block(b)], scaled[:, block(b)], identity[:])
             return back
 
-        def partner_term(t):
-            term = keep.tile([P, S], F32, name=f"partner{t}")[:]
-            nc.vector.tensor_tensor(term, y[t][:].indirect(mix1_tile[:]), oth1_row[:], MULT)
+        def oth1_term(t):
+            term = keep.tile([P, S], F32, name=f"oth1_term{t}")
+            nc.vector.tensor_tensor(term[:], y[t][:].indirect(mix1_tile[:]), oth1_row[:], MULT)
             return term
 
-        picked = [None] + [keep.tile([P, S], F32, name=f"picked{t}", tag=f"picked{t}", align_bytes=64)[:] for t in range(1, PACK)]
-        h2_turned = [keep.tile([P, 2, 2 * P], BF16, name=f"h2_turned{tb}") for tb in range(TOKEN_BLOCKS)]
+        def finish_h1(t, own_term, oth_term):
+            nc.vector.tensor_tensor(h1[t][:, :S], own_term[:], oth_term[:], ADD)
 
-        def pick(t):
-            nc.vector.tensor_copy(picked[t], h1[t][:].indirect(mix2_tile[:]))
+        partners = {
+            t: keep.tile([P, S], F32, name=f"partner{t}", tag=f"partner{t}", align_bytes=64) for t in range(1, TILES)
+        }
+        h2_turned = [keep.tile([P, 2, 2 * P], BF16, name=f"h2_turned{b}") for b in range(TOKEN_BLOCKS)]
 
-        def turn_pair(bank, first, values, v, tb):
-            pair = bank[:, first : first + 2 * P].rearrange("s (u c) -> s u c", u=2)
+        def fetch_partners(t, first, count):
+            nc.vector.tensor_copy(partners[t][:, first : first + count], h1[t][:].indirect(entries(mix2_tile, first, count)))
+
+        def turn_pair(bank, side, tiles, v, b):
+            pair = bank[:, side * 2 * P : (side + 1) * 2 * P].rearrange("s (u c) -> s u c", u=2)
             for u in range(2):
-                nc.tensor.transpose(pair[:, u, :], values[2 * v + u][:, token_cols(tb)], identity[:])
+                nc.tensor.transpose(pair[:, u, :], tiles[2 * v + u][:, block(b)], identity[:])
             return pair
 
-        def own_pairs(v, bank_pair):
-            scaled = []
-            for b, bank in enumerate(bank_pair):
-                pairs = [turn_pair(bank, n * 2 * P, h1, v, 2 * b + n) for n in range(2)]
-                for n, pair in enumerate(pairs):
-                    tb = 2 * b + n
-                    term = keep.tile([P, 2, P], F32, name=f"own2_term{v}_{tb}")
-                    nc.scalar.activation(term[:], pair, COPY, scale=factor_cols[:, 1, tb : tb + 1])
-                    scaled.append(term)
-            return scaled
+        def own2_terms(v, two_banks):
+            terms = []
+            for n, bank in enumerate(two_banks):
+                pairs = [turn_pair(bank, side, h1, v, 2 * n + side) for side in range(2)]
+                for side, pair in enumerate(pairs):
+                    b = 2 * n + side
+                    term = keep.tile([P, 2, P], F32, name=f"own2_term{v}_{b}")
+                    nc.scalar.activation(term[:], pair, COPY, scale=factor_cols[:, OWN2, b : b + 1])
+                    terms.append(term)
+            return terms
 
-        def combine(v, tb, pair, own):
+        def finish_h2(v, b, turned_partners, own_term):
             nc.vector.scalar_tensor_tensor(
-                h2_turned[tb][:, :, token_cols(v)], pair, factor_cols[:, 2, tb : tb + 1], own[:], MULT, ADD
+                h2_turned[b][:, :, block(v)], turned_partners, factor_cols[:, OTH2, b : b + 1], own_term[:], MULT, ADD
             )
 
         out_view = out.rearrange("(m p) s -> p m s", p=P)
 
-        def second_product(tb, bank):
-            words = blocks(bank)[:, :2, :]
+        def second_product(b, bank, weights):
+            quarters = bank[:].rearrange("p (q c) -> p q c", c=P)
+            words, result = quarters[:, :2, :], quarters[:, 2:, :]
             for u in range(2):
-                nc.tensor.transpose(words[:, u, :], h2_turned[tb][:, u, :].bitcast(F32), identity[:])
-            h2_grouped = keep.tile([P, P * PACK], BF16, name=f"h2_grouped{tb}", align_bytes=64)
+                nc.tensor.transpose(words[:, u, :], h2_turned[b][:, u, :].bitcast(F32), identity[:])
+            h2_grouped = keep.tile([P, P * PACK], BF16, name=f"h2_grouped{b}", align_bytes=64)
             nc.scalar.copy(
                 h2_grouped[:].bitcast(F32).rearrange("p (s u) -> p s u", u=2), words.rearrange("p u s -> p s u")
             )
-            h2_codes, h2_scales = quantise(f"h2_{tb}", h2_grouped[:], P)
-            result = blocks(bank)[:, 2:, :]
+            h2_codes, h2_scales = quantise(f"h2_{b}", h2_grouped[:], P)
+            w2_codes, w2_scales = weights
             for m in range(OUT_TILES):
                 nc.tensor.matmul_mx(
                     out=result[:, m, :],
-                    lhsT=w2_codes[:, m * P : (m + 1) * P].bitcast(FP8X4),
-                    lhsT_scale=w2_scales[:, m * P : (m + 1) * P],
+                    lhsT=w2_codes[:, block(m)].bitcast(FP8X4),
+                    lhsT_scale=w2_scales[:, block(m)],
                     rhs=h2_codes[:].bitcast(FP8X4),
                     rhs_scale=h2_scales[:],
                     start=True,
                     stop=True,
                 )
             staged = ring.tile([P, OUT_TILES, P], F32, name="staged", bufs=TOKEN_BLOCKS)
-            copy_out = nc.vector.tensor_copy if tb + 1 == TOKEN_BLOCKS else nc.scalar.copy
+            copy_out = nc.vector.tensor_copy if b + 1 == TOKEN_BLOCKS else nc.scalar.copy
             copy_out(staged[:], result)
-            nc.sync.dma_start(out_view[:, :, token_cols(tb)], staged[:])
+            nc.sync.dma_start(out_view[:, :, block(b)], staged[:])
 
-        partners = [partner_term(0), partner_term(1)]
-        owns = [own_term(0, banks[5], banks[6])]
-        late_weights = quantise("w1_1_0", late_grouped, HALF, "y0")
-        weights = quantised_w1(1, 1, "last_w1")
-        picked[0] = keep.tile([P, S], F32, name="picked0", tag="last_w1", align_bytes=64)[:]
-        owns.append(own_term(1, banks[7], banks[0]))
-        for n in (3, 4):
-            first_product_pass(0, late_weights, n)
-            finish_y(weights, n)
-
+        oth_terms = [oth1_term(0), oth1_term(1)]
+        own_terms = [own1_term(0, turned=banks[5], back=banks[6])]
+        pass0_weights = quantise("w1_1_0", second_grouped, HALF, "y0")
+        pass1_weights = quantise("w1_1_1", regrouped_w1(1, 1, "last_w1", nc.scalar.copy), HALF)
+        partners[0] = keep.tile([P, S], F32, name="partner0", tag="last_w1", align_bytes=64)
+        own_terms.append(own1_term(1, turned=banks[7], back=banks[0]))
+        for piece in second_half:
+            first_product_pass(0, pass0_weights, piece)
+            finish_y(pass1_weights, piece)
         for t in range(2):
-            nc.vector.tensor_tensor(h1[t][:, :S], owns[t][:], partners[t], ADD)
-            pick(t)
+            finish_h1(t, own_terms[t], oth_terms[t])
+            fetch_partners(t, 0, S)
 
-        partners = [partner_term(2), partner_term(3)]
-        owns = [own_term(2, banks[3], banks[4]), own_term(3, banks[1], banks[2])]
-        first_owns = own_pairs(0, (banks[5], banks[7]))
-        w2_grouped = keep.tile([P, N * PACK], BF16, name="w2_grouped", tag="y2", align_bytes=64)
-        interleave(nc.scalar.copy, w2_grouped[:], w2_raw[:])
-        nc.vector.tensor_tensor(h1[2][:, :S], owns[0][:], partners[0], ADD)
-        pick(2)
-        nc.vector.tensor_tensor(h1[3][:], owns[1][:], partners[1], ADD)
-        owns = own_pairs(1, (banks[3], banks[1]))
-        first_pairs = [turn_pair(banks[(4, 2)[tb // 2]], tb % 2 * 2 * P, picked, 0, tb) for tb in range(TOKEN_BLOCKS)]
-        for tb in range(TOKEN_BLOCKS):
-            combine(0, tb, first_pairs[tb], first_owns[tb])
-        for first in (0, half):
-            nc.vector.tensor_copy(picked[3][:, first : first + half], h1[3][:].indirect(entries(mix2_tile, first, half)))
-        for tb in range(TOKEN_BLOCKS):
-            pair = turn_pair(banks[(5, 7, 6, 0)[tb]], 0, picked, 1, tb)
-            combine(1, tb, pair, owns[tb])
-        w2_codes, w2_scales = quantise("w2", w2_grouped[:], N, "picked3")
-        for tb in range(TOKEN_BLOCKS):
-            second_product(tb, banks[(4, 2, 3, 1)[tb]])
+        oth_terms = [oth1_term(2), oth1_term(3)]
+        own_terms = [own1_term(2, turned=banks[3], back=banks[4]), own1_term(3, turned=banks[1], back=banks[2])]
+        first_own2 = own2_terms(0, (banks[5], banks[7]))
+        w2_grouped = keep.tile([P, N * PACK], BF16, name="w2_grouped", tag="y3", align_bytes=64)
+        nc.scalar.copy(
+            w2_grouped[:].rearrange("p (c i j) -> p c j i", i=4, j=PACK), w2_raw[:].rearrange("p j (c i) -> p c j i", i=4)
+        )
+        finish_h1(2, own_terms[0], oth_terms[0])
+        fetch_partners(2, 0, S)
+        finish_h1(3, own_terms[1], oth_terms[1])
+        second_own2 = own2_terms(1, (banks[3], banks[1]))
+        turned = [turn_pair((banks[4], banks[2])[b // 2], b % 2, partners, 0, b) for b in range(TOKEN_BLOCKS)]
+        for b in range(TOKEN_BLOCKS):
+            finish_h2(0, b, turned[b], first_own2[b])
+        for first in (0, HALF_TOKENS):
+            fetch_partners(3, first, HALF_TOKENS)
+        for b, bank in enumerate((banks[5], banks[7], banks[6], banks[0])):
+            finish_h2(1, b, turn_pair(bank, 0, partners, 1, b), second_own2[b])
+        w2_weights = quantise("w2", w2_grouped[:], N, f"partner{TILES - 1}")
+        for b, bank in enumerate((banks[4], banks[2], banks[3], banks[1])):
+            second_product(b, bank, w2_weights)

@@ -13,8 +13,10 @@ U32 = mybir.dt.uint32
 U16 = mybir.dt.uint16
 U8 = mybir.dt.uint8
 FP8X4 = mybir.dt.float8_e4m3fn_x4
-MULT = mybir.AluOpType.mult
-ADD = mybir.AluOpType.add
+ALU = mybir.AluOpType
+MULT = ALU.mult
+ADD = ALU.add
+ABS = mybir.ActivationFunctionType.Abs
 RELU = mybir.ActivationFunctionType.Relu
 COPY = mybir.ActivationFunctionType.Copy
 
@@ -29,9 +31,10 @@ TOKEN_BLOCKS = S // P
 OUT_TILES = N // P
 QUADRANTS = 4
 LIST_ROWS = 16
-SPARE_PRODUCT = 16
-SPARE_COPY = 192
-OWN1, OWN2, OTH2, OTH1 = range(4)
+SPARE = 16
+RATIO_FLOOR = 2.0**-30
+ZERO_FLOOR = 2.0**-100
+OWN1, OWN2, OTH1, OTH2 = range(4)
 
 
 def tile_picked_ybutter_relu_p_kernel(
@@ -87,7 +90,7 @@ def tile_picked_ybutter_relu_p_kernel(
             )
         word_tables = [load_words(0)]
         w1_raw[0, 1] = load_w1(0, 1)
-        for n, factor in enumerate((own1, own2, oth2, oth1)):
+        for n, factor in enumerate((own1, own2, oth1, oth2)):
             nc.sync.dma_start(
                 factor_rows[TOKEN_BLOCKS * n : TOKEN_BLOCKS * (n + 1), :],
                 factor[:1, :].rearrange("r (b c) -> (r b) c", c=P),
@@ -100,9 +103,9 @@ def tile_picked_ybutter_relu_p_kernel(
         w2_raw = keep.tile([P, PACK, N], F32, name="w2_raw")
         nc.sync.dma_start(w2_raw[:], w2.rearrange("(p j) n -> p j n", j=PACK))
 
-        y = [keep.tile([P, S + SPARE_PRODUCT], F32, name=f"y{t}", tag=f"y{t}", align_bytes=64) for t in range(TILES)]
-        h1 = [keep.tile([P, S + SPARE_COPY * (t + 1 < TILES)], F32, name=f"h1_{t}") for t in range(TILES)]
-        for window in y + h1[: TILES - 1]:
+        y = [keep.tile([P, S + SPARE], F32, name=f"y{t}", tag=f"y{t}", align_bytes=64) for t in range(TILES)]
+        h1 = [keep.tile([P, S + SPARE * (t < 2)], F32, name=f"h1_{t}", tag=f"h1_{t}", align_bytes=64) for t in range(TILES)]
+        for window in y + h1[:2]:
             nc.vector.memset(window[:, S:], 0.0)
 
         nc.tensor.transpose(banks[5][:, :P], factor_rows[:], identity[:])
@@ -110,18 +113,24 @@ def tile_picked_ybutter_relu_p_kernel(
         nc.scalar.copy(factor_cols[:], banks[5][:, : 4 * TOKEN_BLOCKS].rearrange("s (n b) -> s n b", n=4))
         own1_for_tile0 = keep.tile([P, TOKEN_BLOCKS], F32, name="own1_for_tile0", tag="last_w1", align_bytes=64)
         nc.scalar.copy(own1_for_tile0[:], banks[5][:, OWN1 * TOKEN_BLOCKS : (OWN1 + 1) * TOKEN_BLOCKS])
+        floor = keep.tile([P, 2 * TOKEN_BLOCKS], F32, name="floor")
+        nc.scalar.activation(floor[:], banks[5][:, 2 * TOKEN_BLOCKS : 4 * TOKEN_BLOCKS], ABS, scale=RATIO_FLOOR)
+        own2_size = keep.tile([P, 2 * TOKEN_BLOCKS], F32, name="own2_size")
+        nc.scalar.activation(own2_size[:], banks[5][:, : 2 * TOKEN_BLOCKS], ABS)
         for b in range(TOKEN_BLOCKS):
             nc.tensor.transpose(banks[6][:, block(b)], factor_cols[:, OTH1, b : b + 1].to_broadcast([P, P]), identity[:])
         oth1_row = keep.tile([P, S], F32, name="oth1_row")
         nc.scalar.copy(oth1_row[:], banks[6][:])
 
-        def regrouped_w1(v, g, tag, copy):
-            grouped = keep.tile([P, 2, P, PACK], BF16, name=f"w1_grouped{v}_{g}", tag=tag, align_bytes=64)
+        def regrouped_w1(v, g, grouped, copy):
             copy(
-                grouped[:].rearrange("p u (m e) j -> p m j u e", e=2),
+                grouped.rearrange("p (u m e j) -> p m j u e", u=2, e=2, j=PACK),
                 w1_raw[v, g][:].rearrange("p j (m u e) -> p m j u e", u=2, e=2),
             )
-            return grouped[:].rearrange("p u c j -> p (u c j)")
+            return grouped
+
+        def grouped_tile(name, tag):
+            return keep.tile([P, HALF * PACK], BF16, name=name, tag=tag, align_bytes=64)[:]
 
         x_codes = [keep.tile([P, S], U32, name=f"x_codes{g}", align_bytes=64) for g in range(PASSES)]
         x_bytes = keep.tile([P, S], U8, name="x_bytes", align_bytes=64)
@@ -148,18 +157,32 @@ def tile_picked_ybutter_relu_p_kernel(
             first_product_pass(1, weights, piece)
             nc.scalar.activation(y[t][:, first : first + count], banks[bank][:, :count], RELU)
 
-        weights = quantise("w1_0_0", regrouped_w1(0, 0, "w1_grouped0_0", nc.scalar.copy), HALF)
+        weights = quantise("w1_0_0", regrouped_w1(0, 0, grouped_tile("w1_grouped0_0", "w1_grouped0_0"), nc.scalar.copy), HALF)
         nc.vector.tensor_copy(x_bytes[:], scale_table[:].indirect(offs_tile[:]))
         nc.vector.tensor_copy(x_codes[0][:], word_tables[0][:].indirect(offs_tile[:]))
         for piece in first_half:
             first_product_pass(0, weights, piece)
-        weights = quantise("w1_0_1", regrouped_w1(0, 1, "w1_grouped0_1", nc.scalar.copy), HALF)
+        weights = quantise("w1_0_1", regrouped_w1(0, 1, grouped_tile("w1_grouped0_1", "w1_grouped0_1"), nc.scalar.copy), HALF)
         for first in (0, HALF_TOKENS):
             nc.vector.tensor_copy(
                 x_codes[1][:, first : first + HALF_TOKENS],
                 word_tables[1][:].indirect(entries(offs_tile, first, HALF_TOKENS)),
             )
-        second_grouped = regrouped_w1(1, 0, "table1", nc.vector.tensor_copy)
+        after_words = keep.tile([P, S + 3 * 8], F32, name="after_words", tag="table1", align_bytes=64)
+        sign_half, safe_size, inverse = [after_words[:, S + 8 * n : S + 8 * (n + 1)] for n in range(3)]
+        own_safe = keep.tile([P, 2 * TOKEN_BLOCKS], F32, name="own_safe")
+        own1_safe, own2_safe = own_safe[:, :TOKEN_BLOCKS], own_safe[:, TOKEN_BLOCKS:]
+        flat_cols = factor_cols[:].rearrange("s n b -> s (n b)")
+        ratio_cols = keep.tile([P, 2 * TOKEN_BLOCKS], F32, name="ratio_cols")
+        nc.vector.scalar_tensor_tensor(safe_size, floor[:], ZERO_FLOOR, own2_size[:], ADD, ALU.max)
+        nc.vector.tensor_scalar(sign_half, flat_cols[:, : 2 * TOKEN_BLOCKS], 0.0, 0.5, ALU.is_ge, ALU.subtract)
+        nc.vector.scalar_tensor_tensor(own_safe[:], safe_size, 2.0, sign_half, MULT, MULT)
+        nc.vector.reciprocal(inverse, own_safe[:])
+        nc.vector.tensor_tensor(ratio_cols[:], flat_cols[:, 2 * TOKEN_BLOCKS :], inverse, MULT)
+        for b in range(TOKEN_BLOCKS):
+            nc.tensor.transpose(banks[3][:, block(b)], ratio_cols[:, TOKEN_BLOCKS + b : TOKEN_BLOCKS + b + 1].to_broadcast([P, P]), identity[:])
+        ratio_row = keep.tile([P, S], F32, name="ratio_row")
+        second_grouped = regrouped_w1(1, 0, after_words[:, :S].bitcast(BF16), nc.vector.tensor_copy)
         for piece in first_half:
             finish_y(weights, piece)
 
@@ -175,59 +198,47 @@ def tile_picked_ybutter_relu_p_kernel(
             return back
 
         def oth1_term(t):
-            term = keep.tile([P, S], F32, name=f"oth1_term{t}")
+            term = keep.tile([P, S], F32, name=f"oth1_term{t}", tag=f"oth1_term{t}")
             nc.vector.tensor_tensor(term[:], y[t][:].indirect(mix1_tile[:]), oth1_row[:], MULT)
             return term
 
         def finish_h1(t, own_term, oth_term):
             nc.vector.tensor_tensor(h1[t][:, :S], own_term[:], oth_term[:], ADD)
 
-        partners = {
-            t: keep.tile([P, S], F32, name=f"partner{t}", tag=f"partner{t}", align_bytes=64) for t in range(1, TILES)
-        }
-        h2_turned = [keep.tile([P, 2, 2 * P], BF16, name=f"h2_turned{b}") for b in range(TOKEN_BLOCKS)]
+        partners = {}
+        h2_turned = [keep.tile([P, 2, 2 * P], BF16, name=f"h2_turned{b}", tag=f"h2_turned{b}", align_bytes=64) for b in range(TOKEN_BLOCKS)]
 
-        def fetch_partners(t, first, count):
-            nc.vector.tensor_copy(partners[t][:, first : first + count], h1[t][:].indirect(entries(mix2_tile, first, count)))
+        def fetch_partners(partner, t, tokens):
+            offsets = entries(mix2_tile, tokens.start, tokens.stop - tokens.start)
+            nc.vector.tensor_tensor(partner, h1[t][:].indirect(offsets), ratio_row[:, tokens], MULT)
 
-        def turn_pair(bank, side, tiles, v, b):
-            pair = bank[:, side * 2 * P : (side + 1) * 2 * P].rearrange("s (u c) -> s u c", u=2)
-            for u in range(2):
-                nc.tensor.transpose(pair[:, u, :], tiles[2 * v + u][:, block(b)], identity[:])
-            return pair
+        def turn_into(place, source, start, stop):
+            nc.tensor.matmul(place, source, identity[:], start=start, stop=stop, is_transpose=True)
 
-        def own2_terms(v, two_banks):
-            terms = []
-            for n, bank in enumerate(two_banks):
-                pairs = [turn_pair(bank, side, h1, v, 2 * n + side) for side in range(2)]
-                for side, pair in enumerate(pairs):
-                    b = 2 * n + side
-                    term = keep.tile([P, 2, P], F32, name=f"own2_term{v}_{b}")
-                    nc.scalar.activation(term[:], pair, COPY, scale=factor_cols[:, OWN2, b : b + 1])
-                    terms.append(term)
-            return terms
-
-        def finish_h2(v, b, turned_partners, own_term):
-            nc.vector.scalar_tensor_tensor(
-                h2_turned[b][:, :, block(v)], turned_partners, factor_cols[:, OTH2, b : b + 1], own_term[:], MULT, ADD
+        def finish_h2(v, b, sums):
+            nc.scalar.activation(
+                h2_turned[b][:, :, block(v)], sums.rearrange("s (u c) -> s u c", u=2), COPY, scale=own2_safe[:, b : b + 1]
             )
 
         out_view = out.rearrange("(m p) s -> p m s", p=P)
 
-        def second_product(b, bank, weights):
-            quarters = bank[:].rearrange("p (q c) -> p q c", c=P)
-            words, result = quarters[:, :2, :], quarters[:, 2:, :]
+        h2_grouped = {}
+
+        def turn_back(b, bank, copy):
+            words = bank[:, :HALF_TOKENS].rearrange("p (u s) -> p u s", u=2)
             for u in range(2):
                 nc.tensor.transpose(words[:, u, :], h2_turned[b][:, u, :].bitcast(F32), identity[:])
-            h2_grouped = keep.tile([P, P * PACK], BF16, name=f"h2_grouped{b}", align_bytes=64)
-            nc.scalar.copy(
-                h2_grouped[:].bitcast(F32).rearrange("p (s u) -> p s u", u=2), words.rearrange("p u s -> p s u")
+            h2_grouped[b] = keep.tile([P, K_PASS], BF16, name=f"h2_grouped{b}", tag=f"h2_grouped{b}", align_bytes=64)
+            copy(
+                h2_grouped[b][:].bitcast(F32).rearrange("p (s u) -> p s u", u=2), words.rearrange("p u s -> p s u")
             )
-            h2_codes, h2_scales = quantise(f"h2_{b}", h2_grouped[:], P)
+
+        def second_product(b, places, weights):
+            h2_codes, h2_scales = quantise(f"h2_{b}", h2_grouped[b][:], P)
             w2_codes, w2_scales = weights
             for m in range(OUT_TILES):
                 nc.tensor.matmul_mx(
-                    out=result[:, m, :],
+                    out=places[m],
                     lhsT=w2_codes[:, block(m)].bitcast(FP8X4),
                     lhsT_scale=w2_scales[:, block(m)],
                     rhs=h2_codes[:].bitcast(FP8X4),
@@ -235,42 +246,81 @@ def tile_picked_ybutter_relu_p_kernel(
                     start=True,
                     stop=True,
                 )
-            staged = ring.tile([P, OUT_TILES, P], F32, name="staged", bufs=TOKEN_BLOCKS)
-            copy_out = nc.vector.tensor_copy if b + 1 == TOKEN_BLOCKS else nc.scalar.copy
-            copy_out(staged[:], result)
-            nc.sync.dma_start(out_view[:, :, block(b)], staged[:])
+
+        def staged_tile(b):
+            tag = f"h2_turned{b + 2}" if b < 2 else f"h2_grouped{b + 1}"
+            return keep.tile([P, OUT_TILES, P], F32, name=f"staged{b}", tag=tag, align_bytes=64)
 
         oth_terms = [oth1_term(0), oth1_term(1)]
         own_terms = [own1_term(0, turned=banks[5], back=banks[6])]
         pass0_weights = quantise("w1_1_0", second_grouped, HALF, "y0")
-        pass1_weights = quantise("w1_1_1", regrouped_w1(1, 1, "last_w1", nc.scalar.copy), HALF)
+        pass1_weights = quantise("w1_1_1", regrouped_w1(1, 1, grouped_tile("w1_grouped1_1", "last_w1"), nc.scalar.copy), HALF)
         partners[0] = keep.tile([P, S], F32, name="partner0", tag="last_w1", align_bytes=64)
         own_terms.append(own1_term(1, turned=banks[7], back=banks[0]))
+        nc.scalar.copy(ratio_row[:], banks[3][:])
+        for b in range(TOKEN_BLOCKS):
+            nc.tensor.transpose(banks[4][:, block(b)], ratio_cols[:, b : b + 1].to_broadcast([P, P]), identity[:])
+        ratio1_row = keep.tile([P, S], F32, name="ratio1_row", tag="ratio1_row")
+        nc.scalar.copy(ratio1_row[:], banks[4][:])
         for piece in second_half:
             first_product_pass(0, pass0_weights, piece)
             finish_y(pass1_weights, piece)
-        for t in range(2):
-            finish_h1(t, own_terms[t], oth_terms[t])
-            fetch_partners(t, 0, S)
+        finish_h1(0, own_terms[0], oth_terms[0])
+        fetch_partners(partners[0][:], 0, slice(0, S))
+        finish_h1(1, own_terms[1], oth_terms[1])
 
-        oth_terms = [oth1_term(2), oth1_term(3)]
-        own_terms = [own1_term(2, turned=banks[3], back=banks[4]), own1_term(3, turned=banks[1], back=banks[2])]
-        first_own2 = own2_terms(0, (banks[5], banks[7]))
-        w2_grouped = keep.tile([P, N * PACK], BF16, name="w2_grouped", tag="y3", align_bytes=64)
+        ratio_term = keep.tile([P, S], F32, name="ratio_term")
+        nc.vector.tensor_tensor(ratio_term[:], y[2][:].indirect(mix1_tile[:]), ratio1_row[:], MULT)
+        oth_term3 = oth1_term(3)
+        partners[1] = keep.tile([P, S], F32, name="partner1", tag="ratio1_row")
+        fetch_partners(partners[1][:], 1, slice(0, S))
+        for b in range(TOKEN_BLOCKS):
+            turn_into(banks[3][:, block(b)], y[2][:, block(b)], b == 0, False)
+        own_term3 = own1_term(3, turned=banks[1], back=banks[2])
+        for b in range(TOKEN_BLOCKS):
+            turn_into(banks[3][:, block(b)], ratio_term[:, block(b)], False, b + 1 == TOKEN_BLOCKS)
+        h1_turned = keep.tile([P, S], F32, name="h1_turned", tag="h1_turned", align_bytes=64)
+        for b in range(TOKEN_BLOCKS):
+            nc.scalar.activation(h1_turned[:, block(b)], banks[3][:, block(b)], COPY, scale=own1_safe[:, b : b + 1])
+        for b in range(TOKEN_BLOCKS):
+            nc.tensor.transpose(banks[4][:, block(b)], h1_turned[:, block(b)], identity[:])
+        nc.scalar.copy(h1[2][:], banks[4][:])
+        first_sums = [(banks[5], banks[7])[b // 2][:, (b % 2) * HALF : (b % 2 + 1) * HALF] for b in range(TOKEN_BLOCKS)]
+        for n, sources in enumerate((h1, partners)):
+            for b in range(TOKEN_BLOCKS):
+                for u in range(2):
+                    first, last = n == 0 and b % 2 == 0 and u == 0, n == 1 and b % 2 == 1 and u == 1
+                    turn_into(first_sums[b][:, block(u)], sources[u][:, block(b)], first, last)
+        w2_grouped = keep.tile([P, N * PACK], BF16, name="w2_grouped", tag="w1_1_1", align_bytes=64)
         nc.scalar.copy(
             w2_grouped[:].rearrange("p (c i j) -> p c j i", i=4, j=PACK), w2_raw[:].rearrange("p j (c i) -> p c j i", i=4)
         )
-        finish_h1(2, own_terms[0], oth_terms[0])
-        fetch_partners(2, 0, S)
-        finish_h1(3, own_terms[1], oth_terms[1])
-        second_own2 = own2_terms(1, (banks[3], banks[1]))
-        turned = [turn_pair((banks[4], banks[2])[b // 2], b % 2, partners, 0, b) for b in range(TOKEN_BLOCKS)]
         for b in range(TOKEN_BLOCKS):
-            finish_h2(0, b, turned[b], first_own2[b])
-        for first in (0, HALF_TOKENS):
-            fetch_partners(3, first, HALF_TOKENS)
-        for b, bank in enumerate((banks[5], banks[7], banks[6], banks[0])):
-            finish_h2(1, b, turn_pair(bank, 0, partners, 1, b), second_own2[b])
-        w2_weights = quantise("w2", w2_grouped[:], N, f"partner{TILES - 1}")
-        for b, bank in enumerate((banks[4], banks[2], banks[3], banks[1])):
-            second_product(b, bank, w2_weights)
+            finish_h2(0, b, first_sums[b])
+        finish_h1(3, own_term3, oth_term3)
+        second_sums = [banks[n][:, :HALF] for n in (6, 0, 3, 1)]
+        for u in range(2):
+            for b in range(TOKEN_BLOCKS):
+                turn_into(second_sums[b][:, block(u)], h1[2 + u][:, block(b)], u == 0, False)
+        late_partners = keep.tile([P, TOKEN_BLOCKS, 2, P], F32, name="late_partners", tag="oth1_term3")
+        product_banks = [banks[n] for n in (4, 2, 5, 7)]
+        for b in range(TOKEN_BLOCKS):
+            for u in (1, 0):
+                fetch_partners(late_partners[:, b, u, :], 2 + u, block(b))
+                turn_into(second_sums[b][:, block(u)], late_partners[:, b, u, :], False, u == 0)
+            finish_h2(1, b, second_sums[b])
+            turn_back(b, product_banks[b], nc.vector.tensor_copy if b < 2 else nc.scalar.copy)
+        w2_weights = quantise("w2", w2_grouped[:], N, "h1_3")
+        last = TOKEN_BLOCKS - 1
+        for b in range(last):
+            second_product(b, [product_banks[b][:, block(2 + m)] for m in range(OUT_TILES)], w2_weights)
+        last_places = [banks[6][:, :P], product_banks[last][:, block(2)]]
+        second_product(last, last_places, w2_weights)
+        for b, copy in enumerate((nc.scalar.copy, nc.scalar.copy, nc.vector.tensor_copy)):
+            staged = staged_tile(b)
+            copy(staged[:], product_banks[b][:, HALF_TOKENS:].rearrange("p (m s) -> p m s", m=OUT_TILES))
+            nc.sync.dma_start(out_view[:, :, block(b)], staged[:])
+        staged = staged_tile(last)
+        for m, copy in enumerate((nc.scalar.copy, nc.vector.tensor_copy)):
+            copy(staged[:, m, :], last_places[m])
+        nc.sync.dma_start(out_view[:, :, block(last)], staged[:])

@@ -34,7 +34,7 @@ LIST_ROWS = 16
 SPARE = 16
 RATIO_FLOOR = 2.0**-30
 ZERO_FLOOR = 2.0**-100
-OWN1, OWN2, OTH1, OTH2 = range(4)
+OWN1, OWN2, OTH1 = range(3)
 
 
 def tile_picked_ybutter_relu_p_kernel(
@@ -64,15 +64,16 @@ def tile_picked_ybutter_relu_p_kernel(
         mix2_tile = keep.tile([P, S // LIST_ROWS], U16, name="mix2_tile")
         nc.sync.dma_start(offs_tile[:], offs)
 
+        factor_tile = keep.tile([P, S], F32, name="factor_tile", tag="factor_tile", align_bytes=64)
+        factor_rows = factor_tile[:, :P]
+        nc.gpsimd.memset(factor_rows, 0.0)
         scale_table = keep.tile([P, T], U8, name="scale_table")
         nc.gpsimd.memset(scale_table[:].bitcast(I32), 0)
         identity = keep.tile([P, P], F32, name="identity")
         make_identity(nc, identity[:])
-        factor_rows = keep.tile([P, P], F32, name="factor_rows")
-        nc.vector.memset(factor_rows[:], 0.0)
 
         def load_w1(v, g):
-            raw = keep.tile([P, PACK, HALF], F32, name=f"w1_raw{v}_{g}")
+            raw = keep.tile([P, PACK, HALF], F32, name=f"w1_raw{v}_{g}", tag=f"w1_raw{v}_{g}", align_bytes=64)
             rows = w1[g * K_PASS : (g + 1) * K_PASS, v * HALF : (v + 1) * HALF]
             nc.sync.dma_start(raw[:], rows.rearrange("(p j) c -> p j c", j=PACK))
             return raw
@@ -83,17 +84,17 @@ def tile_picked_ybutter_relu_p_kernel(
             return table
 
         w1_raw = {(0, 0): load_w1(0, 0)}
-        for q in range(QUADRANTS):
-            nc.sync.dma_start(
-                scale_table[32 * q : 32 * q + 4 * PASSES, :].bitcast(I32),
-                x_scales[:, 4 * q : 4 * q + 4, :].bitcast(I32),
-            )
-        word_tables = [load_words(0)]
-        w1_raw[0, 1] = load_w1(0, 1)
         for n, factor in enumerate((own1, own2, oth1, oth2)):
             nc.sync.dma_start(
                 factor_rows[TOKEN_BLOCKS * n : TOKEN_BLOCKS * (n + 1), :],
                 factor[:1, :].rearrange("r (b c) -> (r b) c", c=P),
+            )
+        word_tables = [load_words(0)]
+        w1_raw[0, 1] = load_w1(0, 1)
+        for q in range(QUADRANTS):
+            nc.sync.dma_start(
+                scale_table[32 * q : 32 * q + 4 * PASSES, :].bitcast(I32),
+                x_scales[:, 4 * q : 4 * q + 4, :].bitcast(I32),
             )
         word_tables.append(load_words(1))
         w1_raw[1, 0] = load_w1(1, 0)
@@ -108,19 +109,37 @@ def tile_picked_ybutter_relu_p_kernel(
         for window in y + h1[:2]:
             nc.vector.memset(window[:, S:], 0.0)
 
-        nc.tensor.transpose(banks[5][:, :P], factor_rows[:], identity[:])
+        nc.tensor.transpose(banks[5][:, :P], factor_rows, identity[:])
         factor_cols = keep.tile([P, 4, TOKEN_BLOCKS], F32, name="factor_cols")
-        nc.scalar.copy(factor_cols[:], banks[5][:, : 4 * TOKEN_BLOCKS].rearrange("s (n b) -> s n b", n=4))
-        own1_for_tile0 = keep.tile([P, TOKEN_BLOCKS], F32, name="own1_for_tile0", tag="last_w1", align_bytes=64)
-        nc.scalar.copy(own1_for_tile0[:], banks[5][:, OWN1 * TOKEN_BLOCKS : (OWN1 + 1) * TOKEN_BLOCKS])
+        turned_factors = banks[5][:, : 4 * TOKEN_BLOCKS].rearrange("s (n b) -> s n b", n=4)
+        nc.scalar.copy(factor_cols[:], turned_factors)
         floor = keep.tile([P, 2 * TOKEN_BLOCKS], F32, name="floor")
-        nc.scalar.activation(floor[:], banks[5][:, 2 * TOKEN_BLOCKS : 4 * TOKEN_BLOCKS], ABS, scale=RATIO_FLOOR)
+        nc.scalar.activation(floor[:].rearrange("s (n b) -> s n b", n=2), turned_factors[:, OTH1:, :], ABS, scale=RATIO_FLOOR)
         own2_size = keep.tile([P, 2 * TOKEN_BLOCKS], F32, name="own2_size")
-        nc.scalar.activation(own2_size[:], banks[5][:, : 2 * TOKEN_BLOCKS], ABS)
+        nc.scalar.activation(own2_size[:].rearrange("s (n b) -> s n b", n=2), turned_factors[:, :OTH1, :], ABS)
+        own1_for_tile0 = keep.tile([P, TOKEN_BLOCKS], F32, name="own1_for_tile0", tag="last_w1", align_bytes=64)
+        nc.scalar.copy(own1_for_tile0[:], turned_factors[:, OWN1, :])
         for b in range(TOKEN_BLOCKS):
             nc.tensor.transpose(banks[6][:, block(b)], factor_cols[:, OTH1, b : b + 1].to_broadcast([P, P]), identity[:])
         oth1_row = keep.tile([P, S], F32, name="oth1_row")
         nc.scalar.copy(oth1_row[:], banks[6][:])
+
+        small = keep.tile([P, 4, 8], F32, name="small", tag="small", align_bytes=64)
+        sign_half, safe_size, inverse, signed_half = [small[:, n, :] for n in range(4)]
+        own_safe = keep.tile([P, 2 * TOKEN_BLOCKS], F32, name="own_safe")
+        own1_safe, own2_safe = own_safe[:, :TOKEN_BLOCKS], own_safe[:, TOKEN_BLOCKS:]
+        flat_cols = factor_cols[:].rearrange("s n b -> s (n b)")
+        ratio_cols = keep.tile([P, 2 * TOKEN_BLOCKS], F32, name="ratio_cols")
+        nc.vector.scalar_tensor_tensor(safe_size, floor[:], ZERO_FLOOR, own2_size[:], ADD, ALU.max)
+        nc.vector.tensor_scalar(sign_half, flat_cols[:, : 2 * TOKEN_BLOCKS], 0.0, 0.5, ALU.is_ge, ALU.subtract)
+        nc.vector.reciprocal(inverse, safe_size)
+        nc.vector.tensor_tensor(signed_half, flat_cols[:, 2 * TOKEN_BLOCKS :], sign_half, MULT)
+        nc.vector.scalar_tensor_tensor(own_safe[:], safe_size, 2.0, sign_half, MULT, MULT)
+        nc.vector.scalar_tensor_tensor(ratio_cols[:], signed_half, 2.0, inverse, MULT, MULT)
+        for b in range(TOKEN_BLOCKS):
+            nc.tensor.transpose(banks[3][:, block(b)], ratio_cols[:, TOKEN_BLOCKS + b : TOKEN_BLOCKS + b + 1].to_broadcast([P, P]), identity[:])
+        for b in range(TOKEN_BLOCKS):
+            nc.tensor.transpose(banks[4][:, block(b)], ratio_cols[:, b : b + 1].to_broadcast([P, P]), identity[:])
 
         def regrouped_w1(v, g, grouped, copy):
             copy(
@@ -132,8 +151,8 @@ def tile_picked_ybutter_relu_p_kernel(
         def grouped_tile(name, tag):
             return keep.tile([P, HALF * PACK], BF16, name=name, tag=tag, align_bytes=64)[:]
 
-        x_codes = [keep.tile([P, S], U32, name=f"x_codes{g}", align_bytes=64) for g in range(PASSES)]
-        x_bytes = keep.tile([P, S], U8, name="x_bytes", align_bytes=64)
+        x_codes = [keep.tile([P, S], U32, name=f"x_codes{g}", tag=tag, align_bytes=64) for g, tag in enumerate(("small", "x_codes1"))]
+        x_bytes = keep.tile([P, S], U8, name="x_bytes", tag="factor_tile", align_bytes=64)
 
         first_half = [(0, 0, HALF_TOKENS, 0), (0, HALF_TOKENS, HALF_TOKENS, 1), (1, 0, S, 2)]
         second_half = [(2, 0, S, 5), (3, 0, S, 7)]
@@ -157,32 +176,22 @@ def tile_picked_ybutter_relu_p_kernel(
             first_product_pass(1, weights, piece)
             nc.scalar.activation(y[t][:, first : first + count], banks[bank][:, :count], RELU)
 
-        weights = quantise("w1_0_0", regrouped_w1(0, 0, grouped_tile("w1_grouped0_0", "w1_grouped0_0"), nc.scalar.copy), HALF)
-        nc.vector.tensor_copy(x_bytes[:], scale_table[:].indirect(offs_tile[:]))
         nc.vector.tensor_copy(x_codes[0][:], word_tables[0][:].indirect(offs_tile[:]))
+        weights = quantise("w1_0_0", regrouped_w1(0, 0, factor_tile[:].bitcast(BF16), nc.scalar.copy), HALF, "table0")
+        nc.vector.tensor_copy(x_bytes[:], scale_table[:].indirect(offs_tile[:]))
         for piece in first_half:
             first_product_pass(0, weights, piece)
         weights = quantise("w1_0_1", regrouped_w1(0, 1, grouped_tile("w1_grouped0_1", "w1_grouped0_1"), nc.scalar.copy), HALF)
+        ratio_row = keep.tile([P, S], F32, name="ratio_row", tag="w1_grouped0_1", align_bytes=64)
+        nc.scalar.copy(ratio_row[:], banks[3][:])
+        ratio1_row = keep.tile([P, S], F32, name="ratio1_row", tag="w1_raw0_1", align_bytes=64)
+        nc.scalar.copy(ratio1_row[:], banks[4][:])
         for first in (0, HALF_TOKENS):
             nc.vector.tensor_copy(
                 x_codes[1][:, first : first + HALF_TOKENS],
                 word_tables[1][:].indirect(entries(offs_tile, first, HALF_TOKENS)),
             )
-        after_words = keep.tile([P, S + 3 * 8], F32, name="after_words", tag="table1", align_bytes=64)
-        sign_half, safe_size, inverse = [after_words[:, S + 8 * n : S + 8 * (n + 1)] for n in range(3)]
-        own_safe = keep.tile([P, 2 * TOKEN_BLOCKS], F32, name="own_safe")
-        own1_safe, own2_safe = own_safe[:, :TOKEN_BLOCKS], own_safe[:, TOKEN_BLOCKS:]
-        flat_cols = factor_cols[:].rearrange("s n b -> s (n b)")
-        ratio_cols = keep.tile([P, 2 * TOKEN_BLOCKS], F32, name="ratio_cols")
-        nc.vector.scalar_tensor_tensor(safe_size, floor[:], ZERO_FLOOR, own2_size[:], ADD, ALU.max)
-        nc.vector.tensor_scalar(sign_half, flat_cols[:, : 2 * TOKEN_BLOCKS], 0.0, 0.5, ALU.is_ge, ALU.subtract)
-        nc.vector.scalar_tensor_tensor(own_safe[:], safe_size, 2.0, sign_half, MULT, MULT)
-        nc.vector.reciprocal(inverse, own_safe[:])
-        nc.vector.tensor_tensor(ratio_cols[:], flat_cols[:, 2 * TOKEN_BLOCKS :], inverse, MULT)
-        for b in range(TOKEN_BLOCKS):
-            nc.tensor.transpose(banks[3][:, block(b)], ratio_cols[:, TOKEN_BLOCKS + b : TOKEN_BLOCKS + b + 1].to_broadcast([P, P]), identity[:])
-        ratio_row = keep.tile([P, S], F32, name="ratio_row")
-        second_grouped = regrouped_w1(1, 0, after_words[:, :S].bitcast(BF16), nc.vector.tensor_copy)
+        second_grouped = regrouped_w1(1, 0, grouped_tile("w1_grouped1_0", "table1"), nc.vector.tensor_copy)
         for piece in first_half:
             finish_y(weights, piece)
 
@@ -257,11 +266,6 @@ def tile_picked_ybutter_relu_p_kernel(
         pass1_weights = quantise("w1_1_1", regrouped_w1(1, 1, grouped_tile("w1_grouped1_1", "last_w1"), nc.scalar.copy), HALF)
         partners[0] = keep.tile([P, S], F32, name="partner0", tag="last_w1", align_bytes=64)
         own_terms.append(own1_term(1, turned=banks[7], back=banks[0]))
-        nc.scalar.copy(ratio_row[:], banks[3][:])
-        for b in range(TOKEN_BLOCKS):
-            nc.tensor.transpose(banks[4][:, block(b)], ratio_cols[:, b : b + 1].to_broadcast([P, P]), identity[:])
-        ratio1_row = keep.tile([P, S], F32, name="ratio1_row", tag="ratio1_row")
-        nc.scalar.copy(ratio1_row[:], banks[4][:])
         for piece in second_half:
             first_product_pass(0, pass0_weights, piece)
             finish_y(pass1_weights, piece)
@@ -272,7 +276,7 @@ def tile_picked_ybutter_relu_p_kernel(
         ratio_term = keep.tile([P, S], F32, name="ratio_term")
         nc.vector.tensor_tensor(ratio_term[:], y[2][:].indirect(mix1_tile[:]), ratio1_row[:], MULT)
         oth_term3 = oth1_term(3)
-        partners[1] = keep.tile([P, S], F32, name="partner1", tag="ratio1_row")
+        partners[1] = keep.tile([P, S], F32, name="partner1", tag="w1_raw0_1", align_bytes=64)
         fetch_partners(partners[1][:], 1, slice(0, S))
         for b in range(TOKEN_BLOCKS):
             turn_into(banks[3][:, block(b)], y[2][:, block(b)], b == 0, False)

@@ -25,16 +25,16 @@ PACK = 4
 K_PASS = P * PACK
 PASSES = K // K_PASS
 TILES = H // P
-HALF = H // 2
 HALF_TOKENS = S // 2
-TOKEN_BLOCKS = S // P
 OUT_TILES = N // P
 QUADRANTS = 4
 LIST_ROWS = 16
+
+HALF = H // 2
+BLOCKS = S // P
 SPARE = 16
 RATIO_FLOOR = 2.0**-30
 ZERO_FLOOR = 2.0**-100
-OWN1, OWN2, OTH1 = range(3)
 
 
 def tile_picked_ybutter_relu_p_kernel(
@@ -43,15 +43,14 @@ def tile_picked_ybutter_relu_p_kernel(
     nc = tc.nc
     with ExitStack() as ctx:
         keep = ctx.enter_context(tc.tile_pool(name="keep", bufs=1))
-        ring = ctx.enter_context(tc.tile_pool(name="ring", bufs=2))
         psum = ctx.enter_context(tc.psum_pool(name="psum", bufs=1))
         banks = [psum.tile([P, S], F32, name=f"bank{b}") for b in range(8)]
 
         def block(b):
             return slice(b * P, (b + 1) * P)
 
-        def entries(list_tile, first, count):
-            return list_tile[:, first // LIST_ROWS : (first + count) // LIST_ROWS]
+        def entries(list_tile, tokens):
+            return list_tile[:, tokens.start // LIST_ROWS : tokens.stop // LIST_ROWS]
 
         def quantise(name, grouped, width, tag=""):
             codes = keep.tile([P, width], U32, name=name + "_codes", tag=tag or name, align_bytes=64)
@@ -59,87 +58,94 @@ def tile_picked_ybutter_relu_p_kernel(
             nc.vector.quantize_mx(out=codes[:].bitcast(FP8X4), scales=scales[:], in_=grouped)
             return codes, scales
 
-        offs_tile = keep.tile([P, S // LIST_ROWS], U16, name="offs_tile")
-        mix1_tile = keep.tile([P, S // LIST_ROWS], U16, name="mix1_tile")
-        mix2_tile = keep.tile([P, S // LIST_ROWS], U16, name="mix2_tile")
-        nc.sync.dma_start(offs_tile[:], offs)
-
-        factor_tile = keep.tile([P, S], F32, name="factor_tile", tag="factor_tile", align_bytes=64)
-        factor_rows = factor_tile[:, :P]
-        nc.gpsimd.memset(factor_rows, 0.0)
-        scale_table = keep.tile([P, T], U8, name="scale_table")
-        nc.gpsimd.memset(scale_table[:].bitcast(I32), 0)
-        identity = keep.tile([P, P], F32, name="identity")
-        make_identity(nc, identity[:])
-
-        def load_w1(v, g):
-            raw = keep.tile([P, PACK, HALF], F32, name=f"w1_raw{v}_{g}", tag=f"w1_raw{v}_{g}", align_bytes=64)
-            rows = w1[g * K_PASS : (g + 1) * K_PASS, v * HALF : (v + 1) * HALF]
-            nc.sync.dma_start(raw[:], rows.rearrange("(p j) c -> p j c", j=PACK))
-            return raw
+        def load(name, source, shape, dtype):
+            tile = keep.tile(shape, dtype, name=name, tag=name, align_bytes=64)
+            nc.sync.dma_start(tile[:], source)
+            return tile
 
         def load_words(g):
-            table = keep.tile([P, T], U32, name=f"word_table{g}", tag=f"table{g}", align_bytes=64)
+            table = keep.tile([P, T], U32, name=f"word_table{g}", tag=f"word_table{g}", align_bytes=64)
             nc.sync.dma_start(table[:].bitcast(I32), x_words[g].rearrange("p n t -> p (n t)").bitcast(I32))
             return table
 
-        w1_raw = {(0, 0): load_w1(0, 0)}
-        for n, factor in enumerate((own1, own2, oth1, oth2)):
+        def load_rows(name, rows):
+            return load(name, rows.rearrange("(p j) c -> p j c", j=PACK), [P, PACK, rows.shape[1]], F32)
+
+        def tile(name, shape, dtype, tag=""):
+            return keep.tile(shape, dtype, name=name, tag=tag or name, align_bytes=64)
+
+        factor_rows = tile("factor_rows", [P, P], F32)
+        nc.gpsimd.memset(factor_rows[:], 0.0)
+        scale_table = tile("scale_table", [P, T], U8)
+        nc.gpsimd.memset(scale_table[:].bitcast(I32), 0)
+        identity = tile("identity", [P, P], F32)
+        make_identity(nc, identity[:])
+
+        def load_w1(v, g):
+            return load_rows(f"w1_raw{v}_{g}", w1[g * K_PASS : (g + 1) * K_PASS, v * HALF : (v + 1) * HALF])
+
+        def load_scales():
+            for q in range(QUADRANTS):
+                nc.sync.dma_start(
+                    scale_table[32 * q : 32 * q + 4 * PASSES, :].bitcast(I32),
+                    x_scales[:, 4 * q : 4 * q + 4, :].bitcast(I32),
+                )
+
+        def load_factor(n, factor):
             nc.sync.dma_start(
-                factor_rows[TOKEN_BLOCKS * n : TOKEN_BLOCKS * (n + 1), :],
-                factor[:1, :].rearrange("r (b c) -> (r b) c", c=P),
+                factor_rows[BLOCKS * n : BLOCKS * (n + 1), :], factor[:1, :].rearrange("r (b c) -> (r b) c", c=P)
             )
+
+        offs_tile = load("offs_tile", offs, [P, S // LIST_ROWS], U16)
+        w1_raw = {(0, 0): load_w1(0, 0)}
+        for n, factor in enumerate((own1, oth1, own2, oth2)):
+            load_factor(n, factor)
         word_tables = [load_words(0)]
         w1_raw[0, 1] = load_w1(0, 1)
-        for q in range(QUADRANTS):
-            nc.sync.dma_start(
-                scale_table[32 * q : 32 * q + 4 * PASSES, :].bitcast(I32),
-                x_scales[:, 4 * q : 4 * q + 4, :].bitcast(I32),
-            )
+        load_scales()
         word_tables.append(load_words(1))
         w1_raw[1, 0] = load_w1(1, 0)
-        nc.sync.dma_start(mix1_tile[:], mix1)
+        mix1_tile = load("mix1_tile", mix1, [P, S // LIST_ROWS], U16)
         w1_raw[1, 1] = load_w1(1, 1)
-        nc.sync.dma_start(mix2_tile[:], mix2)
-        w2_raw = keep.tile([P, PACK, N], F32, name="w2_raw")
-        nc.sync.dma_start(w2_raw[:], w2.rearrange("(p j) n -> p j n", j=PACK))
+        mix2_tile = load("mix2_tile", mix2, [P, S // LIST_ROWS], U16)
+        w2_raw = load_rows("w2_raw", w2)
 
-        y = [keep.tile([P, S + SPARE], F32, name=f"y{t}", tag=f"y{t}", align_bytes=64) for t in range(TILES)]
-        h1 = [keep.tile([P, S + SPARE * (t < 2)], F32, name=f"h1_{t}", tag=f"h1_{t}", align_bytes=64) for t in range(TILES)]
-        for window in y + h1[:2]:
-            nc.vector.memset(window[:, S:], 0.0)
+        y = [tile(f"y{t}", [P, S + SPARE * (t != 1)], F32, "w1_raw1_1" if t == 1 else "") for t in range(TILES)]
+        h1 = [tile(f"h1_{t}", [P, S + SPARE * (t < 2)], F32) for t in range(TILES)]
+        for window in [y[0]] + y[2:] + h1[:2]:
+            nc.gpsimd.memset(window[:, S:], 0.0)
 
-        nc.tensor.transpose(banks[5][:, :P], factor_rows, identity[:])
-        factor_cols = keep.tile([P, 4, TOKEN_BLOCKS], F32, name="factor_cols")
-        turned_factors = banks[5][:, : 4 * TOKEN_BLOCKS].rearrange("s (n b) -> s n b", n=4)
-        nc.scalar.copy(factor_cols[:], turned_factors)
-        floor = keep.tile([P, 2 * TOKEN_BLOCKS], F32, name="floor")
-        nc.scalar.activation(floor[:].rearrange("s (n b) -> s n b", n=2), turned_factors[:, OTH1:, :], ABS, scale=RATIO_FLOOR)
-        own2_size = keep.tile([P, 2 * TOKEN_BLOCKS], F32, name="own2_size")
-        nc.scalar.activation(own2_size[:].rearrange("s (n b) -> s n b", n=2), turned_factors[:, :OTH1, :], ABS)
-        own1_for_tile0 = keep.tile([P, TOKEN_BLOCKS], F32, name="own1_for_tile0", tag="last_w1", align_bytes=64)
-        nc.scalar.copy(own1_for_tile0[:], turned_factors[:, OWN1, :])
-        for b in range(TOKEN_BLOCKS):
-            nc.tensor.transpose(banks[6][:, block(b)], factor_cols[:, OTH1, b : b + 1].to_broadcast([P, P]), identity[:])
-        oth1_row = keep.tile([P, S], F32, name="oth1_row")
-        nc.scalar.copy(oth1_row[:], banks[6][:])
+        def spread(bank, columns):
+            for b in range(BLOCKS):
+                nc.tensor.transpose(bank[:, block(b)], columns[:, b : b + 1].to_broadcast([P, P]), identity[:])
 
-        small = keep.tile([P, 4, 8], F32, name="small", tag="small", align_bytes=64)
-        sign_half, safe_size, inverse, signed_half = [small[:, n, :] for n in range(4)]
-        own_safe = keep.tile([P, 2 * TOKEN_BLOCKS], F32, name="own_safe")
-        own1_safe, own2_safe = own_safe[:, :TOKEN_BLOCKS], own_safe[:, TOKEN_BLOCKS:]
-        flat_cols = factor_cols[:].rearrange("s n b -> s (n b)")
-        ratio_cols = keep.tile([P, 2 * TOKEN_BLOCKS], F32, name="ratio_cols")
-        nc.vector.scalar_tensor_tensor(safe_size, floor[:], ZERO_FLOOR, own2_size[:], ADD, ALU.max)
-        nc.vector.tensor_scalar(sign_half, flat_cols[:, : 2 * TOKEN_BLOCKS], 0.0, 0.5, ALU.is_ge, ALU.subtract)
+        nc.tensor.transpose(banks[5][:, :P], factor_rows[:], identity[:])
+        cols1 = tile("cols1", [P, 2 * BLOCKS], F32)
+        nc.scalar.copy(cols1[:], banks[5][:, : 2 * BLOCKS])
+        grouped00 = tile("grouped00", [P, HALF * PACK], BF16)[:]
+        cols2 = grouped00[:, : 8 * BLOCKS].bitcast(F32).rearrange("s (n b) -> s n b", n=4)
+        nc.scalar.copy(cols2[:, :2, :], banks[5][:, 2 * BLOCKS : 4 * BLOCKS].rearrange("s (n b) -> s n b", n=2))
+        nc.scalar.activation(cols2[:, 2, :], banks[5][:, 2 * BLOCKS : 3 * BLOCKS], ABS)
+        nc.scalar.activation(cols2[:, 3, :], banks[5][:, 3 * BLOCKS : 4 * BLOCKS], ABS, scale=RATIO_FLOOR)
+        own2_cols, oth2_cols, own2_size, floor = [cols2[:, n, :] for n in range(4)]
+        small = tile("small", [P, 4, 8], F32)
+        sign_half, safe_size, inverse, signed_half = [small[:, n, :BLOCKS] for n in range(4)]
+        own2_safe, ratio_cols = [tile(name, [P, BLOCKS], F32)[:] for name in ("own2_safe", "ratio_cols")]
+        nc.vector.scalar_tensor_tensor(safe_size, floor, ZERO_FLOOR, own2_size, ADD, ALU.max)
+        nc.vector.tensor_scalar(sign_half, own2_cols, 0.0, 0.5, ALU.is_ge, ALU.subtract)
         nc.vector.reciprocal(inverse, safe_size)
-        nc.vector.tensor_tensor(signed_half, flat_cols[:, 2 * TOKEN_BLOCKS :], sign_half, MULT)
-        nc.vector.scalar_tensor_tensor(own_safe[:], safe_size, 2.0, sign_half, MULT, MULT)
-        nc.vector.scalar_tensor_tensor(ratio_cols[:], signed_half, 2.0, inverse, MULT, MULT)
-        for b in range(TOKEN_BLOCKS):
-            nc.tensor.transpose(banks[3][:, block(b)], ratio_cols[:, TOKEN_BLOCKS + b : TOKEN_BLOCKS + b + 1].to_broadcast([P, P]), identity[:])
-        for b in range(TOKEN_BLOCKS):
-            nc.tensor.transpose(banks[4][:, block(b)], ratio_cols[:, b : b + 1].to_broadcast([P, P]), identity[:])
+        nc.vector.tensor_tensor(signed_half, oth2_cols, sign_half, MULT)
+        nc.vector.scalar_tensor_tensor(own2_safe, safe_size, 2.0, sign_half, MULT, MULT)
+        nc.vector.scalar_tensor_tensor(ratio_cols, signed_half, 2.0, inverse, MULT, MULT)
+        oth1_bank, ratio_bank = banks[6], banks[7]
+        spread(banks[4], cols1[:, :BLOCKS])
+        spread(oth1_bank, cols1[:, BLOCKS:])
+        own1_row = tile("own1_row", [P, S], F32)
+        spread(ratio_bank, ratio_cols)
+
+
+        def grouped_tile(name, tag):
+            return tile(name, [P, HALF * PACK], BF16, tag)[:]
 
         def regrouped_w1(v, g, grouped, copy):
             copy(
@@ -148,103 +154,159 @@ def tile_picked_ybutter_relu_p_kernel(
             )
             return grouped
 
-        def grouped_tile(name, tag):
-            return keep.tile([P, HALF * PACK], BF16, name=name, tag=tag, align_bytes=64)[:]
-
-        x_codes = [keep.tile([P, S], U32, name=f"x_codes{g}", tag=tag, align_bytes=64) for g, tag in enumerate(("small", "x_codes1"))]
-        x_bytes = keep.tile([P, S], U8, name="x_bytes", tag="factor_tile", align_bytes=64)
-
+        x_codes = [tile(f"x_codes{g}", [P, S], U32, tag) for g, tag in enumerate(("small", "w1_raw0_0"))]
+        x_bytes = tile("x_bytes", [P, S], U8, "grouped00")
         first_half = [(0, 0, HALF_TOKENS, 0), (0, HALF_TOKENS, HALF_TOKENS, 1), (1, 0, S, 2)]
-        second_half = [(2, 0, S, 5), (3, 0, S, 7)]
+        second_half = [(2, 0, S, 3), (3, 0, S, 4)]
 
-        def first_product_pass(g, weights, piece):
+        def first_product_pass(g, weights, piece, closes=True, column=0):
             t, first, count, bank = piece
             tokens = slice(first, first + count)
             codes, scales = weights
             nc.tensor.matmul_mx(
-                out=banks[bank][:, :count],
+                out=banks[bank][:, column : column + count],
                 lhsT=codes[:, block(t % 2)].bitcast(FP8X4),
                 lhsT_scale=scales[:, block(t % 2)],
                 rhs=x_codes[g][:, tokens].bitcast(FP8X4),
                 rhs_scale=x_bytes[4 * g :, tokens],
                 start=(g == 0),
-                stop=(g == PASSES - 1),
+                stop=(g == PASSES - 1 and closes),
             )
+
+        weights00 = quantise("w1_0_0", regrouped_w1(0, 0, grouped00, nc.scalar.copy), HALF)
+        nc.scalar.copy(own1_row[:], banks[4][:])
+        nc.vector.tensor_copy(x_codes[0][:], word_tables[0][:].indirect(offs_tile[:]))
+        nc.vector.tensor_copy(x_bytes[:], scale_table[:].indirect(offs_tile[:]))
+        for piece in first_half:
+            first_product_pass(0, weights00, piece)
+        weights01 = quantise("w1_0_1", regrouped_w1(0, 1, w1_raw[0, 0][:, :2, :].rearrange("p j c -> p (j c)").bitcast(BF16), nc.scalar.copy), HALF)
+        late_rows = tile("late_rows", [P, 2, S], F32, "w1_raw0_1")
+        oth1_row, ratio_row = late_rows[:, 0, :], late_rows[:, 1, :]
+        nc.scalar.copy(oth1_row, oth1_bank[:])
+        nc.scalar.copy(ratio_row, ratio_bank[:])
+
+        halves = [slice(0, HALF_TOKENS), slice(HALF_TOKENS, S)]
+        for tokens in halves:
+            nc.vector.tensor_copy(x_codes[1][:, tokens], word_tables[1][:].indirect(entries(offs_tile, tokens)))
 
         def finish_y(weights, piece):
             t, first, count, bank = piece
             first_product_pass(1, weights, piece)
             nc.scalar.activation(y[t][:, first : first + count], banks[bank][:, :count], RELU)
 
-        nc.vector.tensor_copy(x_codes[0][:], word_tables[0][:].indirect(offs_tile[:]))
-        weights = quantise("w1_0_0", regrouped_w1(0, 0, factor_tile[:].bitcast(BF16), nc.scalar.copy), HALF, "table0")
-        nc.vector.tensor_copy(x_bytes[:], scale_table[:].indirect(offs_tile[:]))
-        for piece in first_half:
-            first_product_pass(0, weights, piece)
-        weights = quantise("w1_0_1", regrouped_w1(0, 1, grouped_tile("w1_grouped0_1", "w1_grouped0_1"), nc.scalar.copy), HALF)
-        ratio_row = keep.tile([P, S], F32, name="ratio_row", tag="w1_grouped0_1", align_bytes=64)
-        nc.scalar.copy(ratio_row[:], banks[3][:])
-        ratio1_row = keep.tile([P, S], F32, name="ratio1_row", tag="w1_raw0_1", align_bytes=64)
-        nc.scalar.copy(ratio1_row[:], banks[4][:])
-        for first in (0, HALF_TOKENS):
-            nc.vector.tensor_copy(
-                x_codes[1][:, first : first + HALF_TOKENS],
-                word_tables[1][:].indirect(entries(offs_tile, first, HALF_TOKENS)),
-            )
-        second_grouped = regrouped_w1(1, 0, grouped_tile("w1_grouped1_0", "table1"), nc.vector.tensor_copy)
-        for piece in first_half:
-            finish_y(weights, piece)
+        grouped10 = regrouped_w1(1, 0, grouped_tile("grouped10", "word_table1"), nc.vector.tensor_copy)
+        finish_y(weights01, first_half[0])
+        first_product_pass(1, weights01, (1, 0, HALF_TOKENS, 2), False)
+        finish_y(weights01, first_half[1])
+        first_product_pass(1, weights01, (1, HALF_TOKENS, HALF_TOKENS, 2), True, HALF_TOKENS)
 
-        def own1_term(t, turned, back):
-            scaled = ring.tile([P, S], F32, name="scaled", align_bytes=64)
-            own_cols = own1_for_tile0[:] if t == 0 else factor_cols[:, OWN1, :]
-            for b in range(TOKEN_BLOCKS):
-                nc.tensor.transpose(turned[:, block(b)], y[t][:, block(b)], identity[:])
-            for b in range(TOKEN_BLOCKS):
-                nc.scalar.activation(scaled[:, block(b)], turned[:, block(b)], COPY, scale=own_cols[:, b : b + 1])
-            for b in range(TOKEN_BLOCKS):
-                nc.tensor.transpose(back[:, block(b)], scaled[:, block(b)], identity[:])
-            return back
+        own_terms = [tile(f"own1_term{t}", [P, S], F32) for t in range(TILES)]
+        oth_terms = [tile(f"oth1_term{t}", [P, S], F32) for t in range(TILES)]
 
-        def oth1_term(t):
-            term = keep.tile([P, S], F32, name=f"oth1_term{t}", tag=f"oth1_term{t}")
-            nc.vector.tensor_tensor(term[:], y[t][:].indirect(mix1_tile[:]), oth1_row[:], MULT)
-            return term
+        def own1_term(piece):
+            t, first, count, bank = piece
+            tokens = slice(first, first + count)
+            nc.vector.scalar_tensor_tensor(own_terms[t][:, tokens], banks[bank][:, :count], 0.0, own1_row[:, tokens], ALU.max, MULT)
 
-        def finish_h1(t, own_term, oth_term):
-            nc.vector.tensor_tensor(h1[t][:, :S], own_term[:], oth_term[:], ADD)
+        def fused1(t):
+            nc.vector.tensor_tensor(oth_terms[t][:], y[t][:].indirect(mix1_tile[:]), oth1_row, MULT)
 
-        partners = {}
-        h2_turned = [keep.tile([P, 2, 2 * P], BF16, name=f"h2_turned{b}", tag=f"h2_turned{b}", align_bytes=64) for b in range(TOKEN_BLOCKS)]
+        def fetch(name, window, list_tile, tag=""):
+            picked = tile(name, [P, S], F32, tag)
+            nc.scalar.activation(picked[:], window[:].indirect(list_tile[:]), COPY)
+            return picked
 
-        def fetch_partners(partner, t, tokens):
-            offsets = entries(mix2_tile, tokens.start, tokens.stop - tokens.start)
-            nc.vector.tensor_tensor(partner, h1[t][:].indirect(offsets), ratio_row[:, tokens], MULT)
+        def finish_h1(t, engine):
+            engine.tensor_tensor(h1[t][:, :S], own_terms[t][:], oth_terms[t][:], ADD)
 
-        def turn_into(place, source, start, stop):
-            nc.tensor.matmul(place, source, identity[:], start=start, stop=stop, is_transpose=True)
+        weights10 = quantise("w1_1_0", grouped10, HALF)
+        fused1(0)
+        grouped11 = regrouped_w1(1, 1, grouped_tile("grouped11", "w1_0_1"), nc.scalar.copy)
+        weights11 = quantise("w1_1_1", grouped11, HALF)
+        nc.scalar.activation(y[1][:, :S], banks[2][:], RELU)
+        own1_term(first_half[0])
+        own1_term(first_half[1])
+        finish_h1(0, nc.gpsimd)
+        picked = tile("picked1_1", [P, S], F32)
+        for tokens in halves:
+            nc.scalar.activation(picked[:, tokens], y[1][:].indirect(entries(mix1_tile, tokens)), COPY)
+        own1_term(first_half[2])
+        nc.vector.tensor_tensor(oth_terms[1][:], picked[:], oth1_bank[:], MULT)
+        finish_h1(1, nc.gpsimd)
+        for piece in second_half:
+            first_product_pass(0, weights10, piece)
+        for piece in second_half:
+            finish_y(weights11, piece)
+        picked = fetch("picked1_2", y[2], mix1_tile)
+        for piece in second_half:
+            own1_term(piece)
+        fused1(3)
+        finish_h1(3, nc.gpsimd)
+        nc.vector.tensor_tensor(oth_terms[2][:], picked[:], oth1_bank[:], MULT)
 
-        def finish_h2(v, b, sums):
-            nc.scalar.activation(
-                h2_turned[b][:, :, block(v)], sums.rearrange("s (u c) -> s u c", u=2), COPY, scale=own2_safe[:, b : b + 1]
-            )
+        partners = [tile(f"partner{t}", [P, S], F32) for t in range(TILES)]
+        picked2 = [fetch(f"picked2_{t}", h1[t], mix2_tile, f"y{t + 2}") for t in range(2)]
+        nc.vector.tensor_tensor(partners[0][:], picked2[0][:], ratio_bank[:], MULT)
+        finish_h1(2, nc.vector)
+        nc.vector.tensor_tensor(partners[1][:], picked2[1][:], ratio_bank[:], MULT)
+
+        last = BLOCKS - 1
+        sum_banks = [banks[n] for n in (5, 0, 1, 2)]
+
+        def place(b, t):
+            bank = banks[3] if b == last and t >= 2 else sum_banks[b]
+            return bank[:, block(2 * (t % 2) + t // 2)]
+
+        def turn_into(b, t, source, start, stop):
+            nc.tensor.matmul(place(b, t), source[:, block(b)], identity[:], start=start, stop=stop, is_transpose=True)
+
+        for t, source in ((1, h1[1]), (0, h1[0]), (0, partners[0]), (3, h1[3]), (2, h1[2]), (1, partners[1])):
+            for b in range(BLOCKS):
+                opens = source is h1[1] or (b == last and source is h1[3])
+                turn_into(b, t, source, opens, b == last and source is partners[1])
+        h2_turned = [tile(f"h2_turned{b}", [P, 2, 2, P], BF16) for b in range(BLOCKS)]
+
+        def finish_h2(b, target, sums):
+            nc.scalar.activation(target, sums, COPY, scale=own2_safe[:, b : b + 1])
+
+        def quarters(bank):
+            return bank[:].rearrange("s (u v c) -> s u v c", u=2, v=2)
+
+        finish_h2(last, h2_turned[last][:, :, 0, :], quarters(sum_banks[last])[:, :, 0, :])
+
+        w2_grouped = tile("w2_grouped", [P, N * PACK], BF16, "own1_term2")
+        nc.vector.tensor_copy(
+            w2_grouped[:].rearrange("p (c i j) -> p c j i", i=4, j=PACK), w2_raw[:].rearrange("p j (c i) -> p c j i", i=4)
+        )
+        w2_codes, w2_scales = quantise("w2", w2_grouped[:], N)
 
         out_view = out.rearrange("(m p) s -> p m s", p=P)
-
-        h2_grouped = {}
-
-        def turn_back(b, bank, copy):
-            words = bank[:, :HALF_TOKENS].rearrange("p (u s) -> p u s", u=2)
+        picked = tile("picked2_2", [P, S], F32)
+        product_banks = [banks[n] for n in (4, 6, 5, 0)]
+        grouped = []
+        for b in range(BLOCKS):
+            if b % 2 == 0:
+                tokens = halves[b // 2]
+                nc.scalar.activation(picked[:, tokens], h1[2][:].indirect(entries(mix2_tile, tokens)), COPY)
+                nc.vector.tensor_tensor(partners[2][:, tokens], picked[:, tokens], ratio_bank[:, tokens], MULT)
+            nc.vector.tensor_tensor(partners[3][:, block(b)], h1[3][:].indirect(entries(mix2_tile, block(b))), ratio_row[:, block(b)], MULT)
+            for t in (2, 3):
+                turn_into(b, t, partners[t], False, t == 3)
+            if b < last:
+                finish_h2(b, h2_turned[b][:], quarters(sum_banks[b]))
+            else:
+                finish_h2(b, h2_turned[b][:, :, 1, :], quarters(banks[3])[:, :, 1, :])
+            words = product_banks[b][:, :HALF_TOKENS].rearrange("p (u s) -> p u s", u=2)
             for u in range(2):
-                nc.tensor.transpose(words[:, u, :], h2_turned[b][:, u, :].bitcast(F32), identity[:])
-            h2_grouped[b] = keep.tile([P, K_PASS], BF16, name=f"h2_grouped{b}", tag=f"h2_grouped{b}", align_bytes=64)
-            copy(
-                h2_grouped[b][:].bitcast(F32).rearrange("p (s u) -> p s u", u=2), words.rearrange("p u s -> p s u")
-            )
-
-        def second_product(b, places, weights):
-            h2_codes, h2_scales = quantise(f"h2_{b}", h2_grouped[b][:], P)
-            w2_codes, w2_scales = weights
+                nc.tensor.transpose(words[:, u, :], h2_turned[b][:, u].rearrange("s v c -> s (v c)").bitcast(F32), identity[:])
+            grouped.append(tile(f"h2_grouped{b}", [P, K_PASS], BF16))
+            copy = nc.vector.tensor_copy if b < 2 else nc.scalar.copy
+            copy(grouped[b][:].bitcast(F32).rearrange("p (s u) -> p s u", u=2), words.rearrange("p u s -> p s u"))
+        for b in range(BLOCKS):
+            h2_codes, h2_scales = quantise(f"h2_{b}", grouped[b][:], P)
+            places = [product_banks[b][:, block(2 + m)] for m in range(OUT_TILES)]
+            if b == last:
+                places[0] = banks[1][:, :P]
             for m in range(OUT_TILES):
                 nc.tensor.matmul_mx(
                     out=places[m],
@@ -255,76 +317,11 @@ def tile_picked_ybutter_relu_p_kernel(
                     start=True,
                     stop=True,
                 )
-
-        def staged_tile(b):
-            tag = f"h2_turned{b + 2}" if b < 2 else f"h2_grouped{b + 1}"
-            return keep.tile([P, OUT_TILES, P], F32, name=f"staged{b}", tag=tag, align_bytes=64)
-
-        oth_terms = [oth1_term(0), oth1_term(1)]
-        own_terms = [own1_term(0, turned=banks[5], back=banks[6])]
-        pass0_weights = quantise("w1_1_0", second_grouped, HALF, "y0")
-        pass1_weights = quantise("w1_1_1", regrouped_w1(1, 1, grouped_tile("w1_grouped1_1", "last_w1"), nc.scalar.copy), HALF)
-        partners[0] = keep.tile([P, S], F32, name="partner0", tag="last_w1", align_bytes=64)
-        own_terms.append(own1_term(1, turned=banks[7], back=banks[0]))
-        for piece in second_half:
-            first_product_pass(0, pass0_weights, piece)
-            finish_y(pass1_weights, piece)
-        finish_h1(0, own_terms[0], oth_terms[0])
-        fetch_partners(partners[0][:], 0, slice(0, S))
-        finish_h1(1, own_terms[1], oth_terms[1])
-
-        ratio_term = keep.tile([P, S], F32, name="ratio_term")
-        nc.vector.tensor_tensor(ratio_term[:], y[2][:].indirect(mix1_tile[:]), ratio1_row[:], MULT)
-        oth_term3 = oth1_term(3)
-        partners[1] = keep.tile([P, S], F32, name="partner1", tag="w1_raw0_1", align_bytes=64)
-        fetch_partners(partners[1][:], 1, slice(0, S))
-        for b in range(TOKEN_BLOCKS):
-            turn_into(banks[3][:, block(b)], y[2][:, block(b)], b == 0, False)
-        own_term3 = own1_term(3, turned=banks[1], back=banks[2])
-        for b in range(TOKEN_BLOCKS):
-            turn_into(banks[3][:, block(b)], ratio_term[:, block(b)], False, b + 1 == TOKEN_BLOCKS)
-        h1_turned = keep.tile([P, S], F32, name="h1_turned", tag="h1_turned", align_bytes=64)
-        for b in range(TOKEN_BLOCKS):
-            nc.scalar.activation(h1_turned[:, block(b)], banks[3][:, block(b)], COPY, scale=own1_safe[:, b : b + 1])
-        for b in range(TOKEN_BLOCKS):
-            nc.tensor.transpose(banks[4][:, block(b)], h1_turned[:, block(b)], identity[:])
-        nc.scalar.copy(h1[2][:], banks[4][:])
-        first_sums = [(banks[5], banks[7])[b // 2][:, (b % 2) * HALF : (b % 2 + 1) * HALF] for b in range(TOKEN_BLOCKS)]
-        for n, sources in enumerate((h1, partners)):
-            for b in range(TOKEN_BLOCKS):
-                for u in range(2):
-                    first, last = n == 0 and b % 2 == 0 and u == 0, n == 1 and b % 2 == 1 and u == 1
-                    turn_into(first_sums[b][:, block(u)], sources[u][:, block(b)], first, last)
-        w2_grouped = keep.tile([P, N * PACK], BF16, name="w2_grouped", tag="w1_1_1", align_bytes=64)
-        nc.scalar.copy(
-            w2_grouped[:].rearrange("p (c i j) -> p c j i", i=4, j=PACK), w2_raw[:].rearrange("p j (c i) -> p c j i", i=4)
-        )
-        for b in range(TOKEN_BLOCKS):
-            finish_h2(0, b, first_sums[b])
-        finish_h1(3, own_term3, oth_term3)
-        second_sums = [banks[n][:, :HALF] for n in (6, 0, 3, 1)]
-        for u in range(2):
-            for b in range(TOKEN_BLOCKS):
-                turn_into(second_sums[b][:, block(u)], h1[2 + u][:, block(b)], u == 0, False)
-        late_partners = keep.tile([P, TOKEN_BLOCKS, 2, P], F32, name="late_partners", tag="oth1_term3")
-        product_banks = [banks[n] for n in (4, 2, 5, 7)]
-        for b in range(TOKEN_BLOCKS):
-            for u in (1, 0):
-                fetch_partners(late_partners[:, b, u, :], 2 + u, block(b))
-                turn_into(second_sums[b][:, block(u)], late_partners[:, b, u, :], False, u == 0)
-            finish_h2(1, b, second_sums[b])
-            turn_back(b, product_banks[b], nc.vector.tensor_copy if b < 2 else nc.scalar.copy)
-        w2_weights = quantise("w2", w2_grouped[:], N, "h1_3")
-        last = TOKEN_BLOCKS - 1
-        for b in range(last):
-            second_product(b, [product_banks[b][:, block(2 + m)] for m in range(OUT_TILES)], w2_weights)
-        last_places = [banks[6][:, :P], product_banks[last][:, block(2)]]
-        second_product(last, last_places, w2_weights)
-        for b, copy in enumerate((nc.scalar.copy, nc.scalar.copy, nc.vector.tensor_copy)):
-            staged = staged_tile(b)
-            copy(staged[:], product_banks[b][:, HALF_TOKENS:].rearrange("p (m s) -> p m s", m=OUT_TILES))
+            staged = tile(f"staged{b}", [P, OUT_TILES, P], F32)
+            if b < last:
+                copy = nc.scalar.copy if b < 2 else nc.vector.tensor_copy
+                copy(staged[:], product_banks[b][:, HALF_TOKENS:].rearrange("p (m s) -> p m s", m=OUT_TILES))
+            else:
+                for m, copy in enumerate((nc.scalar.copy, nc.vector.tensor_copy)):
+                    copy(staged[:, m, :], places[m])
             nc.sync.dma_start(out_view[:, :, block(b)], staged[:])
-        staged = staged_tile(last)
-        for m, copy in enumerate((nc.scalar.copy, nc.vector.tensor_copy)):
-            copy(staged[:, m, :], last_places[m])
-        nc.sync.dma_start(out_view[:, :, block(last)], staged[:])

@@ -52,9 +52,9 @@ def tile_picked_ybutter_relu_p_kernel(
         def entries(list_tile, tokens):
             return list_tile[:, tokens.start // LIST_ROWS : tokens.stop // LIST_ROWS]
 
-        def quantise(name, grouped, width, tag=""):
+        def quantise(name, grouped, width, tag="", scale_tag=""):
             codes = keep.tile([P, width], U32, name=name + "_codes", tag=tag or name, align_bytes=64)
-            scales = keep.tile([P, width], U8, name=name + "_scales", align_bytes=64)
+            scales = keep.tile([P, width], U8, name=name + "_scales", tag=scale_tag or name + "_scales", align_bytes=64)
             nc.vector.quantize_mx(out=codes[:].bitcast(FP8X4), scales=scales[:], in_=grouped)
             return codes, scales
 
@@ -75,21 +75,20 @@ def tile_picked_ybutter_relu_p_kernel(
             return keep.tile(shape, dtype, name=name, tag=tag or name, align_bytes=64)
 
         factor_rows = tile("factor_rows", [P, P], F32)
-        nc.gpsimd.memset(factor_rows[:], 0.0)
+        nc.vector.memset(factor_rows[:], 0.0)
         scale_table = tile("scale_table", [P, T], U8)
-        nc.gpsimd.memset(scale_table[:].bitcast(I32), 0)
+        nc.gpsimd.memset(scale_table[:, : T // 2].bitcast(I32), 0)
+        nc.vector.memset(scale_table[:, T // 2 :].bitcast(I32), 0)
         identity = tile("identity", [P, P], F32)
         make_identity(nc, identity[:])
 
         def load_w1(v, g):
             return load_rows(f"w1_raw{v}_{g}", w1[g * K_PASS : (g + 1) * K_PASS, v * HALF : (v + 1) * HALF])
 
-        def load_scales():
-            for q in range(QUADRANTS):
-                nc.sync.dma_start(
-                    scale_table[32 * q : 32 * q + 4 * PASSES, :].bitcast(I32),
-                    x_scales[:, 4 * q : 4 * q + 4, :].bitcast(I32),
-                )
+        def load_scales(q, g):
+            nc.sync.dma_start(
+                scale_table[32 * q + 4 * g : 32 * q + 4 * g + 4, :].bitcast(I32), x_scales[g, 4 * q : 4 * q + 4, :].bitcast(I32)
+            )
 
         def load_factor(n, factor):
             nc.sync.dma_start(
@@ -98,15 +97,21 @@ def tile_picked_ybutter_relu_p_kernel(
 
         offs_tile = load("offs_tile", offs, [P, S // LIST_ROWS], U16)
         w1_raw = {(0, 0): load_w1(0, 0)}
-        for n, factor in enumerate((own1, oth1, own2, oth2)):
-            load_factor(n, factor)
+        for n, factor in enumerate((oth1, own2, oth2)):
+            load_factor(n + 1, factor)
+        load_scales(1, 0)
+        load_scales(1, 1)
         word_tables = [load_words(0)]
+        nc.sync.dma_start(scale_table[: 4 * PASSES, :].bitcast(I32), x_scales[:, :4, :].bitcast(I32))
         w1_raw[0, 1] = load_w1(0, 1)
-        load_scales()
+        for q in (2, 3):
+            for g in range(PASSES):
+                load_scales(q, g)
         word_tables.append(load_words(1))
         w1_raw[1, 0] = load_w1(1, 0)
         mix1_tile = load("mix1_tile", mix1, [P, S // LIST_ROWS], U16)
         w1_raw[1, 1] = load_w1(1, 1)
+        own1_row = load("own1_row", own1, [P, S], F32)
         mix2_tile = load("mix2_tile", mix2, [P, S // LIST_ROWS], U16)
         w2_raw = load_rows("w2_raw", w2)
 
@@ -120,8 +125,8 @@ def tile_picked_ybutter_relu_p_kernel(
                 nc.tensor.transpose(bank[:, block(b)], columns[:, b : b + 1].to_broadcast([P, P]), identity[:])
 
         nc.tensor.transpose(banks[5][:, :P], factor_rows[:], identity[:])
-        cols1 = tile("cols1", [P, 2 * BLOCKS], F32)
-        nc.scalar.copy(cols1[:], banks[5][:, : 2 * BLOCKS])
+        cols1 = tile("cols1", [P, BLOCKS], F32)
+        nc.scalar.copy(cols1[:], banks[5][:, BLOCKS : 2 * BLOCKS])
         grouped00 = tile("grouped00", [P, HALF * PACK], BF16)[:]
         cols2 = grouped00[:, : 8 * BLOCKS].bitcast(F32).rearrange("s (n b) -> s n b", n=4)
         nc.scalar.copy(cols2[:, :2, :], banks[5][:, 2 * BLOCKS : 4 * BLOCKS].rearrange("s (n b) -> s n b", n=2))
@@ -138,9 +143,7 @@ def tile_picked_ybutter_relu_p_kernel(
         nc.vector.scalar_tensor_tensor(own2_safe, safe_size, 2.0, sign_half, MULT, MULT)
         nc.vector.scalar_tensor_tensor(ratio_cols, signed_half, 2.0, inverse, MULT, MULT)
         oth1_bank, ratio_bank = banks[6], banks[7]
-        spread(banks[4], cols1[:, :BLOCKS])
-        spread(oth1_bank, cols1[:, BLOCKS:])
-        own1_row = tile("own1_row", [P, S], F32)
+        spread(oth1_bank, cols1[:])
         spread(ratio_bank, ratio_cols)
 
 
@@ -174,7 +177,6 @@ def tile_picked_ybutter_relu_p_kernel(
             )
 
         weights00 = quantise("w1_0_0", regrouped_w1(0, 0, grouped00, nc.scalar.copy), HALF)
-        nc.scalar.copy(own1_row[:], banks[4][:])
         nc.vector.tensor_copy(x_codes[0][:], word_tables[0][:].indirect(offs_tile[:]))
         nc.vector.tensor_copy(x_bytes[:], scale_table[:].indirect(offs_tile[:]))
         for piece in first_half:
@@ -274,34 +276,40 @@ def tile_picked_ybutter_relu_p_kernel(
 
         finish_h2(last, h2_turned[last][:, :, 0, :], quarters(sum_banks[last])[:, :, 0, :])
 
-        w2_grouped = tile("w2_grouped", [P, N * PACK], BF16, "own1_term2")
-        nc.vector.tensor_copy(
-            w2_grouped[:].rearrange("p (c i j) -> p c j i", i=4, j=PACK), w2_raw[:].rearrange("p j (c i) -> p c j i", i=4)
-        )
-        w2_codes, w2_scales = quantise("w2", w2_grouped[:], N)
-
         out_view = out.rearrange("(m p) s -> p m s", p=P)
-        picked = tile("picked2_2", [P, S], F32)
+        picked = tile("picked2_2", [P, S], F32, "h1_1")
         product_banks = [banks[n] for n in (4, 6, 5, 0)]
         grouped = []
         for b in range(BLOCKS):
+            if b == 0:
+                nc.vector.tensor_tensor(partners[3][:, block(b)], h1[3][:].indirect(entries(mix2_tile, block(b))), ratio_row[:, block(b)], MULT)
             if b % 2 == 0:
                 tokens = halves[b // 2]
                 nc.scalar.activation(picked[:, tokens], h1[2][:].indirect(entries(mix2_tile, tokens)), COPY)
                 nc.vector.tensor_tensor(partners[2][:, tokens], picked[:, tokens], ratio_bank[:, tokens], MULT)
-            nc.vector.tensor_tensor(partners[3][:, block(b)], h1[3][:].indirect(entries(mix2_tile, block(b))), ratio_row[:, block(b)], MULT)
+            if b > 0:
+                nc.vector.tensor_tensor(partners[3][:, block(b)], h1[3][:].indirect(entries(mix2_tile, block(b))), ratio_row[:, block(b)], MULT)
             for t in (2, 3):
                 turn_into(b, t, partners[t], False, t == 3)
             if b < last:
                 finish_h2(b, h2_turned[b][:], quarters(sum_banks[b]))
             else:
-                finish_h2(b, h2_turned[b][:, :, 1, :], quarters(banks[3])[:, :, 1, :])
+                nc.vector.tensor_scalar(
+                    h2_turned[b][:, :, 1, :], quarters(banks[3])[:, :, 1, :], own2_safe[:, b : b + 1], None, MULT
+                )
             words = product_banks[b][:, :HALF_TOKENS].rearrange("p (u s) -> p u s", u=2)
             for u in range(2):
                 nc.tensor.transpose(words[:, u, :], h2_turned[b][:, u].rearrange("s v c -> s (v c)").bitcast(F32), identity[:])
+        for b in range(BLOCKS):
+            words = product_banks[b][:, :HALF_TOKENS].rearrange("p (u s) -> p u s", u=2)
             grouped.append(tile(f"h2_grouped{b}", [P, K_PASS], BF16))
-            copy = nc.vector.tensor_copy if b < 2 else nc.scalar.copy
-            copy(grouped[b][:].bitcast(F32).rearrange("p (s u) -> p s u", u=2), words.rearrange("p u s -> p s u"))
+            nc.scalar.copy(grouped[b][:].bitcast(F32).rearrange("p (s u) -> p s u", u=2), words.rearrange("p u s -> p s u"))
+        w2_grouped = tile("w2_grouped", [P, N * PACK], BF16, "h1_3")
+        nc.vector.tensor_copy(
+            w2_grouped[:].rearrange("p (c i j) -> p c j i", i=4, j=PACK), w2_raw[:].rearrange("p j (c i) -> p c j i", i=4)
+        )
+        w2_codes, w2_scales = quantise("w2", w2_grouped[:], N, scale_tag="own2_safe")
+
         for b in range(BLOCKS):
             h2_codes, h2_scales = quantise(f"h2_{b}", grouped[b][:], P)
             places = [product_banks[b][:, block(2 + m)] for m in range(OUT_TILES)]

@@ -116,8 +116,8 @@ def tile_picked_ybutter_relu_p_kernel(
         w2_raw = load_rows("w2_raw", w2)
 
         y = [tile(f"y{t}", [P, S + SPARE * (t != 1)], F32, "w1_raw1_1" if t == 1 else "") for t in range(TILES)]
-        h1 = [tile(f"h1_{t}", [P, S + SPARE * (t < 2)], F32) for t in range(TILES)]
-        for window in [y[0]] + y[2:] + h1[:2]:
+        h1 = [tile(f"h1_{t}", [P, S + SPARE * (t < 1)], F32) for t in range(TILES)]
+        for window in [y[0]] + y[2:] + h1[:1]:
             nc.gpsimd.memset(window[:, S:], 0.0)
 
         def spread(bank, columns):
@@ -159,7 +159,7 @@ def tile_picked_ybutter_relu_p_kernel(
 
         x_codes = [tile(f"x_codes{g}", [P, S], U32, tag) for g, tag in enumerate(("small", "w1_raw0_0"))]
         x_bytes = tile("x_bytes", [P, S], U8, "grouped00")
-        first_half = [(0, 0, HALF_TOKENS, 0), (0, HALF_TOKENS, HALF_TOKENS, 1), (1, 0, S, 2)]
+        first_half = [(0, 0, HALF_TOKENS, 0), (0, HALF_TOKENS, P, 1), (0, 3 * P, P, 5), (1, 0, S, 2)]
         second_half = [(2, 0, S, 3), (3, 0, S, 4)]
 
         def first_product_pass(g, weights, piece, closes=True, column=0):
@@ -188,7 +188,7 @@ def tile_picked_ybutter_relu_p_kernel(
         nc.scalar.copy(ratio_row, ratio_bank[:])
 
         halves = [slice(0, HALF_TOKENS), slice(HALF_TOKENS, S)]
-        for tokens in halves:
+        for tokens in (halves[0], block(2), block(3)):
             nc.vector.tensor_copy(x_codes[1][:, tokens], word_tables[1][:].indirect(entries(offs_tile, tokens)))
 
         def finish_y(weights, piece):
@@ -200,6 +200,7 @@ def tile_picked_ybutter_relu_p_kernel(
         finish_y(weights01, first_half[0])
         first_product_pass(1, weights01, (1, 0, HALF_TOKENS, 2), False)
         finish_y(weights01, first_half[1])
+        finish_y(weights01, first_half[2])
         first_product_pass(1, weights01, (1, HALF_TOKENS, HALF_TOKENS, 2), True, HALF_TOKENS)
 
         own_terms = [tile(f"own1_term{t}", [P, S], F32) for t in range(TILES)]
@@ -228,11 +229,12 @@ def tile_picked_ybutter_relu_p_kernel(
         nc.scalar.activation(y[1][:, :S], banks[2][:], RELU)
         own1_term(first_half[0])
         own1_term(first_half[1])
+        own1_term(first_half[2])
         finish_h1(0, nc.gpsimd)
         picked = tile("picked1_1", [P, S], F32)
         for tokens in halves:
             nc.scalar.activation(picked[:, tokens], y[1][:].indirect(entries(mix1_tile, tokens)), COPY)
-        own1_term(first_half[2])
+        own1_term(first_half[3])
         nc.vector.tensor_tensor(oth_terms[1][:], picked[:], oth1_bank[:], MULT)
         finish_h1(1, nc.gpsimd)
         for piece in second_half:
@@ -245,12 +247,16 @@ def tile_picked_ybutter_relu_p_kernel(
         fused1(3)
         finish_h1(3, nc.gpsimd)
         nc.vector.tensor_tensor(oth_terms[2][:], picked[:], oth1_bank[:], MULT)
+        finish_h1(2, nc.gpsimd)
 
         partners = [tile(f"partner{t}", [P, S], F32) for t in range(TILES)]
-        picked2 = [fetch(f"picked2_{t}", h1[t], mix2_tile, f"y{t + 2}") for t in range(2)]
-        nc.vector.tensor_tensor(partners[0][:], picked2[0][:], ratio_bank[:], MULT)
-        finish_h1(2, nc.vector)
-        nc.vector.tensor_tensor(partners[1][:], picked2[1][:], ratio_bank[:], MULT)
+        picked0 = fetch("picked2_0", h1[0], mix2_tile, "y2")
+        picked1 = [tile(f"picked2_1{n}", [P, HALF_TOKENS], F32, tag) for n, tag in enumerate(("h1_0", "y3"))]
+        nc.scalar.activation(picked1[1][:], h1[1][:].indirect(entries(mix2_tile, halves[1])), COPY)
+        nc.vector.tensor_tensor(partners[0][:], picked0[:], ratio_bank[:], MULT)
+        nc.vector.tensor_copy(picked1[0][:], h1[1][:].indirect(entries(mix2_tile, halves[0])))
+        for n in (1, 0):
+            nc.vector.tensor_tensor(partners[1][:, halves[n]], picked1[n][:], ratio_bank[:, halves[n]], MULT)
 
         last = BLOCKS - 1
         sum_banks = [banks[n] for n in (5, 0, 1, 2)]
@@ -262,7 +268,7 @@ def tile_picked_ybutter_relu_p_kernel(
         def turn_into(b, t, source, start, stop):
             nc.tensor.matmul(place(b, t), source[:, block(b)], identity[:], start=start, stop=stop, is_transpose=True)
 
-        for t, source in ((1, h1[1]), (0, h1[0]), (0, partners[0]), (3, h1[3]), (2, h1[2]), (1, partners[1])):
+        for t, source in ((1, h1[1]), (0, h1[0]), (0, partners[0]), (3, h1[3]), (1, partners[1]), (2, h1[2])):
             for b in range(BLOCKS):
                 opens = source is h1[1] or (b == last and source is h1[3])
                 turn_into(b, t, source, opens, b == last and source is partners[1])
@@ -277,20 +283,19 @@ def tile_picked_ybutter_relu_p_kernel(
         finish_h2(last, h2_turned[last][:, :, 0, :], quarters(sum_banks[last])[:, :, 0, :])
 
         out_view = out.rearrange("(m p) s -> p m s", p=P)
-        picked = tile("picked2_2", [P, S], F32, "h1_1")
+        picked = tile("picked2_3", [P, S], F32, "picked2_0b")
         product_banks = [banks[n] for n in (4, 6, 5, 0)]
         grouped = []
         for b in range(BLOCKS):
-            if b == 0:
-                nc.vector.tensor_tensor(partners[3][:, block(b)], h1[3][:].indirect(entries(mix2_tile, block(b))), ratio_row[:, block(b)], MULT)
             if b % 2 == 0:
                 tokens = halves[b // 2]
-                nc.scalar.activation(picked[:, tokens], h1[2][:].indirect(entries(mix2_tile, tokens)), COPY)
-                nc.vector.tensor_tensor(partners[2][:, tokens], picked[:, tokens], ratio_bank[:, tokens], MULT)
-            if b > 0:
-                nc.vector.tensor_tensor(partners[3][:, block(b)], h1[3][:].indirect(entries(mix2_tile, block(b))), ratio_row[:, block(b)], MULT)
-            for t in (2, 3):
-                turn_into(b, t, partners[t], False, t == 3)
+                nc.scalar.activation(picked[:, tokens], h1[3][:].indirect(entries(mix2_tile, tokens)), COPY)
+                nc.vector.tensor_tensor(partners[3][:, tokens], picked[:, tokens], ratio_bank[:, tokens], MULT)
+            if b != 1:
+                tokens = halves[0] if b == 0 else block(b)
+                nc.vector.tensor_tensor(partners[2][:, tokens], h1[2][:].indirect(entries(mix2_tile, tokens)), ratio_row[:, tokens], MULT)
+            for t in (3, 2):
+                turn_into(b, t, partners[t], False, t == 2)
             if b < last:
                 finish_h2(b, h2_turned[b][:], quarters(sum_banks[b]))
             else:
@@ -304,7 +309,7 @@ def tile_picked_ybutter_relu_p_kernel(
             words = product_banks[b][:, :HALF_TOKENS].rearrange("p (u s) -> p u s", u=2)
             grouped.append(tile(f"h2_grouped{b}", [P, K_PASS], BF16))
             nc.scalar.copy(grouped[b][:].bitcast(F32).rearrange("p (s u) -> p s u", u=2), words.rearrange("p u s -> p s u"))
-        w2_grouped = tile("w2_grouped", [P, N * PACK], BF16, "h1_3")
+        w2_grouped = tile("w2_grouped", [P, N * PACK], BF16, "h1_2")
         nc.vector.tensor_copy(
             w2_grouped[:].rearrange("p (c i j) -> p c j i", i=4, j=PACK), w2_raw[:].rearrange("p j (c i) -> p c j i", i=4)
         )

@@ -43,6 +43,7 @@ def tile_picked_ybutter_relu_p_kernel(
     nc = tc.nc
     with ExitStack() as ctx:
         keep = ctx.enter_context(tc.tile_pool(name="keep", bufs=1))
+        chain = ctx.enter_context(tc.tile_pool(name="chain", bufs=1))
         psum = ctx.enter_context(tc.psum_pool(name="psum", bufs=1))
         banks = [psum.tile([P, S], F32, name=f"bank{b}") for b in range(8)]
 
@@ -64,7 +65,7 @@ def tile_picked_ybutter_relu_p_kernel(
             return tile
 
         def load_words(g):
-            table = keep.tile([P, T], U32, name=f"word_table{g}", tag=f"word_table{g}", align_bytes=64)
+            table = chain.tile([P, T], U32, name=f"word_table{g}", offset=T * 4 * (1 - g), align_bytes=64)
             nc.sync.dma_start(table[:].bitcast(I32), x_words[g].rearrange("p n t -> p (n t)").bitcast(I32))
             return table
 
@@ -102,12 +103,11 @@ def tile_picked_ybutter_relu_p_kernel(
         load_scales(1, 0)
         load_scales(1, 1)
         word_tables = [load_words(0)]
-        nc.sync.dma_start(scale_table[: 4 * PASSES, :].bitcast(I32), x_scales[:, :4, :].bitcast(I32))
-        w1_raw[0, 1] = load_w1(0, 1)
-        for q in (2, 3):
+        for q in (0, 2, 3):
             for g in range(PASSES):
                 load_scales(q, g)
         word_tables.append(load_words(1))
+        w1_raw[0, 1] = load_w1(0, 1)
         w1_raw[1, 0] = load_w1(1, 0)
         mix1_tile = load("mix1_tile", mix1, [P, S // LIST_ROWS], U16)
         w1_raw[1, 1] = load_w1(1, 1)
@@ -157,9 +157,9 @@ def tile_picked_ybutter_relu_p_kernel(
             )
             return grouped
 
-        x_codes = [tile(f"x_codes{g}", [P, S], U32, tag) for g, tag in enumerate(("small", "w1_raw0_0"))]
+        x_codes = [tile(f"x_codes{g}", [P, S], U32, tag) for g, tag in enumerate(("small", "scale_table"))]
         x_bytes = tile("x_bytes", [P, S], U8, "grouped00")
-        first_half = [(0, 0, HALF_TOKENS, 0), (0, HALF_TOKENS, P, 1), (0, 3 * P, P, 5), (1, 0, S, 2)]
+        first_half = [(0, 0, HALF_TOKENS, 0), (0, HALF_TOKENS, HALF_TOKENS, 1), (1, 0, S, 2)]
         second_half = [(2, 0, S, 3), (3, 0, S, 4)]
 
         def first_product_pass(g, weights, piece, closes=True, column=0):
@@ -181,27 +181,40 @@ def tile_picked_ybutter_relu_p_kernel(
         nc.vector.tensor_copy(x_bytes[:], scale_table[:].indirect(offs_tile[:]))
         for piece in first_half:
             first_product_pass(0, weights00, piece)
-        weights01 = quantise("w1_0_1", regrouped_w1(0, 1, w1_raw[0, 0][:, :2, :].rearrange("p j c -> p (j c)").bitcast(BF16), nc.scalar.copy), HALF)
-        late_rows = tile("late_rows", [P, 2, S], F32, "w1_raw0_1")
+        late_rows = tile("late_rows", [P, 2, S], F32)
         oth1_row, ratio_row = late_rows[:, 0, :], late_rows[:, 1, :]
         nc.scalar.copy(oth1_row, oth1_bank[:])
         nc.scalar.copy(ratio_row, ratio_bank[:])
-
         halves = [slice(0, HALF_TOKENS), slice(HALF_TOKENS, S)]
-        for tokens in (halves[0], block(2), block(3)):
-            nc.vector.tensor_copy(x_codes[1][:, tokens], word_tables[1][:].indirect(entries(offs_tile, tokens)))
+        nc.vector.tensor_copy(x_codes[1][:], word_tables[1][:].indirect(offs_tile[:]))
+        grouped01 = w1_raw[0, 0][:, :2, :].rearrange("p j c -> p (j c)").bitcast(BF16)
+        for u in range(2):
+            nc.scalar.copy(
+                grouped01[:, u * K_PASS : (u + 1) * K_PASS].rearrange("p (m e j) -> p m j e", e=2, j=PACK),
+                w1_raw[0, 1][:].rearrange("p j (m u e) -> p u m j e", u=2, e=2)[:, u],
+            )
+        pass1_codes = chain.tile([P, HALF], U32, name="pass1_codes", offset=6144, align_bytes=64)
+        pass1_scales = tile("pass1_scales", [P, HALF], U8)
+        weights01 = (pass1_codes, pass1_scales)
+
+        def quantise_pass1(u):
+            nc.vector.quantize_mx(
+                out=pass1_codes[:, block(u)].bitcast(FP8X4),
+                scales=pass1_scales[:, block(u)],
+                in_=grouped01[:, u * K_PASS : (u + 1) * K_PASS],
+            )
 
         def finish_y(weights, piece):
             t, first, count, bank = piece
             first_product_pass(1, weights, piece)
             nc.scalar.activation(y[t][:, first : first + count], banks[bank][:, :count], RELU)
 
-        grouped10 = regrouped_w1(1, 0, grouped_tile("grouped10", "word_table1"), nc.vector.tensor_copy)
+        quantise_pass1(0)
+        grouped10 = regrouped_w1(1, 0, chain.tile([P, HALF * PACK], BF16, name="grouped10", offset=0, align_bytes=64)[:], nc.vector.tensor_copy)
+        quantise_pass1(1)
         finish_y(weights01, first_half[0])
-        first_product_pass(1, weights01, (1, 0, HALF_TOKENS, 2), False)
         finish_y(weights01, first_half[1])
-        finish_y(weights01, first_half[2])
-        first_product_pass(1, weights01, (1, HALF_TOKENS, HALF_TOKENS, 2), True, HALF_TOKENS)
+        first_product_pass(1, weights01, first_half[2])
 
         own_terms = [tile(f"own1_term{t}", [P, S], F32) for t in range(TILES)]
         oth_terms = [tile(f"oth1_term{t}", [P, S], F32) for t in range(TILES)]
@@ -224,17 +237,16 @@ def tile_picked_ybutter_relu_p_kernel(
 
         weights10 = quantise("w1_1_0", grouped10, HALF)
         fused1(0)
-        grouped11 = regrouped_w1(1, 1, grouped_tile("grouped11", "w1_0_1"), nc.scalar.copy)
+        grouped11 = regrouped_w1(1, 1, grouped_tile("grouped11", "w1_raw0_0"), nc.scalar.copy)
         weights11 = quantise("w1_1_1", grouped11, HALF)
         nc.scalar.activation(y[1][:, :S], banks[2][:], RELU)
         own1_term(first_half[0])
         own1_term(first_half[1])
-        own1_term(first_half[2])
         finish_h1(0, nc.gpsimd)
         picked = tile("picked1_1", [P, S], F32)
         for tokens in halves:
             nc.scalar.activation(picked[:, tokens], y[1][:].indirect(entries(mix1_tile, tokens)), COPY)
-        own1_term(first_half[3])
+        own1_term(first_half[2])
         nc.vector.tensor_tensor(oth_terms[1][:], picked[:], oth1_bank[:], MULT)
         finish_h1(1, nc.gpsimd)
         for piece in second_half:
@@ -284,16 +296,20 @@ def tile_picked_ybutter_relu_p_kernel(
 
         out_view = out.rearrange("(m p) s -> p m s", p=P)
         picked = tile("picked2_3", [P, S], F32, "picked2_0b")
+        for tokens in halves:
+            nc.scalar.activation(picked[:, tokens], h1[3][:].indirect(entries(mix2_tile, tokens)), COPY)
+        last_picked = tile("last_picked", [P, HALF_TOKENS], F32)
+        nc.scalar.activation(last_picked[:], h1[2][:].indirect(entries(mix2_tile, halves[1])), COPY)
         product_banks = [banks[n] for n in (4, 6, 5, 0)]
         grouped = []
         for b in range(BLOCKS):
             if b % 2 == 0:
                 tokens = halves[b // 2]
-                nc.scalar.activation(picked[:, tokens], h1[3][:].indirect(entries(mix2_tile, tokens)), COPY)
                 nc.vector.tensor_tensor(partners[3][:, tokens], picked[:, tokens], ratio_bank[:, tokens], MULT)
-            if b != 1:
-                tokens = halves[0] if b == 0 else block(b)
-                nc.vector.tensor_tensor(partners[2][:, tokens], h1[2][:].indirect(entries(mix2_tile, tokens)), ratio_row[:, tokens], MULT)
+            if b < 2:
+                nc.vector.tensor_tensor(partners[2][:, block(b)], h1[2][:].indirect(entries(mix2_tile, block(b))), ratio_row[:, block(b)], MULT)
+            if b == 2:
+                nc.vector.tensor_tensor(partners[2][:, tokens], last_picked[:], ratio_bank[:, tokens], MULT)
             for t in (3, 2):
                 turn_into(b, t, partners[t], False, t == 2)
             if b < last:
@@ -309,7 +325,7 @@ def tile_picked_ybutter_relu_p_kernel(
             words = product_banks[b][:, :HALF_TOKENS].rearrange("p (u s) -> p u s", u=2)
             grouped.append(tile(f"h2_grouped{b}", [P, K_PASS], BF16))
             nc.scalar.copy(grouped[b][:].bitcast(F32).rearrange("p (s u) -> p s u", u=2), words.rearrange("p u s -> p s u"))
-        w2_grouped = tile("w2_grouped", [P, N * PACK], BF16, "h1_2")
+        w2_grouped = tile("w2_grouped", [P, N * PACK], BF16, "last_picked")
         nc.vector.tensor_copy(
             w2_grouped[:].rearrange("p (c i j) -> p c j i", i=4, j=PACK), w2_raw[:].rearrange("p j (c i) -> p c j i", i=4)
         )

@@ -96,8 +96,8 @@ def tile_picked_ybutter_relu_p_kernel(
                 factor_rows[BLOCKS * n : BLOCKS * (n + 1), :], factor[:1, :].rearrange("r (b c) -> (r b) c", c=P)
             )
 
-        offs_tile = load("offs_tile", offs, [P, S // LIST_ROWS], U16)
         w1_raw = {(0, 0): load_w1(0, 0)}
+        offs_tile = load("offs_tile", offs, [P, S // LIST_ROWS], U16)
         for n, factor in enumerate((oth1, own2, oth2)):
             load_factor(n + 1, factor)
         load_scales(1, 0)

@@ -331,6 +331,7 @@ def tile_picked_ybutter_relu_p_kernel(
         )
         w2_codes, w2_scales = quantise("w2", w2_grouped[:], N, scale_tag="own2_safe")
 
+        last_staged = tile("last_staged", [P, OUT_TILES, HALF_TOKENS], F32)
         for b in range(BLOCKS):
             h2_codes, h2_scales = quantise(f"h2_{b}", grouped[b][:], P)
             places = [product_banks[b][:, block(2 + m)] for m in range(OUT_TILES)]
@@ -346,11 +347,13 @@ def tile_picked_ybutter_relu_p_kernel(
                     start=True,
                     stop=True,
                 )
-            staged = tile(f"staged{b}", [P, OUT_TILES, P], F32)
+            staged = tile(f"staged{b}", [P, OUT_TILES, P], F32) if b < 2 else last_staged[:, :, block(b - 2)]
             if b < last:
                 copy = nc.scalar.copy if b < 2 else nc.vector.tensor_copy
                 copy(staged[:], product_banks[b][:, HALF_TOKENS:].rearrange("p (m s) -> p m s", m=OUT_TILES))
             else:
                 for m, copy in enumerate((nc.scalar.copy, nc.vector.tensor_copy)):
                     copy(staged[:, m, :], places[m])
-            nc.sync.dma_start(out_view[:, :, block(b)], staged[:])
+            if b < 2:
+                nc.sync.dma_start(out_view[:, :, block(b)], staged[:])
+        nc.sync.dma_start(out_view[:, :, halves[1]], last_staged[:])

@@ -332,10 +332,10 @@ def tile_picked_ybutter_relu_p_kernel(
         w2_codes, w2_scales = quantise("w2", w2_grouped[:], N, scale_tag="own2_safe")
 
         last_staged = tile("last_staged", [P, OUT_TILES, HALF_TOKENS], F32)
-        for b in range(BLOCKS):
+        for b in (0, 1, 3, 2):
             h2_codes, h2_scales = quantise(f"h2_{b}", grouped[b][:], P)
             places = [product_banks[b][:, block(2 + m)] for m in range(OUT_TILES)]
-            if b == last:
+            if b == 2:
                 places[0] = banks[1][:, :P]
             for m in range(OUT_TILES):
                 nc.tensor.matmul_mx(
@@ -348,8 +348,8 @@ def tile_picked_ybutter_relu_p_kernel(
                     stop=True,
                 )
             staged = tile(f"staged{b}", [P, OUT_TILES, P], F32) if b < 2 else last_staged[:, :, block(b - 2)]
-            if b < last:
-                copy = nc.scalar.copy if b < 2 else nc.vector.tensor_copy
+            if b != 2:
+                copy = nc.vector.tensor_copy if b == 1 else nc.scalar.copy
                 copy(staged[:], product_banks[b][:, HALF_TOKENS:].rearrange("p (m s) -> p m s", m=OUT_TILES))
             else:
                 for m, copy in enumerate((nc.scalar.copy, nc.vector.tensor_copy)):

from contextlib import ExitStack

import concourse.mybir as mybir
from concourse.masks import make_identity

K, T, S, H, N = 1024, 2048, 512, 512, 256
FLOPS = 2 * K * H * S + 2 * H * N * S

F32 = mybir.dt.float32
BF16 = mybir.dt.bfloat16
I32 = mybir.dt.int32
U32 = mybir.dt.uint32
U16 = mybir.dt.uint16
U8 = mybir.dt.uint8
FP8X4 = mybir.dt.float8_e4m3fn_x4
ALU = mybir.AluOpType
MULT = ALU.mult
ADD = ALU.add
ABS = mybir.ActivationFunctionType.Abs
RELU = mybir.ActivationFunctionType.Relu
COPY = mybir.ActivationFunctionType.Copy

P = 128
PACK = 4
K_PASS = P * PACK
PASSES = K // K_PASS
TILES = H // P
HALF_TOKENS = S // 2
OUT_TILES = N // P
QUADRANTS = 4
LIST_ROWS = 16

HALF = H // 2
BLOCKS = S // P
SPARE = 16
RATIO_FLOOR = 2.0**-30
ZERO_FLOOR = 2.0**-100


def tile_picked_ybutter_relu_p_kernel(
    tc, x_words, x_scales, w1, w2, own1, oth1, own2, oth2, offs, mix1, mix2, out
):
    nc = tc.nc
    with ExitStack() as ctx:
        keep = ctx.enter_context(tc.tile_pool(name="keep", bufs=1))
        chain = ctx.enter_context(tc.tile_pool(name="chain", bufs=1))
        psum = ctx.enter_context(tc.psum_pool(name="psum", bufs=1))
        banks = [psum.tile([P, S], F32, name=f"bank{b}") for b in range(8)]

        def block(b):
            return slice(b * P, (b + 1) * P)

        def entries(list_tile, tokens):
            return list_tile[:, tokens.start // LIST_ROWS : tokens.stop // LIST_ROWS]

        def quantise(name, grouped, width, tag="", scale_tag=""):
            codes = keep.tile([P, width], U32, name=name + "_codes", tag=tag or name, align_bytes=64)
            scales = keep.tile([P, width], U8, name=name + "_scales", tag=scale_tag or name + "_scales", align_bytes=64)
            nc.vector.quantize_mx(out=codes[:].bitcast(FP8X4), scales=scales[:], in_=grouped)
            return codes, scales

        def load(name, source, shape, dtype):
            tile = keep.tile(shape, dtype, name=name, tag=name, align_bytes=64)
            nc.sync.dma_start(tile[:], source)
            return tile

        def load_words(g):
            table = chain.tile([P, T], U32, name=f"word_table{g}", offset=T * 4 * (1 - g), align_bytes=64)
            nc.sync.dma_start(table[:].bitcast(I32), x_words[g].rearrange("p n t -> p (n t)").bitcast(I32))
            return table

        def load_rows(name, rows):
            return load(name, rows.rearrange("(p j) c -> p j c", j=PACK), [P, PACK, rows.shape[1]], F32)

        def tile(name, shape, dtype, tag=""):
            return keep.tile(shape, dtype, name=name, tag=tag or name, align_bytes=64)

        factor_rows = tile("factor_rows", [P, P], F32)
        nc.vector.memset(factor_rows[:], 0.0)
        scale_table = tile("scale_table", [P, T], U8)
        nc.gpsimd.memset(scale_table[:, : T // 2].bitcast(I32), 0)
        nc.vector.memset(scale_table[:, T // 2 :].bitcast(I32), 0)
        identity = tile("identity", [P, P], F32)
        make_identity(nc, identity[:])

        def load_w1(v, g):
            return load_rows(f"w1_raw{v}_{g}", w1[g * K_PASS : (g + 1) * K_PASS, v * HALF : (v + 1) * HALF])

        def load_scales(q, g):
            nc.sync.dma_start(
                scale_table[32 * q + 4 * g : 32 * q + 4 * g + 4, :].bitcast(I32), x_scales[g, 4 * q : 4 * q + 4, :].bitcast(I32)
            )

        def load_factor(n, factor):
            nc.sync.dma_start(
                factor_rows[BLOCKS * n : BLOCKS * (n + 1), :], factor[:1, :].rearrange("r (b c) -> (r b) c", c=P)
            )

        w1_raw = {(0, 0): load_w1(0, 0)}
        offs_tile = load("offs_tile", offs, [P, S // LIST_ROWS], U16)
        for n, factor in enumerate((oth1, own2, oth2)):
            load_factor(n + 1, factor)
        load_scales(1, 0)
        load_scales(1, 1)
        word_tables = [load_words(0)]
        for q in (0, 2, 3):
            for g in range(PASSES):
                load_scales(q, g)
        word_tables.append(load_words(1))
        w1_raw[0, 1] = load_w1(0, 1)
        w1_raw[1, 0] = load_w1(1, 0)
        mix1_tile = load("mix1_tile", mix1, [P, S // LIST_ROWS], U16)
        w1_raw[1, 1] = load_w1(1, 1)
        own1_row = load("own1_row", own1, [P, S], F32)
        mix2_tile = load("mix2_tile", mix2, [P, S // LIST_ROWS], U16)
        w2_raw = load_rows("w2_raw", w2)

        y = [tile(f"y{t}", [P, S + SPARE * (t != 1)], F32, "w1_raw1_1" if t == 1 else "") for t in range(TILES)]
        h1 = [tile(f"h1_{t}", [P, S + SPARE * (t < 1)], F32) for t in range(TILES)]
        for window in [y[0]] + y[2:] + h1[:1]:
            nc.gpsimd.memset(window[:, S:], 0.0)

        def spread(bank, columns):
            for b in range(BLOCKS):
                nc.tensor.transpose(bank[:, block(b)], columns[:, b : b + 1].to_broadcast([P, P]), identity[:])

        nc.tensor.transpose(banks[5][:, :P], factor_rows[:], identity[:])
        cols1 = tile("cols1", [P, BLOCKS], F32)
        nc.scalar.copy(cols1[:], banks[5][:, BLOCKS : 2 * BLOCKS])
        grouped00 = tile("grouped00", [P, HALF * PACK], BF16)[:]
        cols2 = grouped00[:, : 8 * BLOCKS].bitcast(F32).rearrange("s (n b) -> s n b", n=4)
        nc.scalar.copy(cols2[:, :2, :], banks[5][:, 2 * BLOCKS : 4 * BLOCKS].rearrange("s (n b) -> s n b", n=2))
        nc.scalar.activation(cols2[:, 2, :], banks[5][:, 2 * BLOCKS : 3 * BLOCKS], ABS)
        nc.scalar.activation(cols2[:, 3, :], banks[5][:, 3 * BLOCKS : 4 * BLOCKS], ABS, scale=RATIO_FLOOR)
        own2_cols, oth2_cols, own2_size, floor = [cols2[:, n, :] for n in range(4)]
        small = tile("small", [P, 4, 8], F32)
        sign_half, safe_size, inverse, signed_half = [small[:, n, :BLOCKS] for n in range(4)]
        own2_safe, ratio_cols = [tile(name, [P, BLOCKS], F32)[:] for name in ("own2_safe", "ratio_cols")]
        nc.vector.scalar_tensor_tensor(safe_size, floor, ZERO_FLOOR, own2_size, ADD, ALU.max)
        nc.vector.tensor_scalar(sign_half, own2_cols, 0.0, 0.5, ALU.is_ge, ALU.subtract)
        nc.vector.reciprocal(inverse, safe_size)
        nc.vector.tensor_tensor(signed_half, oth2_cols, sign_half, MULT)
        nc.vector.scalar_tensor_tensor(own2_safe, safe_size, 2.0, sign_half, MULT, MULT)
        nc.vector.scalar_tensor_tensor(ratio_cols, signed_half, 2.0, inverse, MULT, MULT)
        oth1_bank, ratio_bank = banks[6], banks[7]
        spread(oth1_bank, cols1[:])
        spread(ratio_bank, ratio_cols)


        def grouped_tile(name, tag):
            return tile(name, [P, HALF * PACK], BF16, tag)[:]

        def regrouped_w1(v, g, grouped, copy):
            copy(
                grouped.rearrange("p (u m e j) -> p m j u e", u=2, e=2, j=PACK),
                w1_raw[v, g][:].rearrange("p j (m u e) -> p m j u e", u=2, e=2),
            )
            return grouped

        x_codes = [tile(f"x_codes{g}", [P, S], U32, tag) for g, tag in enumerate(("small", "scale_table"))]
        x_bytes = tile("x_bytes", [P, S], U8, "grouped00")
        first_half = [(0, 0, HALF_TOKENS, 0), (0, HALF_TOKENS, HALF_TOKENS, 1), (1, 0, S, 2)]
        second_half = [(2, 0, S, 3), (3, 0, S, 4)]

        def first_product_pass(g, weights, piece, closes=True, column=0):
            t, first, count, bank = piece
            tokens = slice(first, first + count)
            codes, scales = weights
            nc.tensor.matmul_mx(
                out=banks[bank][:, column : column + count],
                lhsT=codes[:, block(t % 2)].bitcast(FP8X4),
                lhsT_scale=scales[:, block(t % 2)],
                rhs=x_codes[g][:, tokens].bitcast(FP8X4),
                rhs_scale=x_bytes[4 * g :, tokens],
                start=(g == 0),
                stop=(g == PASSES - 1 and closes),
            )

        weights00 = quantise("w1_0_0", regrouped_w1(0, 0, grouped00, nc.scalar.copy), HALF)
        nc.vector.tensor_copy(x_codes[0][:], word_tables[0][:].indirect(offs_tile[:]))
        nc.vector.tensor_copy(x_bytes[:], scale_table[:].indirect(offs_tile[:]))
        for piece in first_half:
            first_product_pass(0, weights00, piece)
        late_rows = tile("late_rows", [P, 2, S], F32)
        oth1_row, ratio_row = late_rows[:, 0, :], late_rows[:, 1, :]
        nc.scalar.copy(oth1_row, oth1_bank[:])
        nc.scalar.copy(ratio_row, ratio_bank[:])
        halves = [slice(0, HALF_TOKENS), slice(HALF_TOKENS, S)]
        nc.vector.tensor_copy(x_codes[1][:], word_tables[1][:].indirect(offs_tile[:]))
        grouped01 = w1_raw[0, 0][:, :2, :].rearrange("p j c -> p (j c)").bitcast(BF16)
        for u in range(2):
            nc.scalar.copy(
                grouped01[:, u * K_PASS : (u + 1) * K_PASS].rearrange("p (m e j) -> p m j e", e=2, j=PACK),
                w1_raw[0, 1][:].rearrange("p j (m u e) -> p u m j e", u=2, e=2)[:, u],
            )
        pass1_codes = chain.tile([P, HALF], U32, name="pass1_codes", offset=6144, align_bytes=64)
        pass1_scales = tile("pass1_scales", [P, HALF], U8)
        weights01 = (pass1_codes, pass1_scales)

        def quantise_pass1(u):
            nc.vector.quantize_mx(
                out=pass1_codes[:, block(u)].bitcast(FP8X4),
                scales=pass1_scales[:, block(u)],
                in_=grouped01[:, u * K_PASS : (u + 1) * K_PASS],
            )

        def finish_y(weights, piece):
            t, first, count, bank = piece
            first_product_pass(1, weights, piece)
            nc.scalar.activation(y[t][:, first : first + count], banks[bank][:, :count], RELU)

        quantise_pass1(0)
        grouped10 = regrouped_w1(1, 0, chain.tile([P, HALF * PACK], BF16, name="grouped10", offset=0, align_bytes=64)[:], nc.vector.tensor_copy)
        quantise_pass1(1)
        finish_y(weights01, first_half[0])
        finish_y(weights01, first_half[1])
        first_product_pass(1, weights01, first_half[2])

        own_terms = [tile(f"own1_term{t}", [P, S], F32) for t in range(TILES)]
        oth_terms = [tile(f"oth1_term{t}", [P, S], F32) for t in range(TILES)]

        def own1_term(piece):
            t, first, count, bank = piece
            tokens = slice(first, first + count)
            nc.vector.scalar_tensor_tensor(own_terms[t][:, tokens], banks[bank][:, :count], 0.0, own1_row[:, tokens], ALU.max, MULT)

        def fused1(t):
            nc.vector.tensor_tensor(oth_terms[t][:], y[t][:].indirect(mix1_tile[:]), oth1_row, MULT)

        def fetch(name, window, list_tile, tag=""):
            picked = tile(name, [P, S], F32, tag)
            nc.scalar.activation(picked[:], window[:].indirect(list_tile[:]), COPY)
            return picked

        def finish_h1(t, engine):
            engine.tensor_tensor(h1[t][:, :S], own_terms[t][:], oth_terms[t][:], ADD)

        weights10 = quantise("w1_1_0", grouped10, HALF)
        fused1(0)
        grouped11 = regrouped_w1(1, 1, grouped_tile("grouped11", "w1_raw0_0"), nc.scalar.copy)
        weights11 = quantise("w1_1_1", grouped11, HALF)
        nc.scalar.activation(y[1][:, :S], banks[2][:], RELU)
        own1_term(first_half[0])
        own1_term(first_half[1])
        finish_h1(0, nc.gpsimd)
        picked = tile("picked1_1", [P, S], F32)
        for tokens in halves:
            nc.scalar.activation(picked[:, tokens], y[1][:].indirect(entries(mix1_tile, tokens)), COPY)
        own1_term(first_half[2])
        nc.vector.tensor_tensor(oth_terms[1][:], picked[:], oth1_bank[:], MULT)
        finish_h1(1, nc.gpsimd)
        for piece in second_half:
            first_product_pass(0, weights10, piece)
        for piece in second_half:
            finish_y(weights11, piece)
        picked = fetch("picked1_2", y[2], mix1_tile)
        for piece in second_half:
            own1_term(piece)
        fused1(3)
        finish_h1(3, nc.gpsimd)
        nc.vector.tensor_tensor(oth_terms[2][:], picked[:], oth1_bank[:], MULT)
        finish_h1(2, nc.gpsimd)

        partners = [tile(f"partner{t}", [P, S], F32) for t in range(TILES)]
        picked0 = fetch("picked2_0", h1[0], mix2_tile, "y2")
        picked1 = [tile(f"picked2_1{n}", [P, HALF_TOKENS], F32, tag) for n, tag in enumerate(("h1_0", "y3"))]
        nc.scalar.activation(picked1[1][:], h1[1][:].indirect(entries(mix2_tile, halves[1])), COPY)
        nc.vector.tensor_tensor(partners[0][:], picked0[:], ratio_bank[:], MULT)
        nc.vector.tensor_copy(picked1[0][:], h1[1][:].indirect(entries(mix2_tile, halves[0])))
        for n in (1, 0):
            nc.vector.tensor_tensor(partners[1][:, halves[n]], picked1[n][:], ratio_bank[:, halves[n]], MULT)

        last = BLOCKS - 1
        sum_banks = [banks[n] for n in (5, 0, 1, 2)]

        def place(b, t):
            bank = banks[3] if b == last and t >= 2 else sum_banks[b]
            return bank[:, block(2 * (t % 2) + t // 2)]

        def turn_into(b, t, source, start, stop):
            nc.tensor.matmul(place(b, t), source[:, block(b)], identity[:], start=start, stop=stop, is_transpose=True)

        for t, source in ((1, h1[1]), (0, h1[0]), (0, partners[0]), (3, h1[3]), (1, partners[1]), (2, h1[2])):
            for b in range(BLOCKS):
                opens = source is h1[1] or (b == last and source is h1[3])
                turn_into(b, t, source, opens, b == last and source is partners[1])
        h2_turned = [tile(f"h2_turned{b}", [P, 2, 2, P], BF16) for b in range(BLOCKS)]

        def finish_h2(b, target, sums):
            nc.scalar.activation(target, sums, COPY, scale=own2_safe[:, b : b + 1])

        def quarters(bank):
            return bank[:].rearrange("s (u v c) -> s u v c", u=2, v=2)

        finish_h2(last, h2_turned[last][:, :, 0, :], quarters(sum_banks[last])[:, :, 0, :])

        out_view = out.rearrange("(m p) s -> p m s", p=P)
        picked = tile("picked2_3", [P, S], F32, "picked2_0b")
        for tokens in halves:
            nc.scalar.activation(picked[:, tokens], h1[3][:].indirect(entries(mix2_tile, tokens)), COPY)
        last_picked = tile("last_picked", [P, HALF_TOKENS], F32)
        nc.scalar.activation(last_picked[:], h1[2][:].indirect(entries(mix2_tile, halves[1])), COPY)
        product_banks = [banks[n] for n in (4, 6, 5, 0)]
        grouped = []
        for b in range(BLOCKS):
            if b % 2 == 0:
                tokens = halves[b // 2]
                nc.vector.tensor_tensor(partners[3][:, tokens], picked[:, tokens], ratio_bank[:, tokens], MULT)
            if b < 2:
                nc.vector.tensor_tensor(partners[2][:, block(b)], h1[2][:].indirect(entries(mix2_tile, block(b))), ratio_row[:, block(b)], MULT)
            if b == 2:
                nc.vector.tensor_tensor(partners[2][:, tokens], last_picked[:], ratio_bank[:, tokens], MULT)
            for t in (3, 2):
                turn_into(b, t, partners[t], False, t == 2)
            if b < last:
                finish_h2(b, h2_turned[b][:], quarters(sum_banks[b]))
            else:
                nc.vector.tensor_scalar(
                    h2_turned[b][:, :, 1, :], quarters(banks[3])[:, :, 1, :], own2_safe[:, b : b + 1], None, MULT
                )
            words = product_banks[b][:, :HALF_TOKENS].rearrange("p (u s) -> p u s", u=2)
            for u in range(2):
                nc.tensor.transpose(words[:, u, :], h2_turned[b][:, u].rearrange("s v c -> s (v c)").bitcast(F32), identity[:])
        for b in range(BLOCKS):
            words = product_banks[b][:, :HALF_TOKENS].rearrange("p (u s) -> p u s", u=2)
            grouped.append(tile(f"h2_grouped{b}", [P, K_PASS], BF16))
            nc.scalar.copy(grouped[b][:].bitcast(F32).rearrange("p (s u) -> p s u", u=2), words.rearrange("p u s -> p s u"))
        w2_grouped = tile("w2_grouped", [P, N * PACK], BF16, "last_picked")
        nc.vector.tensor_copy(
            w2_grouped[:].rearrange("p (c i j) -> p c j i", i=4, j=PACK), w2_raw[:].rearrange("p j (c i) -> p c j i", i=4)
        )
        w2_codes, w2_scales = quantise("w2", w2_grouped[:], N, scale_tag="own2_safe")

        last_staged = tile("last_staged", [P, OUT_TILES, HALF_TOKENS], F32)
        for b in (0, 1, 3, 2):
            h2_codes, h2_scales = quantise(f"h2_{b}", grouped[b][:], P)
            places = [product_banks[b][:, block(2 + m)] for m in range(OUT_TILES)]
            if b == 2:
                places[0] = banks[1][:, :P]
            for m in range(OUT_TILES):
                nc.tensor.matmul_mx(
                    out=places[m],
                    lhsT=w2_codes[:, block(m)].bitcast(FP8X4),
                    lhsT_scale=w2_scales[:, block(m)],
                    rhs=h2_codes[:].bitcast(FP8X4),
                    rhs_scale=h2_scales[:],
                    start=True,
                    stop=True,
                )
            staged = tile(f"staged{b}", [P, OUT_TILES, P], F32) if b < 2 else last_staged[:, :, block(b - 2)]
            if b != 2:
                copy = nc.vector.tensor_copy if b == 1 else nc.scalar.copy
                copy(staged[:], product_banks[b][:, HALF_TOKENS:].rearrange("p (m s) -> p m s", m=OUT_TILES))
            else:
                for m, copy in enumerate((nc.scalar.copy, nc.vector.tensor_copy)):
                    copy(staged[:, m, :], places[m])
            if b < 2:
                nc.sync.dma_start(out_view[:, :, block(b)], staged[:])
        nc.sync.dma_start(out_view[:, :, halves[1]], last_staged[:])
